import numpy as np, ml_dtypes
CORES = [40,41,42,43,44,45,46,47]
N = 8
BF = ml_dtypes.bfloat16
V, R, C, LA, HL, RO, HM = 2048, 128, 5, 256, 64, 2, 2048
Z = V - 1
def climb(fa, v, n):
    for _ in range(n): v = fa[v]
    return v
def mates(rng, fa, dp, a, e):
    key = np.arange(V)
    for _ in range(C): key = np.where(dp[key] > e, fa[key], key)
    o = np.argsort(key[:Z], kind="stable"); ks = key[o]; lo = np.searchsorted(ks, key[a]); hi = np.searchsorted(ks, key[a], side="right")
    return o[lo + (rng.random(a.shape) * (hi - lo)).astype(np.int64)]
def levels(c, top):
    m = V - 1 - R; t = int(np.sum(c)); n = [m * int(i) // t for i in c]; n[0] = min(n[0], top * R)
    for i in range(1, C): n[i] = min(n[i], 14 * n[i - 1])
    n[C - 1] += m - sum(n)
    return n
def forest(rng, n, sp, roots, num, forced):
    kd = np.full((16, V), Z); fa = np.arange(V); dp = np.zeros(V, np.int64); up = roots; pos = 0
    for d in range(C):
        key = rng.exponential(1.0, (len(up), 16)) * np.exp2(rng.integers(-sp, sp + 1, (len(up), 1)))
        for i, (u, j) in enumerate(forced[d] if d < len(forced) else ()): key[u, j] = i - 1000.0
        o = np.argsort(key, axis=None)[:n[d]]; nodes = num[pos:pos + n[d]]; pos += n[d]; u = up[o >> 4]
        kd[o & 15, u] = nodes; fa[nodes] = u; dp[nodes] = d + 1; up = nodes
    return kd, fa, dp
def lanes(rng, fa, dp):
    a = rng.integers(0, Z, LA); b = rng.integers(0, V, LA); p = rng.integers(0, C + 1, LA)
    for e in range(C): b = np.where(p == e, mates(rng, fa, dp, a, e), b)
    return a, b
def base(rng, plan=None):
    kd = np.zeros((N, 8, 16, V), np.int64); fa = np.zeros((N, 8, V), np.int64); dp = fa.copy(); pa = np.zeros((N, 8, LA), np.int64); pb = pa.copy()
    for q in range(N):
        for g in range(8):
            c, top, sp = plan(rng, q, g) if plan else (rng.integers(2, 5, C), 8, 3)
            kd[q, g], fa[q, g], dp[q, g] = forest(rng, levels(c, top), sp, rng.permutation(R), R + rng.permutation(V - 1 - R), ())
            pa[q, g], pb[q, g] = lanes(rng, fa[q, g], dp[q, g])
    x = (rng.random((N, 8, 16, V)) * 256 * np.exp2(rng.integers(-2, 1, (N, 8, 1, V)))).astype(np.int64)
    return dict(x=x, kd=kd, fa=fa, dp=dp, pa=pa, pb=pb, w=rng.integers(0, 256, (N, 8, 16, 1)))
def pack(s):
    x = s["x"].copy(); x[..., Z] = 0; i4 = lambda v, *sh: np.ascontiguousarray(v.reshape(sh)).astype(np.int32)
    return {"xs": np.ascontiguousarray(x.reshape(N, 128, V)).astype(np.float32).astype(BF), "kd": i4(s["kd"], N, 128, V), "fa": i4(s["fa"], N, 8, V), "dp": i4(s["dp"], N, 8, V),
            "pa": i4(s["pa"], N, 8, LA), "pb": i4(s["pb"], N, 8, LA), "wt": i4(s["w"], N, 128, 1)}
def setup_inputs(rng):
    return pack(base(rng))
def setup_inputs_spread(rng):
    s = base(rng, lambda r, q, g: (r.integers(2, 5, C), 8, 6))
    s["x"] = (rng.random((N, 8, 16, V)) * np.exp2(rng.integers(0, 9, (N, 8, 1, V)))).astype(np.int64)
    s["w"] = (rng.random((N, 8, 16, 1)) * np.exp2(rng.integers(0, 9, (N, 8, 16, 1)))).astype(np.int64)
    return pack(s)
def setup_inputs_ends(rng):
    n = [2 * R] + [(36 * V // 100 - 2 * R) // (C - 2)] * (C - 2); n.append(V - 1 - R - sum(n)); s = base(rng)
    forced = ([(0, 0), (0, 15), (1, 0)], [(0, 0), (0, 7), (0, 14), (0, 15), (1, 0), (1, 3), (1, 15)], [(i, j) for i in range(7) for j in (0, 15)])
    k = rng.random((N, 8, 1, V)); x = 255 * rng.integers(0, 2, (N, 8, 16, V)); x = np.where(k < 0.35, 255, np.where(k < 0.6, 0, x)); w = 255 * rng.integers(0, 2, (N, 8, 16, 1))
    for q in range(N):
        for g in range(8):
            num = R + rng.permutation(V - 1 - R)
            for at, v in ((0, V - 3), (1, R), (2, V - 2), (n[0] + 3, V - 4), (n[0], R + 1)):
                j = int(np.flatnonzero(num == v)[0]); num[j] = num[at]; num[at] = v
            kd, fa, dp = forest(rng, n, 3, np.concatenate([np.array([R - 1, 0]), 1 + rng.permutation(R - 2)]), num, forced)
            s["kd"][q, g], s["fa"][q, g], s["dp"][q, g] = kd, fa, dp
            mode = (7 - g + N - 1 - q) % 4; A, B = V - 3, R; y = x[q, g]; fam = []
            for v in (A, B):
                c = kd[:, v]; c = c[c != Z]; t = kd[:, c].reshape(-1); fam.append((c, t[t != Z]))
            y[:, A] = 0; y[:, B] = 0
            for c, t in fam: y[:, c] = 255; y[:, t] = 255
            y[(q + g) % 16, fam[0][0]] = 254
            best = num[n[0] + 1:n[0] + 4] if (q + g) % 2 == 0 else num[n[0] + 3:n[0] + 4]
            y[:, best] = 255
            if mode == 0: w[q, g] = 255
            if mode == 1: y[:, fam[1][0]] = 0; y[:, fam[1][1]] = 0
            if mode == 2: y[:, fam[0][0]] = 0; y[:, fam[0][1]] = 0
            if mode == 3:
                o = rng.permutation(16)[:9]; y[o[:, None], fam[1][0][None]] = 0; y[o[:, None], fam[1][1][None]] = 0
            a, b = lanes(rng, fa, dp); end = rng.random(LA) < 0.72
            a = np.where(end, rng.choice(np.array([0, V - 2]), LA), a); b = np.where(end, rng.choice(np.array([0, Z]), LA), b)
            a = np.where(climb(fa, a, C) == R - 1, 0, a); a[LA - 1] = A; b[LA - 1] = B
            s["pa"][q, g], s["pb"][q, g] = a, b
    s["x"], s["w"] = x, w
    return pack(s)
def setup_inputs_corners(rng):
    def plan(r, q, g):
        return ((r.integers(2, 5, C), 8, 20), ([1] * (C - 1) + [8], 8, 3), ([8] + [1] * (C - 1), 16, 3), (r.integers(2, 5, C), 8, 0))[(q + g) % 4]
    s = base(rng, plan); k = rng.random((N, 8, 1, V)); s["x"] = np.where(k < 0.15, 255, np.where(k < 0.3, 0, s["x"]))
    for q in range(N):
        for g in range(8):
            fa, dp = s["fa"][q, g], s["dp"][q, g]; a = np.where(rng.random(LA) < 0.4, rng.choice(np.array([0, R - 1, R, V - 2]), LA), s["pa"][q, g]); t = rng.integers(0, 5, LA)
            b = np.where(t == 0, rng.choice(np.array([0, R - 1, R, V - 2, Z]), LA), np.where(t == 1, a, np.where(t == 2, fa[a], np.where(t == 3, mates(rng, fa, dp, a, 0), mates(rng, fa, dp, a, C - 2)))))
            s["pa"][q, g], s["pb"][q, g] = a, b
            u = (q + 2 * g) % 5
            if u == 0: s["w"][q, g] = 0
            if u == 1: s["w"][q, g] = 255
    return pack(s)
def setup_inputs_ties(rng):
    s = base(rng)
    for q in range(N):
        for g in range(8):
            m = rng.choice(np.array([0, 0, 0, 8, 9, 16]), V); y = 100 + (rng.permutation(16)[:, None] < m[None]).astype(np.int64); t = rng.random(V)
            if (q + g) % 3: y = np.where(t < 0.12, 0, np.where(t < 0.2, 255, y))
            s["x"][q, g] = y
    return pack(s)
def pairs(rng, s, q, g):
    left = V - 1 - R - 5 * LA; more = left // (C - 2); n = [LA, 2 * LA, 2 * LA + more] + [more] * (C - 3); n[C - 1] += V - 1 - R - sum(n)
    rows = np.argsort(rng.random((LA, 16)), axis=1)[:, :2]; slot = rng.integers(0, 16, 2 * LA); num = R + rng.permutation(V - 1 - R)
    forced = ((), [(i >> 1, int(rows[i >> 1, i & 1])) for i in range(2 * LA)], [(i, int(slot[i])) for i in range(2 * LA)])
    kd, fa, dp = forest(rng, n, 3, rng.permutation(R), num, forced)
    s["kd"][q, g], s["fa"][q, g], s["dp"][q, g] = kd, fa, dp
    at = np.zeros(V, np.int64); at[num[LA:3 * LA]] = np.arange(2 * LA); m = np.flatnonzero(dp == 3); t = at[fa[m]]
    win = rng.integers(0, 2, LA); hi = np.argsort(rng.random((16, LA)), axis=0) < rng.integers(9, 17, LA)[None]
    y = rng.integers(0, 64, (16, V)); x = s["x"][q, g]; low = np.flatnonzero((dp == 2) | (dp > 3)); x[:, low] = y[:, low]
    x[:, m] = 64 + y[:, m] + 128 * (hi[:, t >> 1] == ((t & 1) == win[t >> 1])[None]).astype(np.int64)
    o = rng.permutation(LA); flip = rng.integers(0, 2, LA)
    return num[LA + 2 * o + flip], num[LA + 2 * o + 1 - flip]
def fold(rng, s, q, g):
    roots = np.concatenate([1 + rng.permutation(R - 1), np.array([0])]); num = R + rng.permutation(V - 1 - R); rows = np.argsort(rng.random((8, 16)), axis=1)[:, :2]
    forced = ([(i >> 1, int(rows[i >> 1, i & 1])) for i in range(16)], [(i, int(rows[i >> 1, i & 1])) for i in range(16)])
    kd, fa, dp = forest(rng, levels(rng.integers(2, 5, C), 8), 3, roots, num, forced)
    s["kd"][q, g], s["fa"][q, g], s["dp"][q, g] = kd, fa, dp
    top = climb(fa, np.arange(V), C); x = s["x"][q, g]; x[:2, np.flatnonzero(top == 0)] = 0; x[2:, 0] = 100
    ln = np.concatenate([np.array([HL, LA - 1]), HL + 1 + rng.permutation(LA - HL - 2)[:6]]); off = (0, 0, 0, 0, 0, 0, -1, 1)
    for i in range(8):
        u = int(roots[i]); goal = (V + off[i] - 977 * int(ln[i])) & (HM - 1); c = kd[:, u]; c = c[c != Z]; c1, c2 = int(num[2 * i]), int(num[2 * i + 1])
        x[:, np.flatnonzero((top == u) & (dp > 0))] = 0
        x[0, c] = goal & 15; x[1, c] = goal >> 4; x[2:, c1] = 100; x[2:6, c2] = 255
        for v, val in ((c1, 200), (c2, 50)):
            t = kd[:, v]; t = t[t != Z]; x[2:, t] = val
    a, b = lanes(rng, fa, dp); apart = np.isin(top[a], np.concatenate([roots[:8], np.array([0])]))
    a = np.where(apart, roots[8 + rng.integers(0, R - 9, LA)], a); a[ln] = roots[:8]; b[ln] = Z
    s["w"][q, g] = 0; s["w"][q, g, 0] = 1; s["w"][q, g, 1] = 16
    return a, b
def setup_inputs_crowd(rng):
    s = base(rng)
    for q in range(N):
        for g in range(8):
            kd, fa = s["kd"][q, g], s["fa"][q, g]; kind = (q + g) % 7; cand = rng.permutation(np.flatnonzero(np.add.reduce((kd != Z).astype(np.int64), axis=0) >= 2))
            if kind < 2:
                P = cand[rng.integers(0, 3, LA)] if kind == 0 else cand[np.arange(LA) % len(cand)]
                o = np.argsort(rng.random((16, LA)) + 2 * (kd[:, P] == Z), axis=0); a, b = kd[o[0], P], kd[o[1], P]
            elif kind == 2:
                a = rng.integers(0, R, LA); b = rng.integers(0, R + 1, LA); b = np.where(b == R, Z, b)
            elif kind == 3:
                a = rng.integers(0, Z, LA); t = rng.integers(0, 4, LA); b = np.where(t < 2, a, np.where(t == 2, climb(fa, a, 1), climb(fa, a, 2)))
            elif kind == 4:
                a, b = pairs(rng, s, q, g)
            elif kind == 5:
                P = rng.permutation(np.unique(fa[R:Z])); P = P[np.arange(LA) % len(P)]
                a = kd[np.argmin(rng.random((16, LA)) + 2 * (kd[:, P] == Z), axis=0), P]; b = a.copy()
            else:
                a, b = fold(rng, s, q, g)
            s["pa"][q, g], s["pb"][q, g] = a, b
    return pack(s)
def check_inputs(d):
    bad = []
    for k, lo, hi in (("xs", 0, 255), ("kd", R, Z), ("fa", 0, Z), ("dp", 0, C), ("pa", 0, Z - 1), ("pb", 0, Z), ("wt", 0, 255)):
        v = np.asarray(d[k]).astype(np.float64)
        if not (np.min(v) >= lo and np.max(v) <= hi): bad.append("range of " + k)
        elif np.any(v != np.floor(v)): bad.append("whole numbers of " + k)
    if bad: return bad
    M = N * 8; f = np.asarray(d["fa"]).astype(np.int64).reshape(M, V); e = np.asarray(d["dp"]).astype(np.int64).reshape(M, V); k = np.asarray(d["kd"]).astype(np.int64).reshape(M, 16 * V)
    if np.any(np.asarray(d["xs"]).astype(np.float32)[..., Z] != 0): bad.append("last column of xs")
    own = np.concatenate([np.arange(R), np.array([Z])])
    if np.any(f[:, own] != own) or np.any(e[:, own] != 0): bad.append("roots")
    if np.any(f[:, R:Z] == Z) or np.any(e[:, R:Z] != np.take_along_axis(e, f[:, R:Z], 1) + 1): bad.append("fathers and depths")
    s = np.sort(k, axis=1)
    if np.any(s[:, :Z - R] != np.arange(R, Z)) or np.any(s[:, Z - R:] != Z): bad.append("every node a kid once")
    if np.any((k != Z) & (np.take_along_axis(f, k, 1) != np.tile(np.arange(V), 16))): bad.append("kids and fathers")
    return bad
def pick(t, ix):
    return np.take_along_axis(t, ix, 1)
def cols(t, ix):
    return np.take_along_axis(t, ix[:, None, :], 2)
def ring(x, k, p, o):
    m = k.shape[0]; K = cols(k, p)
    y = cols(x, K.reshape(m, 16 * LA)).reshape(m, 16, 16, LA)
    score = np.add.reduce(np.maximum(y - cols(x, o)[:, :, None, :], 0), axis=1)
    row = np.argmax(score, axis=1)
    lead = np.take_along_axis(K, row[:, None, :], 1)[:, 0]
    z = cols(x, cols(k, lead).reshape(m, 16 * LA)).reshape(m, 16, 16, LA)
    return K, row, lead, np.max(y, axis=2) + np.max(z, axis=2)
def reference(xs, kd, fa, dp, pa, pb, wt):
    M = N * 8; x = xs.astype(np.float32).astype(np.int32).reshape(M, 16, V); k = kd.astype(np.int64).reshape(M, 16, V); f = fa.astype(np.int64).reshape(M, V); e = dp.astype(np.int64).reshape(M, V)
    a = pa.astype(np.int64).reshape(M, LA); b = pb.astype(np.int64).reshape(M, LA); w = wt.astype(np.int64).reshape(M, 16, 1)
    lane = np.arange(LA); lower = np.tri(LA, k=-1, dtype=bool); at = np.arange(M)[:, None]
    asked = ((at // 8 + 1 + lane[None] % (N - 1)) % N) * 8 + at % 8
    for rnd in range(RO):
        for step in range(C):
            da, db, ga, gb = pick(e, a), pick(e, b), pick(f, a), pick(f, b)
            go = (da != db) | (ga != gb)
            a, b = np.where(go & (da >= db), ga, a), np.where(go & (db >= da), gb, b)
        F = pick(f, a); met = (a != b) & (F == pick(f, b))
        KA, rA, lA, UA = ring(x, k, a, b)
        KB, rB, lB, UB = ring(x, k, b, a)
        awin = met & (np.add.reduce((UA > UB).astype(np.int64), axis=1) >= 9)
        bwin = met & (np.add.reduce((UB > UA).astype(np.int64), axis=1) >= 9)
        first = ~np.any((F[:, :, None] == F[:, None, :]) & lower[None], axis=2)
        W, L = np.where(bwin, b, a), np.where(bwin, a, b); lW, lL = np.where(bwin, lB, lA), np.where(bwin, lA, lB); rW, rL = np.where(bwin, rB, rA), np.where(bwin, rA, rB)
        x2, k2, f2 = x.copy(), k.copy(), f.copy()
        m, i = np.nonzero(first & (awin | bwin))
        x2[m, :, W[m, i]] = (x[m, :, W[m, i]] + x[m, :, lW[m, i]]) >> 1
        m, i = np.nonzero(first & (awin | bwin) & (lW != Z) & (lL != Z))
        k2[m, rW[m, i], W[m, i]] = lL[m, i]; k2[m, rL[m, i], L[m, i]] = lW[m, i]
        f2[m, lW[m, i]] = L[m, i]; f2[m, lL[m, i]] = W[m, i]
        h = np.add.reduce(w * UA, axis=1) & (R - 1)
        m, i = np.nonzero(first & ~met)
        x2[m, :, a[m, i]] = (UA[m, :, i] + 2 * x[asked[m, i], :, h[m, i]]) >> 2
        kid = np.where(bwin[:, None, :], KB, KA)[:, lane & 15, lane]
        new = (np.add.reduce(w * (UA + UB), axis=1) + 977 * lane) & (HM - 1); new = np.where(new >= V, new - V, new)
        a = np.where(lW == Z, W, lW); b = np.where(lane < HL, kid, new)
        x, k, f = x2, k2, f2
    return {"yx": x.reshape(N, 128, V).astype(np.float32).astype(BF), "yf": f.reshape(N, 8, V).astype(np.float32)}

@@ -1,0 +1,674 @@
+from concourse.bass import DstId, RemoteDMATransfer
+from concourse.mybir import AluOpType as OP, ActivationFunctionType as AF
+
+X0, XA, XD, YMO, ZMO, R2O = 896, 2048, 2064, 2320, 2576, 2832
+XEND = R2O + 896
+ND = 4
+
+SCRATCH = {}
+for _n, _w, _d in (
+        ("XW", X0 + XEND, "bfloat16"), ("KD", 2576, "int32"), ("F", 2576, "float32"), ("M", 2048, "bfloat16"), ("VAL", 2048, "bfloat16"), ("CM", 2048, "bfloat16"),
+        ("FAI", 128, "int32"), ("DPI", 128, "int32"), ("PAI", 16, "int32"), ("PBI", 16, "int32"), ("WTI", 1, "int32"), ("FDH", 256, "float16"),
+        ("PI", 1, "int32"), ("TI", 2, "int32"), ("COL", 32, "float32"), ("NF", 256, "float32"), ("NR", 256, "float32"), ("NG", 256, "float32"),
+        ("BLK", 128, "float16"), ("NBLK", 128, "float16"), ("WBH", 144, "float16"), ("WB16", 144, "float16"), ("WBB", 144, "bfloat16"), ("WBW", 144, "bfloat16"),
+        ("IDB", 128, "bfloat16"), ("IDN", 128, "bfloat16"), ("ID2", 128, "bfloat16"), ("IDH", 128, "float16"), ("IDM", 128, "bfloat16"), ("BSEL", 2048, "float16"), ("DELR", 16, "float32"), ("B8", 16, "float32"),
+        ("DM", 256, "bfloat16"), ("RMH", 256, "float16"), ("RMB", 1024, "bfloat16"), ("SEL", 8, "bfloat16"), ("KC", 256, "bfloat16"), ("E0", 128, "bfloat16"), ("ZB", 512, "bfloat16"),
+        ("L15", 16, "uint16"), ("DLT", 128, "bfloat16"), ("S1", 128, "bfloat16"), ("S2", 128, "bfloat16"), ("S3", 128, "bfloat16"), ("S4", 128, "bfloat16"), ("S5", 128, "bfloat16"), ("S6", 256, "bfloat16"), ("E4", 256, "float32"), ("E1", 128, "float32"), ("E2", 128, "float32"), ("E3", 128, "float32"), ("P0", 128, "float32"),
+        ("TA", 128, "bfloat16"), ("TB", 128, "bfloat16"), ("DMX", 128, "bfloat16"), ("MS", 128, "bfloat16"), ("RT", 128, "bfloat16"), ("RTN", 128, "bfloat16"), ("RD", 128, "bfloat16"),
+        ("LN", 16, "float32"), ("L977", 16, "float32"), ("QI", 32, "int32"), ("QF", 32, "float32"), ("TBIG", 256, "bfloat16"), ("DUX", 16, "float32"), ("DUF", 32, "float32"),
+        ("RBK", 32, "float32"), ("CNT", 16, "float32"), ("BS1", 48, "float32"), ("BS2", 48, "float32"), ("EQ", 2560, "bfloat16"), ("EQS", 2560, "bfloat16"), ("PX", 64, "float32"), ("PT", 64, "float32"), ("PU", 32, "float32"),
+        ("GM", 2560, "bfloat16"), ("G5", 512, "bfloat16"), ("G", 2048, "float16"), ("SC", 2048, "float16"), ("LS", 160, "uint16"), ("LSI", 32, "int32"),
+        ("VA", 256, "float16"), ("PR", 512, "float16"), ("AW", 32, "float32"), ("LA", 32, "uint16"), ("VALF", 512, "float32"),
+        ("KL", 512, "uint16"), ("KF", 512, "float16"), ("XS", 512, "bfloat16"), ("Y", 8192, "bfloat16"), ("SY", 8192, "bfloat16"), ("MM", 8192, "bfloat16"),
+        ("KS", 512, "float32"), ("PS", 512, "float32"), ("OHT", 512, "bfloat16"), ("OHS", 512, "bfloat16"), ("PL", 512, "float16"), ("LL", 32, "uint16"), ("LW", 32, "float32"),
+        ("ZK", 512, "uint16"), ("Z", 8192, "bfloat16"), ("SZ", 8192, "bfloat16"), ("FG", 512, "float16"), ("FW", 32, "float32"), ("FWH", 16, "float16"),
+        ("EQD", 256, "bfloat16"), ("SQD", 256, "bfloat16"), ("GL", 512, "bfloat16"), ("W", 1152, "float32"), ("SI", 64, "int32"), ("KDD", 128, "float16"), ("KDS", 128, "float16"), ("KN", 8, "float32"),
+        ("LT", 48, "uint16"), ("LX", 16, "uint16"), ("LF", 64, "uint16"), ("TG", 768, "bfloat16"), ("VI", 256, "int32"), ("TK", 512, "float16"), ("NK", 512, "float32")):
+    SCRATCH[_n] = ("sbuf", [128, _w], _d)
+for _b in range(8):
+    SCRATCH["b%d" % _b] = ("psum", [128, 512], "float32")
+SEMAPHORES = ["qV", "qA", "qT", "qG", "sent1", "sent2", "arr1", "arr2"] + ["d%d" % _i for _i in range(12)]
+
+VY = ((1, 0),)
+RELU = ((1, 0),)
+VG = ((0, 0), (1, 1), (1, 3))
+SLACK = 0.0
+KSA, FQ, MQ, GQ = "VA", "VAAV", "AAVA", "AAAAAAAAVA"
+BOOST = {"ma": 6.0, "la": 20.0, "lb": -2.0, "SZ": 32.0, "zb": -4.0, "za": -4.0}
+G5Q = "AAAA"
+CY, GA, WK = 0.00104, 0.00135, 0.09
+
+
+def X(name, lo, hi, st=1, p0=0, p1=128):
+    return ("x", name, lo, hi, st, p0, p1)
+
+
+def IND(win, off):
+    return ("i", win, off)
+
+
+def width(a):
+    if a[0] == "i":
+        return 16 * (a[2][3] - a[2][2])
+    return (a[3] - a[2] + a[4] - 1) // a[4]
+
+
+def spans(a):
+    return [a[1], a[2]] if a[0] == "i" else [a]
+
+
+def gcd(a, b):
+    while b:
+        a, b = b, a % b
+    return a
+
+
+def clash(a, b):
+    if a[2] >= b[3] or b[2] >= a[3] or a[5] >= b[6] or b[5] >= a[6]:
+        return False
+    return (a[2] - b[2]) % gcd(a[4], b[4]) == 0
+
+
+def two(a):
+    return a[0] == "x" and a[1][0] != "b" and SCRATCH[a[1]][2] in ("bfloat16", "float16", "uint16")
+
+
+def psum(a):
+    return a[0] == "x" and a[1][0] == "b"
+
+
+def build():
+    P = []
+    cur = [""]
+
+    def add(qs, what, out, ins, args, cost):
+        P.append(dict(b=cur[0], q=qs, what=what, out=out, ins=ins, args=args, cost=cost, w=(spans(out) if out else []) + (list(args) if what == "count" else []), r=[s for i in ins for s in spans(i)]))
+
+    def ccost(out, ins, fast):
+        n = width(out)
+        if out[0] == "i":
+            return 0.05 + n * 0.0031
+        if ins[0][0] == "i":
+            return 0.05 + n * GA
+        return max(64, n * (0.5 if fast and two(out) and all(two(i) for i in ins) else 1)) * CY
+
+    def tc(out, a, q="V"):
+        add(q, "tc", out, [a], (), ccost(out, [a], True))
+
+    def tt(out, a, b, op):
+        n = width(b)
+        c = 0.05 + n * GA if a[0] == "i" else max(64, n * (1 if psum(a) or psum(b) else 2)) * CY
+        add("V", "tt", out, [a, b], (op,), c)
+
+    def ts(out, a, s1, o1, s2=None, o2=None):
+        ins = [a] + [s for s in (s1, s2) if isinstance(s, tuple)]
+        add("V", "ts", out, ins, (s1, o1, s2, o2), ccost(out, [a], True))
+
+    def scan(out, d0, d1, o0, o1):
+        add("V", "scan", out, [d0, d1], (o0, o1), ccost(out, [d0, d1], True))
+
+    def act(out, a, bias=None):
+        c = 0.065 + width(out) * GA if a[0] == "i" else max(64, width(out)) * CY
+        add("A", "act", out, [a] + ([bias] if bias else []), (bias,), c)
+
+    def relu(out, a):
+        add("A", "relu", out, [a], (), width(out) * CY)
+
+    def gat(out, a, q="A"):
+        add(q, "gat", out, [a], (), 0.06 + width(out) * GA)
+
+    def mm(out, l, r, start, stop):
+        add("T", "mm", out, [l, r], (start, stop), max(64, width(r)) * CY)
+
+    def dma(q, out, a, sem):
+        add(q, "dma", out, [a], (sem,), 0.06)
+
+    def iota(out, pat, cm, base=0):
+        add("G", "iota", out, [], (pat, cm, base), 0.13 + 2 * width(out) * CY)
+
+    def col(i):
+        return X("COL", i, i + 1)
+
+    dma("S", X("FAI", 0, 128), ("d", "fa"), "d0")
+    dma("A", X("DPI", 0, 128), ("d", "dp"), "d1")
+    dma("S", X("PAI", 0, 16), ("d", "pa"), "d2")
+    dma("A", X("PBI", 0, 16), ("d", "pb"), "d3")
+    dma("S", X("KD", 0, 2048), ("d", "kd"), "d5")
+    dma("S", X("XW", X0, X0 + 2048), ("d", "xs"), "d6")
+    dma("S", X("WTI", 0, 1), ("d", "wt"), "d4")
+    add("G", "send", None, [X("XW", X0, X0 + 128)], (1,), 1.0)
+    add("N", "arrive", X("XW", 0, 896), [], (1,), 0)
+
+    iota(X("PI", 0, 1), [[0, 1]], 1)
+    iota(X("NF", 0, 256), [[1, 256]], 0)
+    iota(X("NG", 0, 256), [[1, 16], [0, 16]], 0)
+    iota(X("NR", 0, 256), [[0, 16], [1, 16]], 0)
+    iota(X("XW", X0 + XA, X0 + YMO), [[0, YMO - XA]], 0)
+    ts(X("TI", 0, 1), X("PI", 0, 1), 15, OP.bitwise_and)
+    ts(X("TI", 1, 2), X("PI", 0, 1), 4, OP.arith_shift_right)
+    tc(X("COL", 0, 2), X("TI", 0, 2))
+    tc(col(2), X("PI", 0, 1))
+    N128, R128, G128 = X("NF", 0, 128), X("NR", 0, 128), X("NG", 0, 128)
+    pr, pg, pc = col(0), col(1), col(2)
+    ts(X("BLK", 0, 128), G128, pg, OP.is_equal)
+    ts(X("DELR", 0, 16), X("NF", 0, 16), pr, OP.is_equal)
+    for r in range(16):
+        ts(X("BSEL", 128 * r, 128 * r + 128), X("BLK", 0, 128), X("DELR", r, r + 1), OP.mult)
+    ts(col(6), pr, 1, OP.is_lt)
+    ts(col(15), pr, 6, OP.is_ge)
+    ts(col(5), pr, 11, OP.is_ge)
+    ts(col(3), pr, 1, OP.is_ge)
+    tt(col(3), col(3), col(15), OP.subtract)
+    tt(col(4), col(15), col(5), OP.subtract)
+    ts(col(7), col(3), 16, OP.mult)
+    ts(col(8), col(5), -4096, OP.mult)
+    ts(col(16), col(4), 5, OP.mult, pr, OP.subtract)
+    ts(col(17), col(5), 10, OP.mult)
+    tt(col(10), col(16), col(17), OP.add)
+    ts(col(18), pr, 1, OP.is_ge, -8192, OP.mult)
+    ts(col(19), pr, 1, OP.is_lt)
+    tc(X("FDH", 0, 128), X("FAI", 0, 128))
+    tc(X("FDH", 128, 256), X("DPI", 0, 128))
+    for k in range(2):
+        for r in range(16):
+            b = "b%d" % (4 * k + r // 4)
+            mm(X(b, 128 * (r % 4), 128 * (r % 4) + 128), X("BSEL", 128 * r, 128 * r + 128), X("FDH", 128 * k, 128 * k + 128), True, True)
+    for i in range(4):
+        (act if FQ[i] == "A" else tc)(X("F", 512 * i, 512 * i + 512), X("b%d" % i, 0, 512))
+    add("V", "ms", X("F", XA, XD), [], (2047.0,), 0.066)
+    add("V", "ms", X("KD", XA, XD), [], (2047,), 0.066)
+    ts(X("E1", 0, 128), G128, col(3), OP.mult)
+    ts(X("E2", 0, 128), R128, col(4), OP.mult, col(5), OP.add)
+    tt(X("P0", 0, 128), X("E1", 0, 128), X("E2", 0, 128), OP.add)
+    ts(X("B8", 0, 16), X("NF", 0, 16), 8, OP.mult, col(3), OP.mult)
+    for r in range(16):
+        act(X("VAL", 128 * r, 128 * r + 128), X("P0", 0, 128), X("B8", r, r + 1))
+    ts(X("IDB", 0, 128), N128, pc, OP.is_equal)
+    ts(X("IDM", 0, 128), X("IDB", 0, 128), -256, OP.mult)
+    for i in range(4):
+        add("A", "sq", X("CM", 512 * i, 512 * i + 512), [X("b%d" % (4 + i), 0, 512), col(10)], (), 512 * CY)
+        mm(X("b%d" % i, 0, 512), X("IDB", 0, 128), X("VAL", 512 * i, 512 * i + 512), True, False)
+        mm(X("b%d" % i, 0, 512), X("IDM", 0, 128), X("CM", 512 * i, 512 * i + 512), False, True)
+        if MQ[i] == "A":
+            relu(X("M", 512 * i, 512 * i + 512), X("b%d" % i, 0, 512))
+        else:
+            ts(X("M", 512 * i, 512 * i + 512), X("b%d" % i, 0, 512), 0, OP.max)
+    ts(X("TI", 0, 1), X("TI", 1, 2), 1, OP.bitwise_and)
+    tc(col(14), X("TI", 0, 1))
+    ts(col(13), col(14), -1, OP.mult, 1, OP.add)
+    for s in range(2):
+        src = X("PBI" if s else "PAI", 0, 16)
+        ts(X("PX", 32 * s, 32 * s + 16), src, col(13), OP.mult)
+        ts(X("PX", 32 * s + 16, 32 * s + 32), src, col(14), OP.mult)
+    add("V", "tr", X("PT", 0, 64), [X("PX", 0, 64)], (), 0.07)
+    for s in range(2):
+        tt(X("PU", 16 * s, 16 * s + 16), X("PT", 32 * s, 32 * s + 16), X("PT", 32 * s + 16, 32 * s + 32), OP.add)
+    tc(X("LS", 0, 32), X("PU", 0, 32))
+    ts(X("DM", 0, 256), X("NR", 0, 256), pr, OP.is_equal)
+    ts(X("RMH", 0, 256), X("NR", 0, 256), 0, OP.not_equal)
+    m128 = lambda n: X(n, 0, 128)
+    dl, e3, s1, s2 = m128("DLT"), m128("E3"), m128("S1"), m128("S2")
+    ts(e3, R128, 5, OP.is_gt, 1000, OP.mult)
+    ts(m128("S3"), m128("BLK"), -1000, OP.mult, 1000, OP.add)
+    tt(m128("E4"), R128, e3, OP.add)
+    ts(X("E4", 128, 256), m128("E4"), pr, OP.subtract)
+    tt(dl, X("E4", 128, 256), m128("S3"), OP.add)
+    ts(s1, dl, 1, OP.is_equal, col(7), OP.mult)
+    ts(s2, dl, -4, OP.is_equal, col(4), OP.mult)
+    tt(m128("TA"), s1, s2, OP.add)
+    ts(m128("TB"), m128("TA"), -1, OP.mult)
+    ts(m128("MS"), dl, -10, OP.is_le, col(8), OP.mult)
+    ts(m128("S4"), dl, 0, OP.is_equal, col(7), OP.mult)
+    ts(m128("S5"), dl, -5, OP.is_equal, col(4), OP.mult)
+    tt(m128("S6"), m128("S4"), m128("S5"), OP.add)
+    tt(m128("DMX"), m128("S6"), m128("TA"), OP.subtract)
+    ts(m128("RT"), dl, 1, OP.is_equal, col(6), OP.mult)
+    ts(m128("RTN"), m128("RT"), -1, OP.mult)
+    ts(X("S6", 128, 256), dl, 0, OP.is_equal, col(6), OP.mult)
+    tt(m128("RD"), X("S6", 128, 256), m128("RT"), OP.subtract)
+    iota(X("ZB", 0, 512), [[0, 512]], 0)
+    iota(X("RMB", 0, 1024), [[0, 64], [512, 16]], 0)
+    iota(X("KC", 0, 256), [[0, 16], [-1, 16]], 0, 15)
+    ts(X("WBH", 0, 144), X("NF", 0, 144), 0, OP.mult)
+    ts(X("WBH", 15, 143, 16), X("NF", 0, 8), pg, OP.is_equal)
+    ts(X("WB16", 0, 144), X("WBH", 0, 144), 0.0625, OP.mult)
+    tc(X("WBB", 0, 144), X("WBH", 0, 144))
+    tc(col(12), X("WTI", 0, 1))
+    ts(X("WBW", 0, 144), X("WBB", 0, 144), col(12), OP.mult)
+    ts(m128("NBLK"), m128("BLK"), -1, OP.mult)
+    ts(m128("IDN"), m128("IDB"), -1, OP.mult)
+    ts(m128("ID2"), m128("IDB"), 2, OP.mult)
+    tc(m128("IDH"), m128("IDB"))
+    ts(X("SEL", 0, 8), X("NF", 0, 8), pg, OP.is_equal, 16, OP.mult)
+    ts(col(11), pc, 0, OP.is_equal)
+    ts(m128("E0"), N128, 0, OP.mult, col(11), OP.add)
+    ts(X("L15", 0, 16), X("NF", 0, 16), 16, OP.mult, 15, OP.add)
+    n16 = X("NF", 0, 16)
+    ts(X("LN", 0, 16), n16, 16, OP.mult, pr, OP.add)
+    ln = X("LN", 0, 16)
+    ts(X("L977", 0, 16), ln, 977, OP.mult)
+    ts(X("QI", 0, 16), ln, 9363, OP.mult)
+    ts(X("QI", 16, 32), X("QI", 0, 16), 16, OP.arith_shift_right)
+    ts(X("QF", 0, 16), X("QI", 16, 32), -7, OP.mult)
+    tt(X("QF", 16, 32), X("QF", 0, 16), ln, OP.add)
+    for i, (nm, base) in enumerate((("BS1", -896), ("BS2", R2O))):
+        ts(X(nm, 0, 16), ln, YMO, OP.add)
+        ts(X(nm, 16, 32), ln, ZMO, OP.add)
+        ts(X("RBK", 16 * i, 16 * i + 16), X("QF", 16, 32), 128, OP.mult, base, OP.add)
+    add("V", "ms", X("CNT", 0, 1), [], (0.0,), 0.066)
+    ts(X("TBIG", 0, 256), X("NR", 0, 256), pr, OP.is_ge, 4096, OP.mult)
+    ts(X("DUX", 0, 16), ln, XD, OP.add)
+    ts(X("DUF", 0, 16), ln, XD, OP.add)
+    ts(X("DUF", 16, 32), ln, XD + 256, OP.add)
+
+    xwin, kwin, fwin, mwin = X("XW", X0, X0 + XD), X("KD", 0, XD), X("F", 0, XD), X("M", 0, 2048)
+    for rnd in range(2):
+        last = rnd == 1
+        mm(X("b1", 0, 512), m128("IDB"), X("ZB", 0, 512), True, False)
+        for k in range(5):
+            for s in range(2):
+                ls = X("LS", 32 * k + 16 * s, 32 * k + 16 * s + 16)
+                o = 256 * s
+                if k < 4:
+                    g = X("G", 512 * k + o, 512 * k + o + 256)
+                    sc = ("SC", 512 * k + o, 512 * k + o + 256)
+                    tt(g, IND(X("F", 0, 2048), ls), X("DM", 0, 256), OP.mult)
+                    scan(X(*sc), X("RMH", 0, 256), g, OP.mult, OP.add)
+                    tc(X("LS", 32 * k + 32 + 16 * s, 32 * k + 48 + 16 * s), X(sc[0], sc[1] + 15, sc[2], 16))
+                gm = X("GM", 512 * k + o, 512 * k + o + 256)
+                gat(gm, IND(mwin, ls), "A" if last else GQ[2 * k + s])
+                if k == 4:
+                    g5 = X("G5", o, o + 256)
+                    gat(g5, IND(X("F", 0, 2048), ls), G5Q[2 * rnd + s])
+                mm(X("b0", 0, 256), m128("TB" if s else "TA"), gm, k == 0 and s == 0, k == 4 and s == 1 and False)
+                if k == 0:
+                    mm(X("b0", 0, 256), m128("MS"), gm, False, False)
+                mm(X("b1", o, o + 256), m128("DMX"), gm, False, False)
+                if k == 4:
+                    mm(X("b0", 0, 256), m128("RTN" if s else "RT"), g5, False, s == 1)
+                    mm(X("b1", o, o + 256), m128("RD"), g5, False, s == 1)
+        ts(X("VA", 0, 256), X("b0", 0, 256), col(18), OP.is_equal, col(19), OP.max)
+        for s in range(2):
+            tt(X("PR", 256 * s, 256 * s + 256), X("b1", 256 * s, 256 * s + 256), X("VA", 0, 256), OP.mult)
+        for r in range(16):
+            mm(X("b2", 0, 32), X("WBH", 15 - r, 143 - r), X("PR", r, 512, 16), r == 0, r == 15)
+        tc(X("LA", 0, 32), X("b2", 0, 32))
+        tc(X("AW", 0, 32), X("b2", 0, 32))
+        for r in range(16):
+            mm(X("b2", 32, 48), X("WBH", 15 - r, 143 - r), X("VA", r, 256, 16), r == 0, r == 15)
+        ts(X("W", 64, 80), X("b2", 32, 48), 2, OP.is_ge)
+        mm(X("b3", 0, 512), m128("BLK"), X("PR", 0, 512), True, True)
+        act(X("VALF", 256, 512), X("b3", 0, 256))
+        act(X("VALF", 0, 256), X("b3", 256, 512))
+
+        def la(s):
+            return X("LA", 16 * s, 16 * s + 16)
+        for s in range(2):
+            gat(X("XS", 256 * s, 256 * s + 256), IND(xwin, la(s)))
+            mm(X("b4", 256 - 256 * s, 512 - 256 * s), m128("IDB"), X("XS", 256 * s, 256 * s + 256), True, True)
+        for s in range(2):
+            tc(X("KL", 256 * s, 256 * s + 256), IND(kwin, la(s)))
+        for s in range(2):
+            for q in range(4):
+                gat(X("Y", 4096 * s + 1024 * q, 4096 * s + 1024 * q + 1024), IND(xwin, X("KL", 256 * s + 64 * q, 256 * s + 64 * q + 64)), "V" if (s, q) in VY else "A")
+        for s in range(2):
+            tc(X("KF", 256 * s, 256 * s + 256), X("KL", 256 * s, 256 * s + 256))
+        for s in range(2):
+            kb = "b%d" % (5 + s)
+            cur[0] = "mb" if s else "ma"
+            mm(X(kb, 0, 256), m128("E0"), X("KC", 0, 256), True, False)
+            for h in range(2):
+                base = 4096 * s + 2048 * h
+                for i in range(4):
+                    for j in range(4 * i, 4 * i + 4):
+                        y, m = X("Y", base + j, base + 2048, 16), X("MM", base + 128 * j, base + 128 * j + 128)
+                        if (s, h) in RELU:
+                            b = "b%d" % (i % 2)
+                            c = 128 * (j - 4 * i)
+                            mm(X(b, c, c + 128), m128("IDB"), y, True, False)
+                            mm(X(b, c, c + 128), m128("IDN"), X("XS", 256 - 256 * s + 128 * h, 384 - 256 * s + 128 * h), False, True)
+                        else:
+                            tt(m, y, X("b4", 256 * s + 128 * h, 256 * s + 128 * h + 128), OP.max)
+                    if (s, h) in RELU:
+                        relu(X("MM", base + 512 * i, base + 512 * i + 512), X("b%d" % (i % 2), 0, 512))
+                    for j in range(4 * i, 4 * i + 4):
+                        mm(X(kb, 128 * h + j, 128 * h + 128, 16), X("MM", base + 128 * j, base + 128 * j + 128), X("SEL", 0, 8), False, h == 1 and j == 15)
+        for s in range(2):
+            o = 256 * s
+            kb = "b%d" % (5 + s)
+            cur[0] = "lb" if s else "la"
+            (act if KSA[s] == "A" else tc)(X("KS", o, o + 256), X(kb, 0, 256))
+            scan(X("PS", o, o + 256), X("RMH", 0, 256), X("KS", o, o + 256), OP.mult, OP.max)
+            tt(X("OHT", o, o + 256), IND(X("PS", o, o + 256), X("L15", 0, 16)), X("KS", o, o + 256), OP.is_equal)
+            for h in range(2):
+                mm(X("b7", o + 128 * h, o + 128 * h + 128), X("OHT", o + 128 * h, o + 128 * h + 128), m128("IDB"), True, True)
+            tt(X("PL", o, o + 256), X("b7", o, o + 256), X("KF", o, o + 256), OP.mult)
+            for r in range(16):
+                mm(X("b3", 16 * s, 16 * s + 16), X("WBH", 15 - r, 143 - r), X("PL", o + r, o + 256, 16), r == 0, r == 15)
+            tc(X("LL", 16 * s, 16 * s + 16), X("b3", 16 * s, 16 * s + 16))
+            tc(X("LW", 16 * s, 16 * s + 16), X("b3", 16 * s, 16 * s + 16))
+            tc(X("ZK", o, o + 256), IND(kwin, X("LL", 16 * s, 16 * s + 16)))
+            cur[0] = "zb" if s else "za"
+            for q in range(4):
+                gat(X("Z", 4096 * s + 1024 * q, 4096 * s + 1024 * q + 1024), IND(xwin, X("ZK", o + 64 * q, o + 64 * q + 64)), "AV" if (s, q) in VG else "A")
+            if not last:
+                act(X("OHS", o, o + 256), X("b7", o, o + 256))
+        for n1, n2 in (("Y", "SY"), ("Z", "SZ")):
+            cur[0] = n2
+            for s in range(2):
+                for q in range(4):
+                    lo = 4096 * s + 1024 * q
+                    scan(X(n2, lo, lo + 1024), X("RMB", 0, 1024), X(n1, lo, lo + 1024), OP.min, OP.max)
+        cur[0] = "co"
+        tc(X("FG", 0, 256), IND(fwin, la(0)))
+        for r in range(16):
+            mm(X("b2", 0, 16), X("WB16", 15 - r, 143 - r), X("FG", r, 256, 16), r == 0, r == 15)
+        tc(X("FW", 0, 16), X("b2", 0, 16))
+        tc(X("FWH", 0, 16), X("FW", 0, 16))
+        mm(X("b2", 0, 256), m128("IDB"), X("TBIG", 0, 256), True, False)
+        for r in range(16):
+            mm(X("b2", r, 256, 16), m128("IDH"), X("FWH", 0, 16), False, r == 15)
+        tt(X("EQD", 0, 256), X("FG", 0, 256), X("b2", 0, 256), OP.is_equal)
+        scan(X("SQD", 0, 256), X("RMH", 0, 256), X("EQD", 0, 256), OP.mult, OP.max)
+        for c in range(1, 16):
+            o = 8 * c * (c - 1)
+            ts(X("EQ", o, o + 16 * c), X("FG", 0, 16 * c), X("FW", c, c + 1), OP.is_equal)
+            add("A", "count", X("EQS", o, o + 16 * c), [X("EQ", o, o + 16 * c)], (X("CNT", c, c + 1),), max(64, 16 * c) * CY + 0.02)
+
+        def w(i, n=1):
+            return X("W", 16 * i, 16 * (i + n))
+        tt(w(1), X("CNT", 0, 16), X("SQD", 15, 256, 16), OP.add)
+        ts(w(2), w(1), 0, OP.is_equal)
+        tt(w(3), X("AW", 0, 16), X("AW", 16, 32), OP.not_equal)
+        tt(w(5), w(3), w(4), OP.mult)
+        tt(w(6), w(2), w(5), OP.mult)
+        tt(w(7), w(2), w(6), OP.subtract)
+        ts(w(12, 2), X("LW", 0, 32), 2047, OP.not_equal)
+        tt(w(14), w(12), w(13), OP.mult)
+        tt(w(15), w(14), w(6), OP.mult)
+        tt(w(10), X("AW", 16, 32), X("AW", 0, 16), OP.subtract)
+        tt(w(11), X("LW", 16, 32), X("LW", 0, 16), OP.subtract)
+        ts(w(26), w(5), -90, OP.mult, 99, OP.add)
+        ts(w(27), w(5), -90, OP.mult, 99, OP.add)
+        tt(w(16, 2), X("LW", 0, 32), X("DUF", 0, 32), OP.subtract)
+        for i in range(2):
+            tt(w(16 + i), w(16 + i), w(15), OP.mult)
+        if not last:
+            tt(w(18, 2), X("AW", 0, 32), X("DUF", 0, 32), OP.subtract)
+            for i in range(2):
+                tt(w(18 + i), w(18 + i), w(15), OP.mult)
+        cur[0] = ""
+        for i, src in enumerate(("SY", "SZ")):
+            for r in range(16):
+                mm(X("b5", 0, 32), X("WBW", 15 - r, 143 - r), X(src, 15 + 16 * r, 8192, 256), i == 0 and r == 0, i == 1 and r == 15)
+        act(X("XW", X0 + YMO, X0 + YMO + 256), X("SY", 15, 4096, 16))
+        act(X("XW", X0 + ZMO, X0 + ZMO + 256), X("SZ", 15, 4096, 16))
+        for i, src in enumerate(("SY", "SZ")):
+            for s in range(2):
+                mm(X("b6", 0, 256), m128("IDN" if s else "IDB"), X(src, 4096 * s + 15, 4096 * s + 4096, 16), i + s == 0, i + s == 2)
+        ts(X("GL", 0, 256), X("b6", 0, 256), 0, OP.is_gt)
+        ts(X("GL", 256, 512), X("b6", 0, 256), 0, OP.is_lt)
+        for r in range(16):
+            mm(X("b2", 0, 32), X("WBB", 15 - r, 143 - r), X("GL", r, 512, 16), r == 0, r == 15)
+        tc(X("SI", 0, 32), X("b5", 0, 32))
+        bs = "BS2" if last else "BS1"
+        ts(X("SI", 32, 48), X("SI", 0, 16), 127, OP.bitwise_and)
+        tt(X(bs, 32, 48), X("SI", 32, 48), X("RBK", 16 * rnd, 16 * rnd + 16), OP.add)
+        for i in range(3):
+            tt(w(41 + i), X("LW" if i == 2 else "AW", 0, 16), X(bs, 16 * i, 16 * i + 16), OP.subtract)
+            tt(w(44 + i), X("LW" if i == 2 else "AW", 16, 32), X(bs, 16 * i, 16 * i + 16), OP.subtract)
+        tt(w(20, 2), X("b2", 0, 32), w(26, 2), OP.is_ge)
+        for i in range(6):
+            tt(w(48 + i), w(20 + i // 3), w(41 + i), OP.mult)
+        tt(w(54, 3), w(48, 3), w(51, 3), OP.add)
+        tt(w(57, 3), w(54, 3), X(bs, 0, 48), OP.add)
+        ts(X("LT", 0, 48), w(57, 3), 0 if last else X0, OP.add)
+        tt(w(25), w(20), w(21), OP.add)
+        tt(w(34), w(25), w(16), OP.mult)
+        tt(w(35), w(25), w(17), OP.mult)
+        tt(w(36, 2), w(34, 2), X("DUF", 0, 32), OP.add)
+        tc(X("LF", 0, 32), w(36, 2))
+        add("V", "tc", IND(X("F", 0, 2576), X("LF", 0, 32)), [X("VALF", 0, 512)], (), 0.05 + 512 * 0.0031)
+        tt(w(28), w(21), w(10), OP.mult)
+        tt(w(32), w(28), X("AW", 0, 16), OP.add)
+        if not last:
+            tt(w(29), w(21), w(11), OP.mult)
+            tt(w(33), w(29), X("LW", 0, 16), OP.add)
+        twin = X("XW", X0, X0 + XEND) if last else X("XW", 0, X0 + R2O)
+        for i in range(3):
+            gat(X("TG", 256 * i, 256 * i + 256), IND(twin, X("LT", 16 * i, 16 * i + 16)), "AV")
+        for i in range(3):
+            mm(X("b3", 0, 256), m128("ID2" if i == 2 else "IDB"), X("TG", 256 * i, 256 * i + 256), i == 0, i == 2)
+        tt(w(38), w(2), w(25), OP.mult)
+        tt(w(39), w(38), w(7), OP.add)
+        tt(w(60), w(32), X("DUX", 0, 16), OP.subtract)
+        tt(w(61), w(60), w(39), OP.mult)
+        tt(w(62), w(61), X("DUX", 0, 16), OP.add)
+        tc(X("LX", 0, 16), w(62))
+        ts(X("VI", 0, 256), X("b3", 0, 256), 0.25, OP.mult, -0.375, OP.add)
+        add("W", "waitsent", X("XW", X0, X0 + 128), [], (rnd + 1,), 0)
+        add("V", "tc", IND(X("XW", X0, X0 + YMO), X("LX", 0, 16)), [X("VI", 0, 256)], (), 0.05 + 256 * 0.0031)
+        if last:
+            dma("S", ("d", "yf"), X("F", 0, 2048, 1, 0, 128), "d7")
+            for i in range(2):
+                dma("SA"[i], ("d", "yx%d" % i), X("XW", X0 + 1024 * i, X0 + 1024 * i + 1024), "d%d" % (8 + i))
+            break
+        add("G", "send", None, [X("XW", X0, X0 + 128)], (2,), 1.0)
+        add("N", "arrive", X("XW", X0 + R2O, X0 + XEND), [], (2,), 0)
+        ts(w(63), w(33), 2047, OP.is_equal)
+        tt(w(64), w(32), w(33), OP.subtract)
+        tt(w(65), w(63), w(64), OP.mult)
+        tt(w(66), w(65), w(33), OP.add)
+        tc(X("LS", 0, 16), w(66))
+        for s in range(2):
+            tt(X("KDD", 64 * s, 64 * s + 64), X("KF", 256 * s, 256 * s + 64), X("DM", 0, 64), OP.mult)
+        scan(X("KDS", 0, 128), X("RMH", 0, 128), X("KDD", 0, 128), OP.mult, OP.add)
+        tc(X("KN", 0, 8), X("KDS", 15, 128, 16))
+        tt(X("W", 1072, 1076), X("KN", 4, 8), X("KN", 0, 4), OP.subtract)
+        tt(X("W", 1076, 1080), X("W", 1072, 1076), X("W", 336, 340), OP.mult)
+        tt(X("LSI", 0, 4), X("W", 1076, 1080), X("KN", 0, 4), OP.add)
+        tt(X("SI", 48, 64), X("SI", 0, 16), X("SI", 16, 32), OP.add)
+        tt(X("LSI", 16, 32), X("SI", 48, 64), X("L977", 0, 16), OP.add)
+        ts(X("LSI", 4, 16), X("LSI", 20, 32), 2047, OP.bitwise_and)
+        tc(X("LS", 16, 32), X("LSI", 0, 16))
+        mm(X("b1", 0, 256), m128("BLK"), X("PL", 256, 512), True, False)
+        mm(X("b1", 0, 256), m128("NBLK"), X("PL", 0, 256), False, True)
+        tt(X("TK", 0, 256), X("b1", 0, 256), X("OHS", 0, 256), OP.mult)
+        ts(X("OHS", 256, 512), X("OHS", 256, 512), -1, OP.mult)
+        tt(X("TK", 256, 512), X("b1", 0, 256), X("OHS", 256, 512), OP.mult)
+        mm(X("b4", 0, 512), m128("IDH"), X("TK", 0, 512), True, False)
+        mm(X("b4", 0, 512), m128("IDH"), X("KF", 0, 512), False, True)
+        act(X("NK", 0, 512), X("b4", 0, 512))
+        for i in range(2):
+            tt(w(68 + i), w(25), w(18 + i), OP.mult)
+        tt(w(70, 2), w(68, 2), X("DUF", 0, 32), OP.add)
+        tc(X("LF", 32, 64), w(70, 2))
+        add("V", "tc", IND(X("KD", 0, 2576), X("LF", 32, 64)), [X("NK", 0, 512)], (), 0.05 + 512 * 0.0031)
+    return P
+
+
+def deps(P):
+    hist, n = {}, len(P)
+    preds = [dict() for _ in P]
+    for i, p in enumerate(P):
+        for acc, wr in [(a, False) for a in p["r"]] + [(a, True) for a in p["w"]]:
+            if acc[0] != "x":
+                continue
+            L = hist.setdefault(acc[1], [])
+            for j, b, bw in L:
+                if j == i:
+                    continue
+                if acc[1][0] == "b":
+                    both = p["q"] == "T" and P[j]["q"] == "T"
+                    if p["q"] != P[j]["q"] or ((wr or bw) and clash(acc, b) and not both):
+                        preds[i][j] = True
+                    else:
+                        preds[i].setdefault(j, False)
+                elif (wr or bw) and clash(acc, b):
+                    preds[i][j] = True
+            L.append((i, acc, wr))
+    return preds
+
+
+def order(P, preds):
+    n = len(P)
+    succ = [[] for _ in P]
+    for i in range(n):
+        for j in preds[i]:
+            succ[j].append(i)
+    prio = [0.0] * n
+    for i in range(n - 1, -1, -1):
+        lat = 2.0 if P[i]["what"] == "dma" else 0.0
+        prio[i] = P[i]["cost"] + lat + max([prio[k] + WK for k in succ[i]] + [0.0])
+    left = [len(p) for p in preds]
+    ready = {i: 0.0 for i in range(n) if not left[i]}
+    free = {q: 0.0 for q in "AVTGSNW"}
+    seq, queue = [], [None] * n
+    while ready:
+        cand = []
+        for i, t in ready.items():
+            qs = P[i]["q"]
+            q = min(qs, key=lambda z: max(free[z], t)) if len(qs) > 1 else qs
+            cand.append((max(free[q], t), -prio[i] - BOOST.get(P[i]["b"], 0.0), i, q))
+        first = min(cand)
+        st, _, i, q = min((c for c in cand if c[3] == first[3] and c[0] <= first[0] + SLACK), key=lambda c: (c[1], c[0]))
+        queue[i] = q
+        end = st + P[i]["cost"]
+        free[q] = end
+        if P[i]["what"] == "dma":
+            end += 2.0
+        if P[i]["what"] == "arrive":
+            end += 12.0
+        P[i]["t"] = (st, end)
+        seq.append(i)
+        del ready[i]
+        for k in succ[i]:
+            left[k] -= 1
+            if not left[k]:
+                ready[k] = max([P[j]["t"][1] + (WK if preds[k][j] else 0.0) for j in preds[k]])
+    return seq, queue, preds
+
+
+PLAN = {}
+
+
+def plan():
+    if not PLAN:
+        P = build()
+        preds = deps(P)
+        PLAN["p"] = (P,) + order(P, preds)
+    return PLAN["p"]
+
+
+def rank_program(g, core, T, topo):
+    rank = T.rank_of(core)
+    if rank is None:
+        return
+    P, seq, queue, preds = plan()
+    eng = {"V": g.vector, "A": g.scalar, "T": g.tensor, "G": g, "S": g.sync}
+    cores = list(T.cores)
+    n = len(cores)
+
+    def ap(a):
+        if a[0] == "i":
+            return ap(a[1]).indirect(ap(a[2]))
+        if a[0] == "d":
+            if a[1] == "yf":
+                return T.yf[:]
+            if a[1][:2] == "yx":
+                i = int(a[1][2:])
+                return T.yx[:, 1024 * i:1024 * i + 1024]
+            return T[a[1]][:]
+        _, name, lo, hi, st, p0, p1 = a
+        return T[name][p0:p1, lo:hi] if st == 1 else T[name][p0:p1, lo:hi:st]
+
+    def sc(s):
+        return ap(s) if isinstance(s, tuple) else s
+
+    count = {"V": 0, "A": 0, "T": 0, "G": 0}
+    done, total = {}, {}
+    seen = {q: {} for q in "VATGS"}
+
+    def wait(q, sem, v):
+        if seen[q].get(sem, 0) < v:
+            seen[q][sem] = v
+            eng[q].wait_ge(T.sem[sem], v)
+
+    extra = {}
+    for i in seq:
+        p, q = P[i], queue[i]
+        what, args = p["what"], p["args"]
+        if what == "arrive":
+            done[i] = [("arr%d" % args[0], ND * (n - 1))]
+            total["arr%d" % args[0]] = ND * (n - 1)
+            continue
+        if what == "waitsent":
+            done[i] = [s for j in preds[i] for s in done[j]] + [("sent%d" % args[0], ND)]
+            continue
+        need = {}
+        for j, hard in preds[i].items():
+            if hard:
+                for sem, v in done[j]:
+                    need[sem] = max(need.get(sem, 0), v)
+        for sem in sorted(need):
+            wait(q, sem, need[sem])
+        out = p["out"] and ap(p["out"])
+        ins = [ap(a) for a in p["ins"]]
+        e = eng[q]
+        if what == "dma":
+            src = ins[0]
+            if p["out"][1] == "yf":
+                src = T.F[0::16, 0:2048]
+            e.dma_start(out, src).then_inc(T.sem[args[0]], 16)
+            done[i] = [(args[0], 16)]
+            total[args[0]] = 16
+            continue
+        if what == "send":
+            base = (0 if args[0] == 1 else X0 + R2O)
+            others = [cores[(rank + d) % n] for d in range(1, n)]
+            engines = [x for x in topo.engines(core, others[0]) if all(x in topo.engines(core, o) for o in others)][:ND]
+            ids, dsts = [], []
+            for o in others:
+                rid, pid, _s = topo.addr(o)
+                slot = (rank - T.rank_of(o) - 1) % n
+                ids.append(DstId(rid=rid, pnc=pid))
+                dsts.append(T.XW[:, base + 128 * slot:base + 128 * slot + 128])
+            g.remote_dma_fused([RemoteDMATransfer(dst_ids=ids, dma_engine_mask=sum(1 << x for x in engines), remote_sem=T.sem["arr%d" % args[0]], srcs=[ins[0]], dsts=dsts)], local_sem=T.sem["sent%d" % args[0]])
+            done[i] = [("sent%d" % args[0], ND)]
+            total["sent%d" % args[0]] = ND
+            continue
+        if what == "tc" or (what == "gat" and q == "V"):
+            h = e.tensor_copy(out, ins[0])
+        elif what == "gat":
+            h = e.activation(out, ins[0], AF.Copy)
+        elif what == "count":
+            h = e.activation(out, ins[0], AF.Copy, accum_out=ap(args[0]))
+        elif what == "sq":
+            h = e.activation(out, ins[0], AF.Square, bias=ins[1])
+        elif what == "relu":
+            h = e.activation(out, ins[0], AF.Relu)
+        elif what == "act":
+            h = e.activation(out, ins[0], AF.Identity, bias=ins[1]) if args[0] else e.activation(out, ins[0], AF.Copy)
+        elif what == "tt":
+            h = e.tensor_tensor(out, ins[0], ins[1], args[0])
+        elif what == "ts":
+            s1, o1, s2, o2 = args
+            h = e.tensor_scalar(out, ins[0], sc(s1), None, o1) if o2 is None else e.tensor_scalar(out, ins[0], sc(s1), sc(s2), o1, o2)
+        elif what == "scan":
+            h = e.tensor_tensor_scan(out, ins[0], ins[1], 0.0, args[0], args[1])
+        elif what == "mm":
+            h = e.matmul(out, ins[0], ins[1], args[0], args[1])
+        elif what == "tr":
+            h = e.transpose(out, ins[0])
+        elif what == "ms":
+            h = e.memset(out, args[0])
+        elif what == "iota":
+            h = e.iota(out, args[0], args[2], args[1], allow_small_or_imprecise_dtypes=True)
+        h.then_inc(T.sem["q" + q], 1)
+        count[q] += 1
+        done[i] = [("q" + q, count[q])]
+    for q in "VATG":
+        if count[q]:
+            wait("S", "q" + q, count[q])
+    for sem in sorted(total):
+        wait("S", sem, total[sem])

@@ -1,42 +1,43 @@
 from concourse.bass import DstId, RemoteDMATransfer
 from concourse.mybir import AluOpType as OP, ActivationFunctionType as AF
 
-X0, XA, XD, YMO, ZMO, R2O = 896, 2048, 2064, 2320, 2576, 2832
+X0, XA, XD, MO, R2O = 896, 2048, 2064, 2320, 2832
 XEND = R2O + 896
 ND = 4
+MARK = (0.25, 0.375)
 
 SCRATCH = {}
 for _n, _w, _d in (
-        ("XW", X0 + XEND, "bfloat16"), ("KD", 2576, "int32"), ("F", 2576, "float32"), ("M", 2048, "bfloat16"), ("VAL", 2048, "bfloat16"), ("CM", 2048, "bfloat16"),
+        ("XW", X0 + XEND, "bfloat16"), ("KD", 2576, "int32"), ("F", 2576, "float32"), ("DP", 2048, "bfloat16"),
         ("FAI", 128, "int32"), ("DPI", 128, "int32"), ("PAI", 16, "int32"), ("PBI", 16, "int32"), ("WTI", 1, "int32"), ("FDH", 256, "float16"),
-        ("PI", 1, "int32"), ("TI", 2, "int32"), ("COL", 32, "float32"), ("NF", 256, "float32"), ("NR", 256, "float32"), ("NG", 256, "float32"),
-        ("BLK", 128, "float16"), ("NBLK", 128, "float16"), ("WBH", 144, "float16"), ("WB16", 144, "float16"), ("WBB", 144, "bfloat16"), ("WBW", 144, "bfloat16"),
-        ("IDB", 128, "bfloat16"), ("IDN", 128, "bfloat16"), ("ID2", 128, "bfloat16"), ("IDH", 128, "float16"), ("IDM", 128, "bfloat16"), ("BSEL", 2048, "float16"), ("DELR", 16, "float32"), ("B8", 16, "float32"),
-        ("DM", 256, "bfloat16"), ("RMH", 256, "float16"), ("RMB", 1024, "bfloat16"), ("SEL", 8, "bfloat16"), ("KC", 256, "bfloat16"), ("E0", 128, "bfloat16"), ("ZB", 512, "bfloat16"),
-        ("L15", 16, "uint16"), ("DLT", 128, "bfloat16"), ("S1", 128, "bfloat16"), ("S2", 128, "bfloat16"), ("S3", 128, "bfloat16"), ("S4", 128, "bfloat16"), ("S5", 128, "bfloat16"), ("S6", 256, "bfloat16"), ("E4", 256, "float32"), ("E1", 128, "float32"), ("E2", 128, "float32"), ("E3", 128, "float32"), ("P0", 128, "float32"),
-        ("TA", 128, "bfloat16"), ("TB", 128, "bfloat16"), ("DMX", 128, "bfloat16"), ("MS", 128, "bfloat16"), ("RT", 128, "bfloat16"), ("RTN", 128, "bfloat16"), ("RD", 128, "bfloat16"),
-        ("LN", 16, "float32"), ("L977", 16, "float32"), ("QI", 32, "int32"), ("QF", 32, "float32"), ("TBIG", 256, "bfloat16"), ("DUX", 16, "float32"), ("DUF", 32, "float32"),
-        ("RBK", 32, "float32"), ("CNT", 16, "float32"), ("BS1", 48, "float32"), ("BS2", 48, "float32"), ("EQ", 2560, "bfloat16"), ("EQS", 2560, "bfloat16"), ("PX", 64, "float32"), ("PT", 64, "float32"), ("PU", 32, "float32"),
-        ("GM", 2560, "bfloat16"), ("G5", 512, "bfloat16"), ("G", 2048, "float16"), ("SC", 2048, "float16"), ("LS", 160, "uint16"), ("LSI", 32, "int32"),
-        ("VA", 256, "float16"), ("PR", 512, "float16"), ("AW", 32, "float32"), ("LA", 32, "uint16"), ("VALF", 512, "float32"),
-        ("KL", 512, "uint16"), ("KF", 512, "float16"), ("XS", 512, "bfloat16"), ("Y", 8192, "bfloat16"), ("SY", 8192, "bfloat16"), ("MM", 8192, "bfloat16"),
-        ("KS", 512, "float32"), ("PS", 512, "float32"), ("OHT", 512, "bfloat16"), ("OHS", 512, "bfloat16"), ("PL", 512, "float16"), ("LL", 32, "uint16"), ("LW", 32, "float32"),
-        ("ZK", 512, "uint16"), ("Z", 8192, "bfloat16"), ("SZ", 8192, "bfloat16"), ("FG", 512, "float16"), ("FW", 32, "float32"), ("FWH", 16, "float16"),
-        ("EQD", 256, "bfloat16"), ("SQD", 256, "bfloat16"), ("GL", 512, "bfloat16"), ("W", 1152, "float32"), ("SI", 64, "int32"), ("KDD", 128, "float16"), ("KDS", 128, "float16"), ("KN", 8, "float32"),
+        ("PI", 1, "int32"), ("TI", 3, "int32"), ("COL", 32, "float32"), ("NF", 128, "float32"), ("NR", 272, "float32"), ("NG", 256, "float32"),
+        ("BLK", 128, "float16"), ("NBLK", 128, "float16"), ("WBH", 144, "float16"), ("WBB", 144, "bfloat16"), ("WBW", 144, "bfloat16"),
+        ("IDB", 128, "bfloat16"), ("IDN", 128, "bfloat16"), ("ID2", 128, "bfloat16"), ("IDH", 128, "float16"), ("BSEL", 2048, "float16"), ("DELR", 16, "float32"),
+        ("RMH", 256, "float16"), ("SEL", 8, "bfloat16"), ("KC", 256, "bfloat16"), ("E0", 256, "bfloat16"), ("RMB", 1024, "bfloat16"),
+        ("L15", 16, "uint16"), ("LN", 16, "float32"), ("L977", 16, "float16"), ("QI", 64, "int32"), ("QT", 192, "float32"), ("R3", 192, "bfloat16"), ("CH", 288, "float32"), ("CS", 288, "float32"), ("MD", 96, "float32"), ("CE", 176, "float32"), ("QF", 32, "float32"), ("TBIG", 256, "bfloat16"), ("DUF", 48, "float32"),
+        ("RBK", 32, "float32"), ("CNT", 16, "float32"), ("EQ", 1920, "bfloat16"), ("EQS", 1920, "bfloat16"),
+        ("PX", 64, "float32"), ("PT", 64, "float32"), ("PU", 32, "float32"),
+        ("G", 3072, "float32"), ("SC", 3072, "float32"), ("LS", 160, "uint16"), ("LU", 32, "uint16"), ("LSI", 32, "int32"), ("HM", 800, "bfloat16"), ("DS", 96, "float32"), ("PM", 32, "float32"),
+        ("HK", 160, "float32"), ("C", 192, "float32"), ("E6", 112, "float32"), ("N6", 112, "float32"), ("PC", 288, "float32"), ("SS", 288, "float32"),
+        ("AW", 32, "float32"), ("AWH", 32, "float16"), ("LA", 32, "uint16"), ("VALF", 512, "float32"),
+        ("KL", 512, "uint16"), ("KF", 512, "float16"), ("XS", 512, "bfloat16"), ("Y", 8192, "bfloat16"), ("MM", 8192, "bfloat16"),
+        ("EJ", 128, "bfloat16"), ("PS", 512, "float32"), ("OHT", 544, "bfloat16"), ("OHS", 512, "bfloat16"), ("PL", 512, "float16"), ("LL", 32, "uint16"), ("LW", 32, "float32"),
+        ("ZK", 512, "uint16"), ("Z", 8192, "bfloat16"), ("SZ", 8192, "bfloat16"), ("SY", 8192, "bfloat16"), ("HF", 2560, "float32"), ("FG", 256, "float16"), ("FWH", 16, "float16"), ("FW", 16, "float32"), ("FL", 16, "uint16"),
+        ("EQD", 256, "bfloat16"), ("SQD", 256, "bfloat16"), ("GL", 512, "bfloat16"), ("W", 1152, "float32"), ("SI", 64, "int32"), ("KDS", 128, "float32"), ("KN", 48, "float32"),
         ("LT", 48, "uint16"), ("LX", 16, "uint16"), ("LF", 64, "uint16"), ("TG", 768, "bfloat16"), ("VI", 256, "int32"), ("TK", 512, "float16"), ("NK", 512, "float32")):
     SCRATCH[_n] = ("sbuf", [128, _w], _d)
 for _b in range(8):
     SCRATCH["b%d" % _b] = ("psum", [128, 512], "float32")
 SEMAPHORES = ["qV", "qA", "qT", "qG", "sent1", "sent2", "arr1", "arr2"] + ["d%d" % _i for _i in range(12)]
 
-VY = ((1, 0),)
-RELU = ((1, 0),)
-VG = ((0, 0), (1, 1), (1, 3))
-SLACK = 0.0
-KSA, FQ, MQ, GQ = "VA", "VAAV", "AAVA", "AAAAAAAAVA"
-BOOST = {"ma": 6.0, "la": 20.0, "lb": -2.0, "SZ": 32.0, "zb": -4.0, "za": -4.0}
-G5Q = "AAAA"
-CY, GA, WK = 0.00104, 0.00135, 0.09
+CFG = dict(
+    Y00="VAAA", Y01="AAAA", Y10="VAAA", Y11="AAAA", Z00="AAAV", Z01="AAAAAAAV", Z10="AAAA", Z11="AAAAAAAV",
+    RQ="VVVVVVVV",
+    CQ="AAVAVAVAAVAVAAAAAAAAAAAA", FQ="AVAVAVAA", TQ="AAAAAA", SM="VA", CP="AVVAVAAAVV",
+    PUT=[1, 2, 1, 1, 2],
+    SLACK={'T': 0, 'V': 0.6, 'A': 0.6}, MARGIN=0.0, KEEP=2, SWEEPS=3,
+    BOOST={'1': 6, 'vd0': 3, 'lb0': 3, 'zb0': 3, 'co0': -12, '': -12, 'cl0': 6, 'za1': 1, 'yb0': 6, 'nb0': -1, '0': 1, 'la0': -1, 'fs0': 12, 'ya1': 3, 'yb1': -1})
+CY, GA, SCA, WS, WK, BW = 0.00085, 0.00115, 0.003, 0.19, 0.19, 400e3
 
 
 def X(name, lo, hi, st=1, p0=0, p1=128):
@@ -79,15 +80,33 @@ def psum(a):
 
 def build():
     P = []
-    cur = [""]
+    cur = ["", ""]
+    now, nuse, unit = {}, [0], [None]
+
+    def content(a, fresh=False):
+        if not (isinstance(a, tuple) and a and psum(a)):
+            return a
+        if fresh and now.get(a[1], (0, True))[1]:
+            nuse[0] += 1
+            now[a[1]] = (nuse[0], False)
+        return ("x", "b%d" % now[a[1]][0]) + a[2:]
 
     def add(qs, what, out, ins, args, cost):
-        P.append(dict(b=cur[0], q=qs, what=what, out=out, ins=ins, args=args, cost=cost, w=(spans(out) if out else []) + (list(args) if what == "count" else []), r=[s for i in ins for s in spans(i)]))
+        for a in ins:
+            if psum(a):
+                now[a[1]] = (now[a[1]][0], True)
+        out, ins, args = content(out, what == "mm" and args[0]), [content(a) for a in ins], tuple(content(a) for a in args)
+        use = sorted({int(a[1][1:]) for a in [out] + ins if a and psum(a)})
+        P.append(dict(b=cur[0] + cur[1], g=len(P) if unit[0] is None else unit[0], use=use, q=qs, what=what, out=out, ins=ins, args=args, cost=cost,
+                      w=(spans(out) if out else []) + (list(args) if what == "count" else []), r=[s for i in ins for s in spans(i)]))
+
+    def together(on):
+        unit[0] = len(P) if on else None
 
     def ccost(out, ins, fast):
         n = width(out)
         if out[0] == "i":
-            return 0.05 + n * 0.0031
+            return 0.05 + n * SCA
         if ins[0][0] == "i":
             return 0.05 + n * GA
         return max(64, n * (0.5 if fast and two(out) and all(two(i) for i in ins) else 1)) * CY
@@ -97,220 +116,262 @@ def build():
 
     def tt(out, a, b, op):
         n = width(b)
-        c = 0.05 + n * GA if a[0] == "i" else max(64, n * (1 if psum(a) or psum(b) else 2)) * CY
+        c = ccost(out, [a], False) if "i" in (a[0], out[0]) else max(64, n * (1 if psum(a) or psum(b) else 2)) * CY
         add("V", "tt", out, [a, b], (op,), c)
 
     def ts(out, a, s1, o1, s2=None, o2=None):
         ins = [a] + [s for s in (s1, s2) if isinstance(s, tuple)]
         add("V", "ts", out, ins, (s1, o1, s2, o2), ccost(out, [a], True))
 
-    def scan(out, d0, d1, o0, o1):
-        add("V", "scan", out, [d0, d1], (o0, o1), ccost(out, [d0, d1], True))
+    def scan(out, d0, d1, o0, o1, init=0.0):
+        add("V", "scan", out, [d0, d1] + ([init] if isinstance(init, tuple) else []), (o0, o1, init), ccost(out, [d0, d1], True))
 
-    def act(out, a, bias=None):
+    def act(out, a, bias=None, scale=1.0, func=None):
         c = 0.065 + width(out) * GA if a[0] == "i" else max(64, width(out)) * CY
-        add("A", "act", out, [a] + ([bias] if bias else []), (bias,), c)
+        add("A", "act", out, [a] + [s for s in (bias, scale) if isinstance(s, tuple)], (bias, scale, func), c)
 
-    def relu(out, a):
-        add("A", "relu", out, [a], (), width(out) * CY)
+    def lin(q, out, a, scale, bias, cut=False):
+        if q == "A":
+            act(out, a, bias, scale, "Relu" if cut else None)
+        elif cut:
+            ts(out, a, bias if scale == 1.0 else scale, OP.add if scale == 1.0 else OP.mult, 0, OP.max)
+        else:
+            ts(out, a, scale, OP.mult, bias, OP.add)
 
     def gat(out, a, q="A"):
         add(q, "gat", out, [a], (), 0.06 + width(out) * GA)
 
+    def put(win, lst, src, n):
+        k = width(lst) // n
+        for i in range(n):
+            tc(IND(win, X(lst[1], lst[2] + k * i, lst[2] + k * i + k)), X(src[1], src[2] + 16 * k * i, src[2] + 16 * k * (i + 1)))
+
     def mm(out, l, r, start, stop):
         add("T", "mm", out, [l, r], (start, stop), max(64, width(r)) * CY)
 
+    def wrap(out, sel, src, start=True, stop=True, step=1):
+        together(True)
+        for r in range(16):
+            mm(out, X(sel, 15 - r, 143 - r), X(src[1], src[2] + r * step, src[3], 16 * step), start and r == 0, stop and r == 15)
+        together(False)
+
     def dma(q, out, a, sem):
-        add(q, "dma", out, [a], (sem,), 0.06)
+        s = out if out[0] == "x" else a
+        add(q, "dma", out, [a], (sem, width(s) * (2 if two(s) else 4) * (8 if out[1] == "yf" else 128) / BW), 0.06)
 
     def iota(out, pat, cm, base=0):
         add("G", "iota", out, [], (pat, cm, base), 0.13 + 2 * width(out) * CY)
 
+    def ms(out, v):
+        add("V", "ms", out, [], (v,), max(64, width(out) * (0.5 if two(out) else 1)) * CY)
+
     def col(i):
         return X("COL", i, i + 1)
 
-    dma("S", X("FAI", 0, 128), ("d", "fa"), "d0")
-    dma("A", X("DPI", 0, 128), ("d", "dp"), "d1")
-    dma("S", X("PAI", 0, 16), ("d", "pa"), "d2")
+    def m128(n):
+        return X(n, 0, 128)
+
+    def w(i, n=1):
+        return X("W", 16 * i, 16 * (i + n))
+
+    together(True)
+    dma("A", X("FAI", 0, 128), ("d", "fa"), "d0")
     dma("A", X("PBI", 0, 16), ("d", "pb"), "d3")
-    dma("S", X("KD", 0, 2048), ("d", "kd"), "d5")
-    dma("S", X("XW", X0, X0 + 2048), ("d", "xs"), "d6")
+    together(True)
+    dma("S", X("DPI", 0, 128), ("d", "dp"), "d1")
+    dma("S", X("PAI", 0, 16), ("d", "pa"), "d2")
     dma("S", X("WTI", 0, 1), ("d", "wt"), "d4")
+    dma("S", X("XW", X0, X0 + 2048), ("d", "xs"), "d6")
+    dma("S", X("KD", 0, 2048), ("d", "kd"), "d5")
+    together(False)
     add("G", "send", None, [X("XW", X0, X0 + 128)], (1,), 1.0)
     add("N", "arrive", X("XW", 0, 896), [], (1,), 0)
 
     iota(X("PI", 0, 1), [[0, 1]], 1)
-    iota(X("NF", 0, 256), [[1, 256]], 0)
-    iota(X("NG", 0, 256), [[1, 16], [0, 16]], 0)
-    iota(X("NR", 0, 256), [[0, 16], [1, 16]], 0)
-    iota(X("XW", X0 + XA, X0 + YMO), [[0, YMO - XA]], 0)
+    iota(m128("NG"), [[1, 8], [0, 16]], 0)
+    iota(m128("NF"), [[1, 128]], 0)
+    iota(X("NR", 0, 272), [[0, 17], [1, 16]], 0)
+    iota(X("XW", X0 + XA, X0 + MO), [[0, MO - XA]], 0)
+    iota(X("F", XA, XD), [[0, XD - XA]], 0)
+    iota(X("E6", 0, 16), [[0, 16]], 0)
+    iota(X("N6", 0, 16), [[0, 16]], 0)
+    ms(X("WBH", 0, 144), 0.0)
+    iota(X("KC", 0, 256), [[0, 16], [-1, 16]], 0, 15)
+    iota(X("CNT", 0, 1), [[0, 1]], 0)
     ts(X("TI", 0, 1), X("PI", 0, 1), 15, OP.bitwise_and)
     ts(X("TI", 1, 2), X("PI", 0, 1), 4, OP.arith_shift_right)
+    ts(X("TI", 2, 3), X("TI", 1, 2), 1, OP.bitwise_and)
     tc(X("COL", 0, 2), X("TI", 0, 2))
     tc(col(2), X("PI", 0, 1))
-    N128, R128, G128 = X("NF", 0, 128), X("NR", 0, 128), X("NG", 0, 128)
+    tc(col(3), X("TI", 2, 3))
+    ts(col(4), col(3), -1, OP.mult, 1, OP.add)
     pr, pg, pc = col(0), col(1), col(2)
-    ts(X("BLK", 0, 128), G128, pg, OP.is_equal)
-    ts(X("DELR", 0, 16), X("NF", 0, 16), pr, OP.is_equal)
+    n16 = X("NF", 0, 16)
+    ts(m128("BLK"), m128("NG"), pg, OP.is_equal)
+    ts(X("DELR", 0, 16), n16, pr, OP.is_equal)
     for r in range(16):
-        ts(X("BSEL", 128 * r, 128 * r + 128), X("BLK", 0, 128), X("DELR", r, r + 1), OP.mult)
-    ts(col(6), pr, 1, OP.is_lt)
-    ts(col(15), pr, 6, OP.is_ge)
-    ts(col(5), pr, 11, OP.is_ge)
-    ts(col(3), pr, 1, OP.is_ge)
-    tt(col(3), col(3), col(15), OP.subtract)
-    tt(col(4), col(15), col(5), OP.subtract)
-    ts(col(7), col(3), 16, OP.mult)
-    ts(col(8), col(5), -4096, OP.mult)
-    ts(col(16), col(4), 5, OP.mult, pr, OP.subtract)
-    ts(col(17), col(5), 10, OP.mult)
-    tt(col(10), col(16), col(17), OP.add)
-    ts(col(18), pr, 1, OP.is_ge, -8192, OP.mult)
-    ts(col(19), pr, 1, OP.is_lt)
-    tc(X("FDH", 0, 128), X("FAI", 0, 128))
-    tc(X("FDH", 128, 256), X("DPI", 0, 128))
+        ts(X("BSEL", 128 * r, 128 * r + 128), m128("BLK"), X("DELR", r, r + 1), OP.mult)
+    tc(X("FDH", 0, 128), m128("DPI"))
+    tc(X("FDH", 128, 256), m128("FAI"))
     for k in range(2):
-        for r in range(16):
-            b = "b%d" % (4 * k + r // 4)
-            mm(X(b, 128 * (r % 4), 128 * (r % 4) + 128), X("BSEL", 128 * r, 128 * r + 128), X("FDH", 128 * k, 128 * k + 128), True, True)
-    for i in range(4):
-        (act if FQ[i] == "A" else tc)(X("F", 512 * i, 512 * i + 512), X("b%d" % i, 0, 512))
-    add("V", "ms", X("F", XA, XD), [], (2047.0,), 0.066)
-    add("V", "ms", X("KD", XA, XD), [], (2047,), 0.066)
-    ts(X("E1", 0, 128), G128, col(3), OP.mult)
-    ts(X("E2", 0, 128), R128, col(4), OP.mult, col(5), OP.add)
-    tt(X("P0", 0, 128), X("E1", 0, 128), X("E2", 0, 128), OP.add)
-    ts(X("B8", 0, 16), X("NF", 0, 16), 8, OP.mult, col(3), OP.mult)
-    for r in range(16):
-        act(X("VAL", 128 * r, 128 * r + 128), X("P0", 0, 128), X("B8", r, r + 1))
-    ts(X("IDB", 0, 128), N128, pc, OP.is_equal)
-    ts(X("IDM", 0, 128), X("IDB", 0, 128), -256, OP.mult)
-    for i in range(4):
-        add("A", "sq", X("CM", 512 * i, 512 * i + 512), [X("b%d" % (4 + i), 0, 512), col(10)], (), 512 * CY)
-        mm(X("b%d" % i, 0, 512), X("IDB", 0, 128), X("VAL", 512 * i, 512 * i + 512), True, False)
-        mm(X("b%d" % i, 0, 512), X("IDM", 0, 128), X("CM", 512 * i, 512 * i + 512), False, True)
-        if MQ[i] == "A":
-            relu(X("M", 512 * i, 512 * i + 512), X("b%d" % i, 0, 512))
-        else:
-            ts(X("M", 512 * i, 512 * i + 512), X("b%d" % i, 0, 512), 0, OP.max)
-    ts(X("TI", 0, 1), X("TI", 1, 2), 1, OP.bitwise_and)
-    tc(col(14), X("TI", 0, 1))
-    ts(col(13), col(14), -1, OP.mult, 1, OP.add)
+        for i in range(4):
+            together(True)
+            for r in range(4 * i, 4 * i + 4):
+                mm(X("b0", 128 * (r % 4), 128 * (r % 4) + 128), X("BSEL", 128 * r, 128 * r + 128), X("FDH", 128 * k, 128 * k + 128), True, True)
+            together(False)
+            (act if CFG["FQ"][4 * k + i] == "A" else tc)(X("F" if k else "DP", 512 * i, 512 * i + 512), X("b0", 0, 512))
     for s in range(2):
         src = X("PBI" if s else "PAI", 0, 16)
-        ts(X("PX", 32 * s, 32 * s + 16), src, col(13), OP.mult)
-        ts(X("PX", 32 * s + 16, 32 * s + 32), src, col(14), OP.mult)
+        ts(X("PX", 32 * s, 32 * s + 16), src, col(4), OP.mult)
+        ts(X("PX", 32 * s + 16, 32 * s + 32), src, col(3), OP.mult)
     add("V", "tr", X("PT", 0, 64), [X("PX", 0, 64)], (), 0.07)
     for s in range(2):
         tt(X("PU", 16 * s, 16 * s + 16), X("PT", 32 * s, 32 * s + 16), X("PT", 32 * s + 16, 32 * s + 32), OP.add)
-    tc(X("LS", 0, 32), X("PU", 0, 32))
-    ts(X("DM", 0, 256), X("NR", 0, 256), pr, OP.is_equal)
     ts(X("RMH", 0, 256), X("NR", 0, 256), 0, OP.not_equal)
-    m128 = lambda n: X(n, 0, 128)
-    dl, e3, s1, s2 = m128("DLT"), m128("E3"), m128("S1"), m128("S2")
-    ts(e3, R128, 5, OP.is_gt, 1000, OP.mult)
-    ts(m128("S3"), m128("BLK"), -1000, OP.mult, 1000, OP.add)
-    tt(m128("E4"), R128, e3, OP.add)
-    ts(X("E4", 128, 256), m128("E4"), pr, OP.subtract)
-    tt(dl, X("E4", 128, 256), m128("S3"), OP.add)
-    ts(s1, dl, 1, OP.is_equal, col(7), OP.mult)
-    ts(s2, dl, -4, OP.is_equal, col(4), OP.mult)
-    tt(m128("TA"), s1, s2, OP.add)
-    ts(m128("TB"), m128("TA"), -1, OP.mult)
-    ts(m128("MS"), dl, -10, OP.is_le, col(8), OP.mult)
-    ts(m128("S4"), dl, 0, OP.is_equal, col(7), OP.mult)
-    ts(m128("S5"), dl, -5, OP.is_equal, col(4), OP.mult)
-    tt(m128("S6"), m128("S4"), m128("S5"), OP.add)
-    tt(m128("DMX"), m128("S6"), m128("TA"), OP.subtract)
-    ts(m128("RT"), dl, 1, OP.is_equal, col(6), OP.mult)
-    ts(m128("RTN"), m128("RT"), -1, OP.mult)
-    ts(X("S6", 128, 256), dl, 0, OP.is_equal, col(6), OP.mult)
-    tt(m128("RD"), X("S6", 128, 256), m128("RT"), OP.subtract)
-    iota(X("ZB", 0, 512), [[0, 512]], 0)
-    iota(X("RMB", 0, 1024), [[0, 64], [512, 16]], 0)
-    iota(X("KC", 0, 256), [[0, 16], [-1, 16]], 0, 15)
-    ts(X("WBH", 0, 144), X("NF", 0, 144), 0, OP.mult)
+    ts(X("HM", 256, 528), X("NR", 0, 272), pr, OP.is_equal, -4096, OP.mult)
+    ts(X("HM", 544, 800), X("HM", 257, 513), -2, OP.mult)
+    tt(X("HM", 0, 256), X("HM", 256, 512), X("HM", 544, 800), OP.add)
+    ts(col(9), pr, 0, OP.is_equal, 8192, OP.mult)
+    ts(col(8), col(9), -4096, OP.add)
+    ts(col(7), col(8), -1, OP.mult)
+    tc(col(16), X("HM", 15, 16))
+    ts(X("COL", 17, 22), X("NF", 1, 6), -4096, OP.mult, col(16), OP.add)
+    for i in range(10):
+        act(X("HF", 256 * i, 256 * i + 256), X("HM", 0, 256))
+
+    def hold(out, src):
+        scan(out, src, X("HM", 0, width(out)), OP.min, OP.add, 4096.0)
     ts(X("WBH", 15, 143, 16), X("NF", 0, 8), pg, OP.is_equal)
-    ts(X("WB16", 0, 144), X("WBH", 0, 144), 0.0625, OP.mult)
     tc(X("WBB", 0, 144), X("WBH", 0, 144))
-    tc(col(12), X("WTI", 0, 1))
-    ts(X("WBW", 0, 144), X("WBB", 0, 144), col(12), OP.mult)
+    tc(col(6), X("WTI", 0, 1))
+    ts(X("WBW", 0, 144), X("WBB", 0, 144), col(6), OP.mult)
+    ts(m128("IDB"), m128("NF"), pc, OP.is_equal)
     ts(m128("NBLK"), m128("BLK"), -1, OP.mult)
     ts(m128("IDN"), m128("IDB"), -1, OP.mult)
     ts(m128("ID2"), m128("IDB"), 2, OP.mult)
     tc(m128("IDH"), m128("IDB"))
     ts(X("SEL", 0, 8), X("NF", 0, 8), pg, OP.is_equal, 16, OP.mult)
-    ts(col(11), pc, 0, OP.is_equal)
-    ts(m128("E0"), N128, 0, OP.mult, col(11), OP.add)
-    ts(X("L15", 0, 16), X("NF", 0, 16), 16, OP.mult, 15, OP.add)
-    n16 = X("NF", 0, 16)
-    ts(X("LN", 0, 16), n16, 16, OP.mult, pr, OP.add)
+    ts(col(5), pc, 0, OP.is_equal)
+    act(X("E0", 0, 256), X("NR", 0, 256), col(5), 0.0)
+    ts(m128("EJ"), X("NR", 0, 128), 0, OP.is_equal, col(5), OP.mult)
+    for s in range(2):
+        iota(X("OHT", 272 * s, 272 * s + 16), [[0, 16]], 0, 1)
+    iota(X("RMB", 0, 1024), [[0, 64], [512, 16]], 0)
+    tc(X("L15", 0, 16), n16)
     ln = X("LN", 0, 16)
-    ts(X("L977", 0, 16), ln, 977, OP.mult)
+    ts(ln, n16, 16, OP.mult, pr, OP.add)
     ts(X("QI", 0, 16), ln, 9363, OP.mult)
     ts(X("QI", 16, 32), X("QI", 0, 16), 16, OP.arith_shift_right)
     ts(X("QF", 0, 16), X("QI", 16, 32), -7, OP.mult)
     tt(X("QF", 16, 32), X("QF", 0, 16), ln, OP.add)
-    for i, (nm, base) in enumerate((("BS1", -896), ("BS2", R2O))):
-        ts(X(nm, 0, 16), ln, YMO, OP.add)
-        ts(X(nm, 16, 32), ln, ZMO, OP.add)
-        ts(X("RBK", 16 * i, 16 * i + 16), X("QF", 16, 32), 128, OP.mult, base, OP.add)
-    add("V", "ms", X("CNT", 0, 1), [], (0.0,), 0.066)
+    for i, base in enumerate((-896, R2O)):
+        lin("A", X("RBK", 16 * i, 16 * i + 16), X("QF", 16, 32), 128.0, float(base))
     ts(X("TBIG", 0, 256), X("NR", 0, 256), pr, OP.is_ge, 4096, OP.mult)
-    ts(X("DUX", 0, 16), ln, XD, OP.add)
-    ts(X("DUF", 0, 16), ln, XD, OP.add)
-    ts(X("DUF", 16, 32), ln, XD + 256, OP.add)
+    for i in range(2):
+        lin("A", X("DUF", 16 * i, 16 * i + 16), ln, 1.0, float(XD + 256 * i))
+    dux = X("DUF", 0, 16)
 
-    xwin, kwin, fwin, mwin = X("XW", X0, X0 + XD), X("KD", 0, XD), X("F", 0, XD), X("M", 0, 2048)
+    iota(X("QT", 0, 192), [[0, 64], [1, 3]], 0)
+    ts(X("R3", 0, 192), X("QT", 0, 192), 0, OP.not_equal)
+    for i in range(2):
+        lin("A", X("CH", 48 * i, 48 * i + 48, 3), ln, 1.0, float(XD + 256 * i))
+        lin("A", X("CH", 96 + 48 * i, 144 + 48 * i, 3), ln, 1.0, float(MO + 256 * i))
+        for s in range(2):
+            lin("A", X("MD", 32 * i + 16 * s, 32 * i + 16 * s + 16), ln, 1.0, float(MO + 256 * i))
+        lin("A", X("MD", 64 + 16 * i, 80 + 16 * i), ln, 1.0, float(XD))
+    ts(X("QI", 32, 48), ln, 977, OP.mult)
+    ts(X("QI", 48, 64), X("QI", 32, 48), 2047, OP.bitwise_and)
+    tc(X("L977", 0, 16), X("QI", 48, 64))
+
+    def choose(out, first, changes, *more):
+        for i, d in enumerate(changes):
+            for s in range(2):
+                tt(X("CH", 48 * (first + i) + 1 + s, 48 * (first + i + 1), 3), w(20 + s), d[s], OP.mult)
+        lo, hi = 48 * first, 48 * (first + len(changes))
+        scan(X("CS", lo, hi), X("R3", 0, hi - lo), X("CH", lo, hi), OP.mult, OP.add)
+        ts(out, X("CS", lo + 2, hi, 3), *more)
+
+    xwin, kwin, fwin, dwin = X("XW", X0, X0 + 2048), X("KD", 0, 2048), X("F", 0, XD), X("DP", 0, 2048)
     for rnd in range(2):
         last = rnd == 1
-        mm(X("b1", 0, 512), m128("IDB"), X("ZB", 0, 512), True, False)
-        for k in range(5):
+        sm, relu = CFG["SM"][rnd], [(s, h) for s in range(2) for h in range(2) if CFG["RQ"][4 * rnd + 2 * s + h] == "A"]
+        cur[0], cur[1] = "cl", str(rnd)
+        if not last:
+            tc(X("LU", 0, 32), X("PU", 0, 32))
             for s in range(2):
-                ls = X("LS", 32 * k + 16 * s, 32 * k + 16 * s + 16)
-                o = 256 * s
-                if k < 4:
-                    g = X("G", 512 * k + o, 512 * k + o + 256)
-                    sc = ("SC", 512 * k + o, 512 * k + o + 256)
-                    tt(g, IND(X("F", 0, 2048), ls), X("DM", 0, 256), OP.mult)
-                    scan(X(*sc), X("RMH", 0, 256), g, OP.mult, OP.add)
-                    tc(X("LS", 32 * k + 32 + 16 * s, 32 * k + 48 + 16 * s), X(sc[0], sc[1] + 15, sc[2], 16))
-                gm = X("GM", 512 * k + o, 512 * k + o + 256)
-                gat(gm, IND(mwin, ls), "A" if last else GQ[2 * k + s])
-                if k == 4:
-                    g5 = X("G5", o, o + 256)
-                    gat(g5, IND(X("F", 0, 2048), ls), G5Q[2 * rnd + s])
-                mm(X("b0", 0, 256), m128("TB" if s else "TA"), gm, k == 0 and s == 0, k == 4 and s == 1 and False)
-                if k == 0:
-                    mm(X("b0", 0, 256), m128("MS"), gm, False, False)
-                mm(X("b1", o, o + 256), m128("DMX"), gm, False, False)
-                if k == 4:
-                    mm(X("b0", 0, 256), m128("RTN" if s else "RT"), g5, False, s == 1)
-                    mm(X("b1", o, o + 256), m128("RD"), g5, False, s == 1)
-        ts(X("VA", 0, 256), X("b0", 0, 256), col(18), OP.is_equal, col(19), OP.max)
+                lin(sm, X("PM", 16 * s, 16 * s + 16), X("PU", 16 * s, 16 * s + 16), 1.0, MARK[s])
+                o = 2560 + 256 * s
+                gat(X("G", o, o + 256), IND(dwin, X("LU", 16 * s, 16 * s + 16)), CFG["CQ"][s])
+                hold(X("SC", o, o + 256), X("G", o, o + 256))
+            tt(X("DS", 16, 32), X("SC", 2575, 2816, 16), X("SC", 2831, 3072, 16), OP.subtract)
         for s in range(2):
-            tt(X("PR", 256 * s, 256 * s + 256), X("b1", 256 * s, 256 * s + 256), X("VA", 0, 256), OP.mult)
+            lin("V", X("DS", 32 + 16 * s, 48 + 16 * s), X("DS", 16, 32), 4096.0 if s else -4096.0, 0.0, True)
+        v = X("DS", 64, 96)
+        tt(v, X("DS", 32, 64), X("PM", 0, 32), OP.add)
+        ts(X("LS", 0, 32), v, 2048, OP.min)
+        for s in range(2):
+            lin(sm, X("C", 80 * s, 80 * s + 80, 5), X("DS", 64 + 16 * s, 80 + 16 * s), 1.0, col(8))
+        for k in range(5):
+            ts(X("HF", 512 * k + 15, 512 * k + 512, 16), v, col(17 + k), OP.add, col(16), OP.max)
+            for s in range(2):
+                o = 512 * k + 256 * s
+                gat(X("G", o, o + 256), IND(fwin, X("LS", 32 * k + 16 * s, 32 * k + 16 * s + 16)), CFG["CQ"][12 * rnd + 2 + 2 * k + s])
+                scan(X("SC", o, o + 256), X("G", o, o + 256), X("HF", o, o + 256), OP.min, OP.add, 4096.0)
+                ck = X("SC", o + 15, o + 256, 16)
+                if k < 4:
+                    ts(X("LS", 32 * k + 32 + 16 * s, 32 * k + 48 + 16 * s), ck, col(7), OP.add, 2048, OP.min)
+                    lin(CFG["CP"][5 * rnd + k], X("C", 80 * s + k + 1, 80 * s + 80, 5), ck, 1.0, 0.0)
+        eq, ne = X("E6", 16, 96), X("N6", 16, 96)
+        tt(eq, X("C", 0, 80), X("C", 80, 160), OP.is_equal)
+        tt(ne, X("C", 0, 80), X("C", 80, 160), OP.not_equal)
+        for s in range(2):
+            tt(X("PC", 80 * s, 80 * s + 80), ne, X("C", 80 * s, 80 * s + 80), OP.mult)
+            scan(X("SS", 80 * s, 80 * s + 80), eq, X("PC", 80 * s, 80 * s + 80), OP.mult, OP.add)
+        top = X("SC", 2063, 2560, 16)
+        for s in range(2):
+            tt(X("CE", 16 * s, 16 * s + 16), X("SC", 2063, 2304, 16), X("SC", 2319, 2560, 16), OP.is_equal)
+        tt(X("CE", 32, 64), X("SS", 4, 160, 5), top, OP.subtract)
+        tt(X("CE", 64, 96), X("CE", 32, 64), X("CE", 0, 32), OP.mult)
+        tt(X("CE", 96, 128), X("CE", 64, 96), top, OP.add)
+        ts(X("LA", 0, 32), X("CE", 96, 128), col(7), OP.add)
+        cur[0] = "co"
+        tt(X("PC", 160, 240), X("N6", 15, 95), X("C", 0, 80), OP.mult)
+        scan(X("SS", 160, 240), X("E6", 15, 95), X("PC", 160, 240), OP.mult, OP.add)
+        tt(X("CE", 128, 144), X("SS", 164, 240, 5), X("SC", 2063, 2304, 16), OP.subtract)
+        tt(X("CE", 144, 160), X("CE", 128, 144), X("E6", 20, 96, 5), OP.mult)
+        tt(X("CE", 160, 176), X("CE", 144, 160), X("SC", 2063, 2304, 16), OP.add)
+        ts(X("FL", 0, 16), X("CE", 160, 176), col(7), OP.add)
+        tc(X("AW", 0, 32), X("LA", 0, 32))
+        tc(X("AWH", 0, 32), X("LA", 0, 32))
+        together(True)
         for r in range(16):
-            mm(X("b2", 0, 32), X("WBH", 15 - r, 143 - r), X("PR", r, 512, 16), r == 0, r == 15)
-        tc(X("LA", 0, 32), X("b2", 0, 32))
-        tc(X("AW", 0, 32), X("b2", 0, 32))
-        for r in range(16):
-            mm(X("b2", 32, 48), X("WBH", 15 - r, 143 - r), X("VA", r, 256, 16), r == 0, r == 15)
-        ts(X("W", 64, 80), X("b2", 32, 48), 2, OP.is_ge)
-        mm(X("b3", 0, 512), m128("BLK"), X("PR", 0, 512), True, True)
+            mm(X("b3", r, 512, 16), X("BSEL", 128 * r, 128 * r + 128), X("AWH", 0, 32), True, True)
+        together(False)
         act(X("VALF", 256, 512), X("b3", 0, 256))
         act(X("VALF", 0, 256), X("b3", 256, 512))
 
+        cur[0] = ""
+
         def la(s):
             return X("LA", 16 * s, 16 * s + 16)
-        for s in range(2):
-            gat(X("XS", 256 * s, 256 * s + 256), IND(xwin, la(s)))
-            mm(X("b4", 256 - 256 * s, 512 - 256 * s), m128("IDB"), X("XS", 256 * s, 256 * s + 256), True, True)
+
+        def kids(out, lst, s, qs):
+            n, mine = len(qs), cur[0]
+            for q in range(n):
+                lo, k = 4096 * s + 4096 // n * q, 256 * s + 256 // n * q
+                cur[0] = mine
+                gat(X(out, lo, lo + 4096 // n), IND(xwin, X(lst, k, k + 256 // n)), qs[q])
+                cur[0] = "S" + mine
+                scan(X("S" + out, lo, lo + 4096 // n), X("RMB", 0, 4096 // n), X(out, lo, lo + 4096 // n), OP.min, OP.max)
         for s in range(2):
             tc(X("KL", 256 * s, 256 * s + 256), IND(kwin, la(s)))
         for s in range(2):
-            for q in range(4):
-                gat(X("Y", 4096 * s + 1024 * q, 4096 * s + 1024 * q + 1024), IND(xwin, X("KL", 256 * s + 64 * q, 256 * s + 64 * q + 64)), "V" if (s, q) in VY else "A")
+            gat(X("XS", 256 * s, 256 * s + 256), IND(xwin, la(s)))
+            if (1 - s, 0) not in relu or (1 - s, 1) not in relu:
+                mm(X("bx%d" % (1 - s), 0, 256), m128("IDB"), X("XS", 256 * s, 256 * s + 256), True, True)
+        for s in range(2):
+            cur[0] = "yb" if s else "ya"
+            kids("Y", "KL", s, CFG["Y%d%d" % (rnd, s)])
         for s in range(2):
             tc(X("KF", 256 * s, 256 * s + 256), X("KL", 256 * s, 256 * s + 256))
         for s in range(2):
@@ -319,176 +380,190 @@ def build():
             mm(X(kb, 0, 256), m128("E0"), X("KC", 0, 256), True, False)
             for h in range(2):
                 base = 4096 * s + 2048 * h
+                soft = (s, h) in relu
                 for i in range(4):
+                    together(soft)
                     for j in range(4 * i, 4 * i + 4):
                         y, m = X("Y", base + j, base + 2048, 16), X("MM", base + 128 * j, base + 128 * j + 128)
-                        if (s, h) in RELU:
-                            b = "b%d" % (i % 2)
+                        if soft:
                             c = 128 * (j - 4 * i)
-                            mm(X(b, c, c + 128), m128("IDB"), y, True, False)
-                            mm(X(b, c, c + 128), m128("IDN"), X("XS", 256 - 256 * s + 128 * h, 384 - 256 * s + 128 * h), False, True)
+                            mm(X("b1", c, c + 128), m128("IDB"), y, True, False)
+                            mm(X("b1", c, c + 128), m128("IDN"), X("XS", 256 - 256 * s + 128 * h, 384 - 256 * s + 128 * h), False, True)
                         else:
-                            tt(m, y, X("b4", 256 * s + 128 * h, 256 * s + 128 * h + 128), OP.max)
-                    if (s, h) in RELU:
-                        relu(X("MM", base + 512 * i, base + 512 * i + 512), X("b%d" % (i % 2), 0, 512))
+                            tt(m, y, X("bx%d" % s, 128 * h, 128 * h + 128), OP.max)
+                    together(False)
+                    if soft:
+                        act(X("MM", base + 512 * i, base + 512 * i + 512), X("b1", 0, 512), func="Relu")
+                    together(True)
                     for j in range(4 * i, 4 * i + 4):
                         mm(X(kb, 128 * h + j, 128 * h + 128, 16), X("MM", base + 128 * j, base + 128 * j + 128), X("SEL", 0, 8), False, h == 1 and j == 15)
+                    together(False)
         for s in range(2):
             o = 256 * s
             kb = "b%d" % (5 + s)
             cur[0] = "lb" if s else "la"
-            (act if KSA[s] == "A" else tc)(X("KS", o, o + 256), X(kb, 0, 256))
-            scan(X("PS", o, o + 256), X("RMH", 0, 256), X("KS", o, o + 256), OP.mult, OP.max)
-            tt(X("OHT", o, o + 256), IND(X("PS", o, o + 256), X("L15", 0, 16)), X("KS", o, o + 256), OP.is_equal)
+            scan(X("PS", o, o + 256), X("RMH", 0, 256), X(kb, 0, 256), OP.mult, OP.max)
+            e = 16 + 272 * s
+            tc(X("HK", 16 * s, 16 * s + 16), X("PS", o + 15, o + 256, 16))
+            tt(X("OHT", e, e + 256), IND(X("HK", 16 * s, 16 * s + 16), X("L15", 0, 16)), X("PS", o, o + 256), OP.is_equal)
+            mm(X("b7", 0, 256), m128("EJ"), X("E0", 0, 256), True, False)
+            together(True)
             for h in range(2):
-                mm(X("b7", o + 128 * h, o + 128 * h + 128), X("OHT", o + 128 * h, o + 128 * h + 128), m128("IDB"), True, True)
-            tt(X("PL", o, o + 256), X("b7", o, o + 256), X("KF", o, o + 256), OP.mult)
-            for r in range(16):
-                mm(X("b3", 16 * s, 16 * s + 16), X("WBH", 15 - r, 143 - r), X("PL", o + r, o + 256, 16), r == 0, r == 15)
-            tc(X("LL", 16 * s, 16 * s + 16), X("b3", 16 * s, 16 * s + 16))
-            tc(X("LW", 16 * s, 16 * s + 16), X("b3", 16 * s, 16 * s + 16))
+                mm(X("b7", 128 * h, 128 * h + 128), X("OHT", e + 128 * h, e + 128 * h + 128), m128("IDB"), False, False)
+                mm(X("b7", 128 * h, 128 * h + 128), X("OHT", e + 128 * h - 1, e + 128 * h + 127), m128("IDN"), False, h == 1)
+            together(False)
+            tt(X("PL", o, o + 256), X("b7", 0, 256), X("KF", o, o + 256), OP.mult)
+            wrap(X("b3", 0, 16), "WBH", X("PL", o, o + 256))
+            tc(X("LL", 16 * s, 16 * s + 16), X("b3", 0, 16))
             tc(X("ZK", o, o + 256), IND(kwin, X("LL", 16 * s, 16 * s + 16)))
             cur[0] = "zb" if s else "za"
-            for q in range(4):
-                gat(X("Z", 4096 * s + 1024 * q, 4096 * s + 1024 * q + 1024), IND(xwin, X("ZK", o + 64 * q, o + 64 * q + 64)), "AV" if (s, q) in VG else "A")
+            kids("Z", "ZK", s, CFG["Z%d%d" % (rnd, s)])
+            cur[0] = ""
+            tc(X("LW", 16 * s, 16 * s + 16), X("LL", 16 * s, 16 * s + 16))
             if not last:
-                act(X("OHS", o, o + 256), X("b7", o, o + 256))
-        for n1, n2 in (("Y", "SY"), ("Z", "SZ")):
-            cur[0] = n2
-            for s in range(2):
-                for q in range(4):
-                    lo = 4096 * s + 1024 * q
-                    scan(X(n2, lo, lo + 1024), X("RMB", 0, 1024), X(n1, lo, lo + 1024), OP.min, OP.max)
+                act(X("OHS", o, o + 256), X("b7", 0, 256), scale=-1.0 if s else 1.0)
         cur[0] = "co"
         tc(X("FG", 0, 256), IND(fwin, la(0)))
-        for r in range(16):
-            mm(X("b2", 0, 16), X("WB16", 15 - r, 143 - r), X("FG", r, 256, 16), r == 0, r == 15)
-        tc(X("FW", 0, 16), X("b2", 0, 16))
-        tc(X("FWH", 0, 16), X("FW", 0, 16))
+        tc(X("FWH", 0, 16), X("FL", 0, 16))
+        tc(X("FW", 0, 16), X("FL", 0, 16))
+        together(True)
         mm(X("b2", 0, 256), m128("IDB"), X("TBIG", 0, 256), True, False)
         for r in range(16):
             mm(X("b2", r, 256, 16), m128("IDH"), X("FWH", 0, 16), False, r == 15)
+        together(False)
         tt(X("EQD", 0, 256), X("FG", 0, 256), X("b2", 0, 256), OP.is_equal)
         scan(X("SQD", 0, 256), X("RMH", 0, 256), X("EQD", 0, 256), OP.mult, OP.max)
         for c in range(1, 16):
             o = 8 * c * (c - 1)
             ts(X("EQ", o, o + 16 * c), X("FG", 0, 16 * c), X("FW", c, c + 1), OP.is_equal)
             add("A", "count", X("EQS", o, o + 16 * c), [X("EQ", o, o + 16 * c)], (X("CNT", c, c + 1),), max(64, 16 * c) * CY + 0.02)
-
-        def w(i, n=1):
-            return X("W", 16 * i, 16 * (i + n))
+        aw, bw, lw = X("AW", 0, 16), X("AW", 16, 32), X("LW", 0, 16)
         tt(w(1), X("CNT", 0, 16), X("SQD", 15, 256, 16), OP.add)
         ts(w(2), w(1), 0, OP.is_equal)
-        tt(w(3), X("AW", 0, 16), X("AW", 16, 32), OP.not_equal)
-        tt(w(5), w(3), w(4), OP.mult)
+        tt(w(3), aw, bw, OP.not_equal)
+        tt(w(5), w(3), X("CE", 0, 16), OP.mult)
         tt(w(6), w(2), w(5), OP.mult)
         tt(w(7), w(2), w(6), OP.subtract)
         ts(w(12, 2), X("LW", 0, 32), 2047, OP.not_equal)
         tt(w(14), w(12), w(13), OP.mult)
-        tt(w(15), w(14), w(6), OP.mult)
-        tt(w(10), X("AW", 16, 32), X("AW", 0, 16), OP.subtract)
-        tt(w(11), X("LW", 16, 32), X("LW", 0, 16), OP.subtract)
-        ts(w(26), w(5), -90, OP.mult, 99, OP.add)
-        ts(w(27), w(5), -90, OP.mult, 99, OP.add)
-        tt(w(16, 2), X("LW", 0, 32), X("DUF", 0, 32), OP.subtract)
         for i in range(2):
-            tt(w(16 + i), w(16 + i), w(15), OP.mult)
+            tt(w(8 + i), w(14), w(6), OP.mult)
+            lin(sm, w(26 + i), w(5), -90.0, 99.0)
+        tt(w(44, 2), X("LW", 0, 32), X("DUF", 0, 32), OP.subtract)
+        tt(w(16, 2), w(44, 2), w(8, 2), OP.mult)
         if not last:
-            tt(w(18, 2), X("AW", 0, 32), X("DUF", 0, 32), OP.subtract)
-            for i in range(2):
-                tt(w(18 + i), w(18 + i), w(15), OP.mult)
+            tt(w(46, 2), X("AW", 0, 32), X("DUF", 0, 32), OP.subtract)
+            tt(w(18, 2), w(46, 2), w(8, 2), OP.mult)
+        for i in range(2):
+            tt(w(48 + 2 * i, 2), X("AW", 0, 32), X("MD", 32 * i, 32 * i + 32), OP.subtract)
+        tt(w(54, 2), X("AW", 0, 32), X("MD", 64, 96), OP.subtract)
+        for i in range(2):
+            tt(w(56 + i), w(54 + i), w(6), OP.mult)
+        tt(w(58), w(54), w(7), OP.mult)
+        tt(X("CH", 240, 288, 3), w(58), dux, OP.add)
+        cur[0] = "su"
+        for i, src in enumerate(("SY", "SZ")):
+            wrap(X("b0", 0, 16), "WBW", X(src, 15, 4096), i == 0, i == 1, 16)
+        if not last:
+            mm(X("bs", 0, 12), m128("IDH"), X("L977", 4, 16), True, False)
+            for i in range(4):
+                wrap(X("bs", 0, 12), "WBW", X("SZ" if i > 1 else "SY", 4096 * (i % 2) + 1039, 4096 * (i % 2) + 4096), False, i == 3, 16)
+        act(X("XW", X0 + MO, X0 + MO + 256), X("SY", 15, 4096, 16))
+        act(X("XW", X0 + MO + 256, X0 + MO + 512), X("SZ", 15, 4096, 16))
         cur[0] = ""
-        for i, src in enumerate(("SY", "SZ")):
-            for r in range(16):
-                mm(X("b5", 0, 32), X("WBW", 15 - r, 143 - r), X(src, 15 + 16 * r, 8192, 256), i == 0 and r == 0, i == 1 and r == 15)
-        act(X("XW", X0 + YMO, X0 + YMO + 256), X("SY", 15, 4096, 16))
-        act(X("XW", X0 + ZMO, X0 + ZMO + 256), X("SZ", 15, 4096, 16))
-        for i, src in enumerate(("SY", "SZ")):
-            for s in range(2):
-                mm(X("b6", 0, 256), m128("IDN" if s else "IDB"), X(src, 4096 * s + 15, 4096 * s + 4096, 16), i + s == 0, i + s == 2)
-        ts(X("GL", 0, 256), X("b6", 0, 256), 0, OP.is_gt)
-        ts(X("GL", 256, 512), X("b6", 0, 256), 0, OP.is_lt)
-        for r in range(16):
-            mm(X("b2", 0, 32), X("WBB", 15 - r, 143 - r), X("GL", r, 512, 16), r == 0, r == 15)
-        tc(X("SI", 0, 32), X("b5", 0, 32))
-        bs = "BS2" if last else "BS1"
-        ts(X("SI", 32, 48), X("SI", 0, 16), 127, OP.bitwise_and)
-        tt(X(bs, 32, 48), X("SI", 32, 48), X("RBK", 16 * rnd, 16 * rnd + 16), OP.add)
         for i in range(3):
-            tt(w(41 + i), X("LW" if i == 2 else "AW", 0, 16), X(bs, 16 * i, 16 * i + 16), OP.subtract)
-            tt(w(44 + i), X("LW" if i == 2 else "AW", 16, 32), X(bs, 16 * i, 16 * i + 16), OP.subtract)
+            mm(X("b4", 0, 256), m128("IDN" if i == 1 else "IDB"), X("SZ" if i == 2 else "SY", 4096 * (i % 2) + 15, 4096 * (i % 2) + 4096, 16), i == 0, i == 2)
+        tt(X("GL", 0, 256), X("b4", 0, 256), X("SZ", 4111, 8192, 16), OP.is_gt)
+        tt(X("GL", 256, 512), X("b4", 0, 256), X("SZ", 4111, 8192, 16), OP.is_lt)
+        wrap(X("b2", 0, 32), "WBB", X("GL", 0, 512))
+        cur[0] = "su"
+        tc(X("SI", 0, 16), X("b0", 0, 16))
+        ts(X("SI", 32, 48), X("SI", 0, 16), 127, OP.bitwise_and)
+        root = X("CH", 192, 240, 3)
+        tt(root, X("SI", 32, 48), X("RBK", 16 * rnd, 16 * rnd + 16), OP.add)
+        for s in range(2):
+            tt(w(52 + s), X("LW", 16 * s, 16 * s + 16), root, OP.subtract)
+        cur[0] = "vd"
         tt(w(20, 2), X("b2", 0, 32), w(26, 2), OP.is_ge)
-        for i in range(6):
-            tt(w(48 + i), w(20 + i // 3), w(41 + i), OP.mult)
-        tt(w(54, 3), w(48, 3), w(51, 3), OP.add)
-        tt(w(57, 3), w(54, 3), X(bs, 0, 48), OP.add)
-        ts(X("LT", 0, 48), w(57, 3), 0 if last else X0, OP.add)
-        tt(w(25), w(20), w(21), OP.add)
-        tt(w(34), w(25), w(16), OP.mult)
-        tt(w(35), w(25), w(17), OP.mult)
-        tt(w(36, 2), w(34, 2), X("DUF", 0, 32), OP.add)
-        tc(X("LF", 0, 32), w(36, 2))
-        add("V", "tc", IND(X("F", 0, 2576), X("LF", 0, 32)), [X("VALF", 0, 512)], (), 0.05 + 512 * 0.0031)
-        tt(w(28), w(21), w(10), OP.mult)
-        tt(w(32), w(28), X("AW", 0, 16), OP.add)
-        if not last:
-            tt(w(29), w(21), w(11), OP.mult)
-            tt(w(33), w(29), X("LW", 0, 16), OP.add)
+        choose(X("LF", 0, 32), 0, [(w(16), w(16)), (w(17), w(17))], 0, OP.add)
+        cur[0] = "fs"
+        put(X("F", 0, 2576), X("LF", 0, 32), X("VALF", 0, 512), CFG["PUT"][rnd])
+        cur[0] = "xw"
+        choose(X("LT", 0, 48), 2, [(w(48 + 2 * i), w(49 + 2 * i)) for i in range(3)], 0 if last else X0, OP.add)
+        choose(X("LX", 0, 16), 5, [(w(56), w(57))], 0, OP.add)
         twin = X("XW", X0, X0 + XEND) if last else X("XW", 0, X0 + R2O)
         for i in range(3):
-            gat(X("TG", 256 * i, 256 * i + 256), IND(twin, X("LT", 16 * i, 16 * i + 16)), "AV")
+            gat(X("TG", 256 * i, 256 * i + 256), IND(twin, X("LT", 16 * i, 16 * i + 16)), CFG["TQ"][3 * rnd + i])
         for i in range(3):
             mm(X("b3", 0, 256), m128("ID2" if i == 2 else "IDB"), X("TG", 256 * i, 256 * i + 256), i == 0, i == 2)
-        tt(w(38), w(2), w(25), OP.mult)
-        tt(w(39), w(38), w(7), OP.add)
-        tt(w(60), w(32), X("DUX", 0, 16), OP.subtract)
-        tt(w(61), w(60), w(39), OP.mult)
-        tt(w(62), w(61), X("DUX", 0, 16), OP.add)
-        tc(X("LX", 0, 16), w(62))
         ts(X("VI", 0, 256), X("b3", 0, 256), 0.25, OP.mult, -0.375, OP.add)
         add("W", "waitsent", X("XW", X0, X0 + 128), [], (rnd + 1,), 0)
-        add("V", "tc", IND(X("XW", X0, X0 + YMO), X("LX", 0, 16)), [X("VI", 0, 256)], (), 0.05 + 256 * 0.0031)
+        put(X("XW", X0, X0 + MO), X("LX", 0, 16), X("VI", 0, 256), CFG["PUT"][2 + rnd])
         if last:
-            dma("S", ("d", "yf"), X("F", 0, 2048, 1, 0, 128), "d7")
+            dma("S", ("d", "yf"), X("F", 0, 2048), "d7")
             for i in range(2):
                 dma("SA"[i], ("d", "yx%d" % i), X("XW", X0 + 1024 * i, X0 + 1024 * i + 1024), "d%d" % (8 + i))
             break
         add("G", "send", None, [X("XW", X0, X0 + 128)], (2,), 1.0)
         add("N", "arrive", X("XW", X0 + R2O, X0 + XEND), [], (2,), 0)
-        ts(w(63), w(33), 2047, OP.is_equal)
-        tt(w(64), w(32), w(33), OP.subtract)
-        tt(w(65), w(63), w(64), OP.mult)
-        tt(w(66), w(65), w(33), OP.add)
-        tc(X("LS", 0, 16), w(66))
+        cur[0] = "np"
+
+        def kn(i):
+            return X("KN", 4 * i, 4 * i + 4)
+        tt(w(28, 2), X("LW", 0, 32), X("AW", 0, 32), OP.subtract)
+        tt(w(30, 2), w(28, 2), w(12, 2), OP.mult)
+        tt(w(32, 2), w(30, 2), X("AW", 0, 32), OP.add)
+        tt(w(34), w(33), w(32), OP.subtract)
+        lin(sm, w(35), w(32), 1.0, MARK[0])
         for s in range(2):
-            tt(X("KDD", 64 * s, 64 * s + 64), X("KF", 256 * s, 256 * s + 64), X("DM", 0, 64), OP.mult)
-        scan(X("KDS", 0, 128), X("RMH", 0, 128), X("KDD", 0, 128), OP.mult, OP.add)
-        tc(X("KN", 0, 8), X("KDS", 15, 128, 16))
-        tt(X("W", 1072, 1076), X("KN", 4, 8), X("KN", 0, 4), OP.subtract)
-        tt(X("W", 1076, 1080), X("W", 1072, 1076), X("W", 336, 340), OP.mult)
-        tt(X("LSI", 0, 4), X("W", 1076, 1080), X("KN", 0, 4), OP.add)
-        tt(X("SI", 48, 64), X("SI", 0, 16), X("SI", 16, 32), OP.add)
-        tt(X("LSI", 16, 32), X("SI", 48, 64), X("L977", 0, 16), OP.add)
-        ts(X("LSI", 4, 16), X("LSI", 20, 32), 2047, OP.bitwise_and)
-        tc(X("LS", 16, 32), X("LSI", 0, 16))
+            hold(X("KDS", 64 * s, 64 * s + 64), X("KF", 256 * s, 256 * s + 64))
+        ts(X("KN", 0, 8), X("KDS", 15, 128, 16), col(7), OP.add)
+        tt(kn(2), kn(1), kn(0), OP.subtract)
+        ts(kn(3), kn(0), MARK[1], OP.add)
+        gat(X("G", 2560, 2816), IND(dwin, la(0)))
+        hold(X("SC", 2560, 2816), X("G", 2560, 2816))
+        tt(w(36), X("SC", 2575, 2816, 16), w(12), OP.add)
+        ts(kn(4), X("SC", 2575, 2624, 16), col(7), OP.add, 1, OP.add)
+        ts(X("KN", 20, 28), X("KN", 0, 8), 2047, OP.not_equal)
+        for s in range(2):
+            tt(kn(7 + s), kn(5 + s), kn(4), OP.mult)
+        ts(kn(9), X("W", 576, 580), col(7), OP.add)
+        tt(X("W", 592, 596), kn(9), kn(7), OP.subtract)
+        tt(w(38), w(13), w(12), OP.subtract)
+        tt(kn(10), kn(8), kn(7), OP.subtract)
+        tt(X("W", 608, 612), X("W", 608, 612), kn(10), OP.subtract)
+        cur[0] = "nb"
+        tc(X("LSI", 16, 28), X("bs", 0, 12))
+        ts(X("LSI", 0, 12), X("LSI", 16, 28), 2047, OP.bitwise_and)
+        tc(X("LU", 0, 12), X("LSI", 0, 12))
+        ts(X("PM", 20, 32), X("LSI", 0, 12), MARK[1], OP.add)
+        gat(X("G", 2816, 3008), IND(dwin, X("LU", 0, 12)), CFG["CQ"][12])
+        scan(X("SC", 2816, 3008), X("G", 2816, 3008), X("HM", 0, 192), OP.min, OP.add, 4096.0)
+        tt(X("W", 596, 608), X("W", 580, 592), X("SC", 2831, 3008, 16), OP.subtract)
+        cur[0] = "vd"
+        tt(w(39), w(21), w(38), OP.mult)
+        tt(X("DS", 16, 32), w(39), w(37), OP.add)
+        tt(w(40), w(21), w(34), OP.mult)
+        tt(X("PM", 0, 16), w(40), w(35), OP.add)
+        tt(kn(11), X("W", 336, 340), kn(2), OP.mult)
+        tt(X("PM", 16, 20), kn(11), kn(3), OP.add)
+        cur[0] = "kd"
+        together(True)
         mm(X("b1", 0, 256), m128("BLK"), X("PL", 256, 512), True, False)
         mm(X("b1", 0, 256), m128("NBLK"), X("PL", 0, 256), False, True)
-        tt(X("TK", 0, 256), X("b1", 0, 256), X("OHS", 0, 256), OP.mult)
-        ts(X("OHS", 256, 512), X("OHS", 256, 512), -1, OP.mult)
-        tt(X("TK", 256, 512), X("b1", 0, 256), X("OHS", 256, 512), OP.mult)
-        mm(X("b4", 0, 512), m128("IDH"), X("TK", 0, 512), True, False)
-        mm(X("b4", 0, 512), m128("IDH"), X("KF", 0, 512), False, True)
+        together(False)
+        for s in range(2):
+            tt(X("TK", 256 * s, 256 * s + 256), X("b1", 0, 256), X("OHS", 256 * s, 256 * s + 256), OP.mult)
+        mm(X("b4", 0, 512), m128("IDH"), X("KF", 0, 512), True, False)
+        mm(X("b4", 0, 512), m128("IDH"), X("TK", 0, 512), False, True)
         act(X("NK", 0, 512), X("b4", 0, 512))
-        for i in range(2):
-            tt(w(68 + i), w(25), w(18 + i), OP.mult)
-        tt(w(70, 2), w(68, 2), X("DUF", 0, 32), OP.add)
-        tc(X("LF", 32, 64), w(70, 2))
-        add("V", "tc", IND(X("KD", 0, 2576), X("LF", 32, 64)), [X("NK", 0, 512)], (), 0.05 + 512 * 0.0031)
+        choose(X("LF", 32, 64), 0, [(w(18), w(18)), (w(19), w(19))], 0, OP.add)
+        put(X("KD", 0, 2576), X("LF", 32, 64), X("NK", 0, 512), CFG["PUT"][4])
     return P
 
 
 def deps(P):
-    hist, n = {}, len(P)
+    hist = {}
     preds = [dict() for _ in P]
     for i, p in enumerate(P):
         for acc, wr in [(a, False) for a in p["r"]] + [(a, True) for a in p["w"]]:
@@ -502,7 +577,7 @@ def deps(P):
                     both = p["q"] == "T" and P[j]["q"] == "T"
                     if p["q"] != P[j]["q"] or ((wr or bw) and clash(acc, b) and not both):
                         preds[i][j] = True
-                    else:
+                    elif both:
                         preds[i].setdefault(j, False)
                 elif (wr or bw) and clash(acc, b):
                     preds[i][j] = True
@@ -512,40 +587,114 @@ def deps(P):
 
 def order(P, preds):
     n = len(P)
-    succ = [[] for _ in P]
-    for i in range(n):
-        for j in preds[i]:
-            succ[j].append(i)
+    units, uses = {}, {}
+    for i, p in enumerate(P):
+        units.setdefault(p["g"], []).append(i)
+        for v in p["use"]:
+            uses.setdefault(v, []).append(i)
+    late = [2.0 + p["args"][1] if p["what"] == "dma" else 12.0 if p["what"] == "arrive" else 0.0 for p in P]
+
+    length = {u: sum(P[i]["cost"] for i in m) for u, m in units.items()}
+
+    def wake(i, j, hard):
+        return (WS if P[i]["q"] == P[j]["q"] else WK) if hard else 0.0
+
+    def turn(pre):
+        suc = [dict() for _ in P]
+        for i in range(n):
+            for j, h in pre[i].items():
+                suc[j][i] = h
+        return suc
+
+    def sweep(pre, prio, fixed):
+        back = fixed is not None
+        pre = [dict(d) for d in pre]
+        member = {u: m[::-1] if back else m for u, m in units.items()}
+        ext = {u: {j for i in m for j in pre[i] if P[j]["g"] != u} for u, m in member.items()}
+        left = {u: len(e) for u, e in ext.items()}
+        waits = {}
+        for u, e in ext.items():
+            for j in e:
+                waits.setdefault(j, []).append(u)
+        t = [None] * n
+
+        def when(u):
+            at, off = 0.0, 0.0
+            for i in member[u]:
+                at = max([at] + [t[j][1] + wake(i, j, h) + (late[i] if back else 0.0) - off for j, h in pre[i].items() if P[j]["g"] != u])
+                off += P[i]["cost"]
+            return at
+        ready = {u: when(u) + (late[member[u][0]] if back else 0.0) for u in units if not left[u]}
+        free = {q: 0.0 for q in "AVTGSNWD"}
+        seq, queue = [], [None] * n
+        bank, holder, unopened, open_ = {}, [None] * 8, sorted(uses), {v: len(m) for v, m in uses.items()}
+        while ready:
+            idle = [] if back else sorted((max([t[j][1] for j in uses[v]]) + WK if v is not None else 0.0, b) for b, v in enumerate(holder) if v is None or not open_[v])
+            cand = []
+            for u, at in ready.items():
+                i = member[u][0]
+                new = [] if back else [v for v in P[i]["use"] if v not in bank]
+                if new:
+                    if len(idle) < (1 if new[0] == unopened[0] else 1 + CFG["KEEP"]):
+                        continue
+                    at = max(at, idle[0][0])
+                q = P[i]["q"]
+                cand.append((max(free[q], at), -prio[i], u, q))
+            first = min(cand)
+            mine = [c for c in cand if c[3] == first[3]]
+            soon = min((c for c in mine if c[0] <= first[0] + CFG["SLACK"].get(first[3], 0.0) * length[first[2]]), key=lambda c: (c[1], c[0]))
+            if soon[1] < first[1] - CFG["MARGIN"]:
+                first = min([c for c in mine if c[0] + length[c[2]] <= soon[0] + 0.03] or [soon], key=lambda c: (c[1], c[0]))
+            st, _, u, q = first
+            del ready[u]
+            for i in member[u]:
+                for v in P[i]["use"]:
+                    open_[v] -= 1
+                    if not back and v not in bank:
+                        b = idle[0][1]
+                        if holder[b] is not None:
+                            for j in uses[holder[b]]:
+                                pre[i][j] = pre[i].get(j, False) or P[j]["q"] != "T"
+                        bank[v], holder[b] = b, v
+                        unopened.remove(v)
+                queue[i] = q
+                end = st + P[i]["cost"]
+                free[q] = end
+                if not back and P[i]["what"] == "dma" and P[i]["args"][1] > 0.5:
+                    free["D"] = max(end + 1.3, free["D"]) + P[i]["args"][1]
+                    end = free["D"] + 0.7
+                elif not back:
+                    end += late[i]
+                t[i] = (st, end)
+                st = free[q]
+                seq.append(i)
+            for i in member[u]:
+                for k in waits.get(i, []):
+                    left[k] -= 1
+                    if not left[k]:
+                        ready[k] = when(k)
+        assert len(seq) == n
+        return max(e for _, e in t), t, seq, queue, pre, bank
+    succ = turn(preds)
     prio = [0.0] * n
     for i in range(n - 1, -1, -1):
-        lat = 2.0 if P[i]["what"] == "dma" else 0.0
-        prio[i] = P[i]["cost"] + lat + max([prio[k] + WK for k in succ[i]] + [0.0])
-    left = [len(p) for p in preds]
-    ready = {i: 0.0 for i in range(n) if not left[i]}
-    free = {q: 0.0 for q in "AVTGSNW"}
-    seq, queue = [], [None] * n
-    while ready:
-        cand = []
-        for i, t in ready.items():
-            qs = P[i]["q"]
-            q = min(qs, key=lambda z: max(free[z], t)) if len(qs) > 1 else qs
-            cand.append((max(free[q], t), -prio[i] - BOOST.get(P[i]["b"], 0.0), i, q))
-        first = min(cand)
-        st, _, i, q = min((c for c in cand if c[3] == first[3] and c[0] <= first[0] + SLACK), key=lambda c: (c[1], c[0]))
-        queue[i] = q
-        end = st + P[i]["cost"]
-        free[q] = end
-        if P[i]["what"] == "dma":
-            end += 2.0
-        if P[i]["what"] == "arrive":
-            end += 12.0
-        P[i]["t"] = (st, end)
-        seq.append(i)
-        del ready[i]
-        for k in succ[i]:
-            left[k] -= 1
-            if not left[k]:
-                ready[k] = max([P[j]["t"][1] + (WK if preds[k][j] else 0.0) for j in preds[k]])
+        prio[i] = P[i]["cost"] + late[i] + max([prio[k] + wake(i, k, h) for k, h in succ[i].items()] + [0.0])
+    best = None
+    for _ in range(CFG["SWEEPS"]):
+        got = sweep(preds, [prio[i] + CFG["BOOST"].get(P[i]["b"], 0.0) for i in range(n)], None)
+        if best is None or got[0] < best[0]:
+            best = got
+        prio = [e for _, e in sweep(succ, [e for _, e in got[1]], got[3])[1]]
+    _, t, seq, queue, preds, bank = best
+    for i, p in enumerate(P):
+        p["t"] = t[i]
+
+    def named(a):
+        if isinstance(a, tuple) and a and a[0] == "x" and a[1][0] == "b":
+            return ("x", "b%d" % bank[int(a[1][1:])]) + a[2:]
+        return a
+    for p in P:
+        p["out"], p["ins"], p["args"] = named(p["out"]), [named(a) for a in p["ins"]], tuple(named(a) for a in p["args"])
     return seq, queue, preds
 
 
@@ -566,6 +715,7 @@ def rank_program(g, core, T, topo):
         return
     P, seq, queue, preds = plan()
     eng = {"V": g.vector, "A": g.scalar, "T": g.tensor, "G": g, "S": g.sync}
+    funcs = {None: AF.Identity, "Relu": AF.Relu, "Abs": AF.Abs, "Sign": AF.Sign}
     cores = list(T.cores)
     n = len(cores)
 
@@ -594,7 +744,6 @@ def rank_program(g, core, T, topo):
             seen[q][sem] = v
             eng[q].wait_ge(T.sem[sem], v)
 
-    extra = {}
     for i in seq:
         p, q = P[i], queue[i]
         what, args = p["what"], p["args"]
@@ -643,19 +792,19 @@ def rank_program(g, core, T, topo):
             h = e.activation(out, ins[0], AF.Copy)
         elif what == "count":
             h = e.activation(out, ins[0], AF.Copy, accum_out=ap(args[0]))
-        elif what == "sq":
-            h = e.activation(out, ins[0], AF.Square, bias=ins[1])
-        elif what == "relu":
-            h = e.activation(out, ins[0], AF.Relu)
         elif what == "act":
-            h = e.activation(out, ins[0], AF.Identity, bias=ins[1]) if args[0] else e.activation(out, ins[0], AF.Copy)
+            bias, scale, func = args
+            if bias is None and scale == 1.0 and func is None:
+                h = e.activation(out, ins[0], AF.Copy)
+            else:
+                h = e.activation(out, ins[0], funcs[func], bias=0.0 if bias is None else sc(bias), scale=sc(scale))
         elif what == "tt":
             h = e.tensor_tensor(out, ins[0], ins[1], args[0])
         elif what == "ts":
             s1, o1, s2, o2 = args
             h = e.tensor_scalar(out, ins[0], sc(s1), None, o1) if o2 is None else e.tensor_scalar(out, ins[0], sc(s1), sc(s2), o1, o2)
         elif what == "scan":
-            h = e.tensor_tensor_scan(out, ins[0], ins[1], 0.0, args[0], args[1])
+            h = e.tensor_tensor_scan(out, ins[0], ins[1], sc(args[2]), args[0], args[1])
         elif what == "mm":
             h = e.matmul(out, ins[0], ins[1], args[0], args[1])
         elif what == "tr":

@@ -8,14 +8,14 @@ MARK = (0.25, 0.375)
 
 SCRATCH = {}
 for _n, _w, _d in (
-        ("XW", X0 + XEND, "bfloat16"), ("KD", 2576, "int32"), ("F", 2576, "float32"), ("DP", 2048, "bfloat16"),
+        ("XW", X0 + XEND, "bfloat16"), ("KD", 2576, "int32"), ("F", 5152, "float32"), ("DP", 2048, "bfloat16"),
         ("FAI", 128, "int32"), ("DPI", 128, "int32"), ("PAI", 16, "int32"), ("PBI", 16, "int32"), ("WTI", 1, "int32"), ("FDH", 256, "float16"),
         ("PI", 1, "int32"), ("TI", 3, "int32"), ("COL", 32, "float32"), ("NF", 128, "float32"), ("NR", 272, "float32"), ("NG", 256, "float32"),
         ("BLK", 128, "float16"), ("NBLK", 128, "float16"), ("WBH", 144, "float16"), ("WBB", 144, "bfloat16"), ("WBW", 144, "bfloat16"),
         ("IDB", 128, "bfloat16"), ("IDN", 128, "bfloat16"), ("ID2", 128, "bfloat16"), ("IDH", 128, "float16"), ("BSEL", 2048, "float16"), ("DELR", 16, "float32"),
         ("RMH", 256, "float16"), ("SEL", 8, "bfloat16"), ("KC", 256, "bfloat16"), ("E0", 256, "bfloat16"), ("RMB", 1024, "bfloat16"),
-        ("L15", 16, "uint16"), ("LN", 16, "float32"), ("L977", 16, "float16"), ("QI", 64, "int32"), ("QT", 192, "float32"), ("R3", 192, "bfloat16"), ("CH", 288, "float32"), ("CS", 288, "float32"), ("MD", 96, "float32"), ("CE", 176, "float32"), ("QF", 32, "float32"), ("TBIG", 256, "bfloat16"), ("DUF", 48, "float32"),
-        ("RBK", 32, "float32"), ("CNT", 16, "float32"), ("EQ", 1920, "bfloat16"), ("EQS", 1920, "bfloat16"),
+        ("L15", 16, "uint16"), ("LN", 16, "float32"), ("L977", 16, "float16"), ("QI", 64, "int32"), ("QT", 192, "float32"), ("R3", 192, "bfloat16"), ("CH", 384, "float32"), ("CS", 384, "float32"), ("MD", 96, "float32"), ("CE", 176, "float32"), ("QF", 32, "float32"), ("TBIG", 256, "bfloat16"), ("DUF", 64, "float32"),
+        ("RBK", 32, "float32"), ("EQ", 1920, "float16"),
         ("PX", 64, "float32"), ("PT", 64, "float32"), ("PU", 32, "float32"),
         ("G", 3072, "float32"), ("SC", 3072, "float32"), ("LS", 160, "uint16"), ("LU", 32, "uint16"), ("LSI", 32, "int32"), ("HM", 800, "bfloat16"), ("DS", 96, "float32"), ("PM", 32, "float32"),
         ("HK", 160, "float32"), ("C", 192, "float32"), ("E6", 112, "float32"), ("N6", 112, "float32"), ("PC", 288, "float32"), ("SS", 288, "float32"),
@@ -23,7 +23,7 @@ for _n, _w, _d in (
         ("KL", 512, "uint16"), ("KF", 512, "float16"), ("XS", 512, "bfloat16"), ("Y", 8192, "bfloat16"), ("MM", 8192, "bfloat16"),
         ("EJ", 128, "bfloat16"), ("PS", 512, "float32"), ("OHT", 544, "bfloat16"), ("OHS", 512, "bfloat16"), ("PL", 512, "float16"), ("LL", 32, "uint16"), ("LW", 32, "float32"),
         ("ZK", 512, "uint16"), ("Z", 8192, "bfloat16"), ("SZ", 8192, "bfloat16"), ("SY", 8192, "bfloat16"), ("HF", 2560, "float32"), ("FG", 256, "float16"), ("FWH", 16, "float16"), ("FW", 16, "float32"), ("FL", 16, "uint16"),
-        ("EQD", 256, "bfloat16"), ("SQD", 256, "bfloat16"), ("GL", 512, "bfloat16"), ("W", 1152, "float32"), ("SI", 64, "int32"), ("KDS", 128, "float32"), ("KN", 48, "float32"),
+        ("EQD", 256, "float16"), ("GL", 512, "bfloat16"), ("W", 1152, "float32"), ("SI", 64, "int32"), ("KDS", 128, "float32"), ("KN", 48, "float32"),
         ("LT", 48, "uint16"), ("LX", 16, "uint16"), ("LF", 64, "uint16"), ("TG", 768, "bfloat16"), ("VI", 256, "int32"), ("TK", 512, "float16"), ("NK", 512, "float32")):
     SCRATCH[_n] = ("sbuf", [128, _w], _d)
 for _b in range(8):
@@ -31,13 +31,16 @@ for _b in range(8):
 SEMAPHORES = ["qV", "qA", "qT", "qG", "sent1", "sent2", "arr1", "arr2"] + ["d%d" % _i for _i in range(12)]
 
 CFG = dict(
-    Y00="VAAA", Y01="AAAA", Y10="VAAA", Y11="AAAA", Z00="AAAV", Z01="AAAAAAAV", Z10="AAAA", Z11="AAAAAAAV",
+    HALVES=[2, 2, 2, 2],
+    PLAN=dict(kl=(0, 0.1), ya=(0.6, 1.0), kf=(2.2, 0), ma=(2.4, 0.3), la=(2.0, 0.1), yb=(4.9, 1.4), mb=(7.9, 0.3), lb=(7.0, 0.1), za=(10.6, 1.4), zb=(16.3, 0.7),
+              Sya=(12, 0.5), Syb=(14, 0.5), Sza=(14.5, 0.5), Szb=(17, 0.7), eq=(13, 0.1), qd=(13.5, 0), vf=(14, 0), pre=(16, 0.05), np=(16.5, 0.05), su=(17, 0.1), sb=(17.5, 0), gl=(17.2, 0)),
+    Y00="AVAA", Y01="AAAA", Y10="AVAA", Y11="AAAA", Z00="AAAA", Z01="AAAAAAAV", Z10="AAAA", Z11="AAAAAAAV",
     RQ="VVVVVVVV",
-    CQ="AAVAVAVAAVAVAAAAAAAAAAAA", FQ="AVAVAVAA", TQ="AAAAAA", SM="VA", CP="AVVAVAAAVV",
-    PUT=[1, 2, 1, 1, 2],
-    SLACK={'T': 0, 'V': 0.6, 'A': 0.6}, MARGIN=0.0, KEEP=2, SWEEPS=3,
-    BOOST={'1': 6, 'vd0': 3, 'lb0': 3, 'zb0': 3, 'co0': -12, '': -12, 'cl0': 6, 'za1': 1, 'yb0': 6, 'nb0': -1, '0': 1, 'la0': -1, 'fs0': 12, 'ya1': 3, 'yb1': -1})
-CY, GA, SCA, WS, WK, BW = 0.00085, 0.00115, 0.003, 0.19, 0.19, 400e3
+    CQ="VAA", C0="AAAV" * 5, C1="A" * 20, PARTS=[2, 2], FQ="AVAVAVAV", TQ="AAAAVA", SM="VA",
+    PUT=[1, 2, 1, 1, 4],
+    SLACK={'T': 0.6, 'V': 0.6, 'A': 0.6}, MARGIN=0.0, KEEP=1, SWEEPS=3, REPAIR=[(0, 0, 30000), (1, 1, 50000), (2, 2, 30000), (3, 3, 50000), (4, 4, 20000)], LAP=30, MU=2, FAR=16, CHAIN=60, PULL=0.03, WORSE=0.08,
+    BOOST={'nb0': 1, 'ya1': -1, 'gl1': 1, 'qd0': 8, 'xw1': 8, 'Sza0': 1, 'sb0': -1, 'ya0': 1, 'lb1': 5, 'fs0': 16, 'za0': -1, 'za1': 1, 'kf0': -8, 'Szb1': -12, 'Sza1': -5, 'vf0': -1, 'pre1': -3, 'qd1': 1})
+CY, GA, SCA, WS, WK, BW = 0.00087, 0.00133, 0.003, 0.2, 0.2, 400e3
 
 
 def X(name, lo, hi, st=1, p0=0, p1=128):
@@ -131,15 +134,13 @@ def build():
         add("A", "act", out, [a] + [s for s in (bias, scale) if isinstance(s, tuple)], (bias, scale, func), c)
 
     def lin(q, out, a, scale, bias, cut=False):
-        if q == "A":
-            act(out, a, bias, scale, "Relu" if cut else None)
-        elif cut:
-            ts(out, a, bias if scale == 1.0 else scale, OP.add if scale == 1.0 else OP.mult, 0, OP.max)
-        else:
-            ts(out, a, scale, OP.mult, bias, OP.add)
+        add(q, "lin", out, [a] + ([bias] if isinstance(bias, tuple) else []), (bias, scale, "Relu" if cut else None), max(64, width(out)) * CY)
 
     def gat(out, a, q="A"):
-        add(q, "gat", out, [a], (), 0.06 + width(out) * GA)
+        add(q, "gat", out, [a], (), 0.06 + width(out) * GA if a[0] == "i" else max(64, width(out)) * CY)
+
+    def pool(out, a):
+        add("G", "sel", out, [a], ([[0, width(out)]], 0, 1, OP.is_gt, 0.0), 0.17 + 2 * width(out) * CY)
 
     def put(win, lst, src, n):
         k = width(lst) // n
@@ -193,11 +194,8 @@ def build():
     iota(X("NR", 0, 272), [[0, 17], [1, 16]], 0)
     iota(X("XW", X0 + XA, X0 + MO), [[0, MO - XA]], 0)
     iota(X("F", XA, XD), [[0, XD - XA]], 0)
-    iota(X("E6", 0, 16), [[0, 16]], 0)
-    iota(X("N6", 0, 16), [[0, 16]], 0)
     ms(X("WBH", 0, 144), 0.0)
     iota(X("KC", 0, 256), [[0, 16], [-1, 16]], 0, 15)
-    iota(X("CNT", 0, 1), [[0, 1]], 0)
     ts(X("TI", 0, 1), X("PI", 0, 1), 15, OP.bitwise_and)
     ts(X("TI", 1, 2), X("PI", 0, 1), 4, OP.arith_shift_right)
     ts(X("TI", 2, 3), X("TI", 1, 2), 1, OP.bitwise_and)
@@ -209,8 +207,10 @@ def build():
     n16 = X("NF", 0, 16)
     ts(m128("BLK"), m128("NG"), pg, OP.is_equal)
     ts(X("DELR", 0, 16), n16, pr, OP.is_equal)
+    together(True)
     for r in range(16):
         ts(X("BSEL", 128 * r, 128 * r + 128), m128("BLK"), X("DELR", r, r + 1), OP.mult)
+    together(False)
     tc(X("FDH", 0, 128), m128("DPI"))
     tc(X("FDH", 128, 256), m128("FAI"))
     for k in range(2):
@@ -219,7 +219,7 @@ def build():
             for r in range(4 * i, 4 * i + 4):
                 mm(X("b0", 128 * (r % 4), 128 * (r % 4) + 128), X("BSEL", 128 * r, 128 * r + 128), X("FDH", 128 * k, 128 * k + 128), True, True)
             together(False)
-            (act if CFG["FQ"][4 * k + i] == "A" else tc)(X("F" if k else "DP", 512 * i, 512 * i + 512), X("b0", 0, 512))
+            gat(X("F" if k else "DP", 512 * i, 512 * i + 512), X("b0", 0, 512), CFG["FQ"][4 * k + i])
     for s in range(2):
         src = X("PBI" if s else "PAI", 0, 16)
         ts(X("PX", 32 * s, 32 * s + 16), src, col(4), OP.mult)
@@ -237,7 +237,7 @@ def build():
     tc(col(16), X("HM", 15, 16))
     ts(X("COL", 17, 22), X("NF", 1, 6), -4096, OP.mult, col(16), OP.add)
     for i in range(10):
-        act(X("HF", 256 * i, 256 * i + 256), X("HM", 0, 256))
+        gat(X("HF", 256 * i, 256 * i + 256), X("HM", 0, 256))
 
     def hold(out, src):
         scan(out, src, X("HM", 0, width(out)), OP.min, OP.add, 4096.0)
@@ -266,9 +266,10 @@ def build():
     tt(X("QF", 16, 32), X("QF", 0, 16), ln, OP.add)
     for i, base in enumerate((-896, R2O)):
         lin("A", X("RBK", 16 * i, 16 * i + 16), X("QF", 16, 32), 128.0, float(base))
-    ts(X("TBIG", 0, 256), X("NR", 0, 256), pr, OP.is_ge, 4096, OP.mult)
+    ts(X("TBIG", 0, 256), X("NR", 0, 256), pr, OP.is_le, 4096, OP.mult)
     for i in range(2):
         lin("A", X("DUF", 16 * i, 16 * i + 16), ln, 1.0, float(XD + 256 * i))
+        lin("A", X("DUF", 32 + 16 * i, 48 + 16 * i), ln, 1.0, float(XD + 256 * i + 2576))
     dux = X("DUF", 0, 16)
 
     iota(X("QT", 0, 192), [[0, 64], [1, 3]], 0)
@@ -284,9 +285,11 @@ def build():
     tc(X("L977", 0, 16), X("QI", 48, 64))
 
     def choose(out, first, changes, *more):
+        together(True)
         for i, d in enumerate(changes):
             for s in range(2):
                 tt(X("CH", 48 * (first + i) + 1 + s, 48 * (first + i + 1), 3), w(20 + s), d[s], OP.mult)
+        together(False)
         lo, hi = 48 * first, 48 * (first + len(changes))
         scan(X("CS", lo, hi), X("R3", 0, hi - lo), X("CH", lo, hi), OP.mult, OP.add)
         ts(out, X("CS", lo + 2, hi, 3), *more)
@@ -300,9 +303,10 @@ def build():
             tc(X("LU", 0, 32), X("PU", 0, 32))
             for s in range(2):
                 lin(sm, X("PM", 16 * s, 16 * s + 16), X("PU", 16 * s, 16 * s + 16), 1.0, MARK[s])
-                o = 2560 + 256 * s
-                gat(X("G", o, o + 256), IND(dwin, X("LU", 16 * s, 16 * s + 16)), CFG["CQ"][s])
-                hold(X("SC", o, o + 256), X("G", o, o + 256))
+                for h in range(2):
+                    o = 2560 + 256 * s + 128 * h
+                    gat(X("G", o, o + 128), IND(dwin, X("LU", 16 * s + 8 * h, 16 * s + 8 * h + 8)), CFG["CQ"][s])
+                    hold(X("SC", o, o + 128), X("G", o, o + 128))
             tt(X("DS", 16, 32), X("SC", 2575, 2816, 16), X("SC", 2831, 3072, 16), OP.subtract)
         for s in range(2):
             lin("V", X("DS", 32 + 16 * s, 48 + 16 * s), X("DS", 16, 32), 4096.0 if s else -4096.0, 0.0, True)
@@ -315,12 +319,19 @@ def build():
             ts(X("HF", 512 * k + 15, 512 * k + 512, 16), v, col(17 + k), OP.add, col(16), OP.max)
             for s in range(2):
                 o = 512 * k + 256 * s
-                gat(X("G", o, o + 256), IND(fwin, X("LS", 32 * k + 16 * s, 32 * k + 16 * s + 16)), CFG["CQ"][12 * rnd + 2 + 2 * k + s])
-                scan(X("SC", o, o + 256), X("G", o, o + 256), X("HF", o, o + 256), OP.min, OP.add, 4096.0)
+                n = 16 // CFG["PARTS"][rnd]
+                for c in range(0, 16, n):
+                    a, z, l = o + 16 * c, o + 16 * (c + n), 32 * k + 16 * s + c
+                    gat(X("G", a, z), IND(fwin, X("LS", l, l + n)), CFG["C%d" % rnd][4 * k + 2 * s + c // 8])
+                    scan(X("SC", a, z), X("G", a, z), X("HF", a, z), OP.min, OP.add, 4096.0)
+                    if k < 4:
+                        ts(X("LS", l + 32, l + 32 + n), X("SC", a + 15, z, 16), col(7), OP.add, 2048, OP.min)
                 ck = X("SC", o + 15, o + 256, 16)
                 if k < 4:
-                    ts(X("LS", 32 * k + 32 + 16 * s, 32 * k + 48 + 16 * s), ck, col(7), OP.add, 2048, OP.min)
-                    lin(CFG["CP"][5 * rnd + k], X("C", 80 * s + k + 1, 80 * s + 80, 5), ck, 1.0, 0.0)
+                    if k < 3:
+                        pool(X("C", 80 * s + k + 1, 80 * s + 80, 5), ck)
+                    else:
+                        gat(X("C", 80 * s + k + 1, 80 * s + 80, 5), ck, "V")
         eq, ne = X("E6", 16, 96), X("N6", 16, 96)
         tt(eq, X("C", 0, 80), X("C", 80, 160), OP.is_equal)
         tt(ne, X("C", 0, 80), X("C", 80, 160), OP.not_equal)
@@ -334,13 +345,7 @@ def build():
         tt(X("CE", 64, 96), X("CE", 32, 64), X("CE", 0, 32), OP.mult)
         tt(X("CE", 96, 128), X("CE", 64, 96), top, OP.add)
         ts(X("LA", 0, 32), X("CE", 96, 128), col(7), OP.add)
-        cur[0] = "co"
-        tt(X("PC", 160, 240), X("N6", 15, 95), X("C", 0, 80), OP.mult)
-        scan(X("SS", 160, 240), X("E6", 15, 95), X("PC", 160, 240), OP.mult, OP.add)
-        tt(X("CE", 128, 144), X("SS", 164, 240, 5), X("SC", 2063, 2304, 16), OP.subtract)
-        tt(X("CE", 144, 160), X("CE", 128, 144), X("E6", 20, 96, 5), OP.mult)
-        tt(X("CE", 160, 176), X("CE", 144, 160), X("SC", 2063, 2304, 16), OP.add)
-        ts(X("FL", 0, 16), X("CE", 160, 176), col(7), OP.add)
+        cur[0] = "vf"
         tc(X("AW", 0, 32), X("LA", 0, 32))
         tc(X("AWH", 0, 32), X("LA", 0, 32))
         together(True)
@@ -350,7 +355,7 @@ def build():
         act(X("VALF", 256, 512), X("b3", 0, 256))
         act(X("VALF", 0, 256), X("b3", 256, 512))
 
-        cur[0] = ""
+        cur[0] = "kl"
 
         def la(s):
             return X("LA", 16 * s, 16 * s + 16)
@@ -372,18 +377,19 @@ def build():
         for s in range(2):
             cur[0] = "yb" if s else "ya"
             kids("Y", "KL", s, CFG["Y%d%d" % (rnd, s)])
+        cur[0] = "kf"
         for s in range(2):
             tc(X("KF", 256 * s, 256 * s + 256), X("KL", 256 * s, 256 * s + 256))
         for s in range(2):
-            kb = "b%d" % (5 + s)
             cur[0] = "mb" if s else "ma"
-            mm(X(kb, 0, 256), m128("E0"), X("KC", 0, 256), True, False)
             for h in range(2):
                 base = 4096 * s + 2048 * h
                 soft = (s, h) in relu
                 for i in range(4):
                     together(soft)
                     for j in range(4 * i, 4 * i + 4):
+                        if not soft and j % CFG["MU"] == 0:
+                            together(True)
                         y, m = X("Y", base + j, base + 2048, 16), X("MM", base + 128 * j, base + 128 * j + 128)
                         if soft:
                             c = 128 * (j - 4 * i)
@@ -395,51 +401,67 @@ def build():
                     if soft:
                         act(X("MM", base + 512 * i, base + 512 * i + 512), X("b1", 0, 512), func="Relu")
                     together(True)
+                    apart = CFG["HALVES"][2 * rnd + s] == 2
+                    kb = "bk%d%d" % (s, h * apart)
+                    if i == 0 and (apart or h == 0):
+                        mm(X(kb, 128 * h, 128 * h + (128 if apart else 256)), m128("E0"), X("KC", 0, 128 if apart else 256), True, False)
                     for j in range(4 * i, 4 * i + 4):
-                        mm(X(kb, 128 * h + j, 128 * h + 128, 16), X("MM", base + 128 * j, base + 128 * j + 128), X("SEL", 0, 8), False, h == 1 and j == 15)
+                        mm(X(kb, 128 * h + j, 128 * h + 128, 16), X("MM", base + 128 * j, base + 128 * j + 128), X("SEL", 0, 8), False, (apart or h == 1) and j == 15)
                     together(False)
         for s in range(2):
-            o = 256 * s
-            kb = "b%d" % (5 + s)
-            cur[0] = "lb" if s else "la"
-            scan(X("PS", o, o + 256), X("RMH", 0, 256), X(kb, 0, 256), OP.mult, OP.max)
-            e = 16 + 272 * s
-            tc(X("HK", 16 * s, 16 * s + 16), X("PS", o + 15, o + 256, 16))
-            tt(X("OHT", e, e + 256), IND(X("HK", 16 * s, 16 * s + 16), X("L15", 0, 16)), X("PS", o, o + 256), OP.is_equal)
-            mm(X("b7", 0, 256), m128("EJ"), X("E0", 0, 256), True, False)
-            together(True)
-            for h in range(2):
-                mm(X("b7", 128 * h, 128 * h + 128), X("OHT", e + 128 * h, e + 128 * h + 128), m128("IDB"), False, False)
-                mm(X("b7", 128 * h, 128 * h + 128), X("OHT", e + 128 * h - 1, e + 128 * h + 127), m128("IDN"), False, h == 1)
-            together(False)
-            tt(X("PL", o, o + 256), X("b7", 0, 256), X("KF", o, o + 256), OP.mult)
-            wrap(X("b3", 0, 16), "WBH", X("PL", o, o + 256))
-            tc(X("LL", 16 * s, 16 * s + 16), X("b3", 0, 16))
-            tc(X("ZK", o, o + 256), IND(kwin, X("LL", 16 * s, 16 * s + 16)))
+            n = 256 // CFG["HALVES"][2 * rnd + s]
+            for a in range(0, 256, n):
+                o, l, e = 256 * s + a, 16 * s + a // 16, 16 + 272 * s + a
+                cur[0] = "lb" if s else "la"
+                scan(X("PS", o, o + n), X("RMH", 0, n), X("bk%d%d" % (s, a // 128), a, a + n), OP.mult, OP.max)
+                tc(X("HK", l, l + n // 16), X("PS", o + 15, o + n, 16))
+                tt(X("OHT", e, e + n), IND(X("HK", l, l + n // 16), X("L15", 0, n // 16)), X("PS", o, o + n), OP.is_equal)
+                together(True)
+                mm(X("b7", 0, n), m128("EJ"), X("E0", 0, n), True, False)
+                for h in range(0, n, 128):
+                    mm(X("b7", h, h + 128), X("OHT", e + h, e + h + 128), m128("IDB"), False, False)
+                    mm(X("b7", h, h + 128), X("OHT", e + h - 1, e + h + 127), m128("IDN"), False, h + 128 == n)
+                together(False)
+                tt(X("PL", o, o + n), X("b7", 0, n), X("KF", o, o + n), OP.mult)
+                wrap(X("b3", 0, n // 16), "WBH", X("PL", o, o + n))
+                tc(X("LL", l, l + n // 16), X("b3", 0, n // 16))
+                tc(X("ZK", o, o + n), IND(kwin, X("LL", l, l + n // 16)))
+                cur[0] = ""
+                if not last:
+                    act(X("OHS", o, o + n), X("b7", 0, n), scale=-1.0 if s else 1.0)
             cur[0] = "zb" if s else "za"
             kids("Z", "ZK", s, CFG["Z%d%d" % (rnd, s)])
-            cur[0] = ""
-            tc(X("LW", 16 * s, 16 * s + 16), X("LL", 16 * s, 16 * s + 16))
-            if not last:
-                act(X("OHS", o, o + 256), X("b7", 0, 256), scale=-1.0 if s else 1.0)
-        cur[0] = "co"
+        cur[0] = ""
+        tc(X("LW", 0, 32), X("LL", 0, 32))
+        cur[0] = "eq"
         tc(X("FG", 0, 256), IND(fwin, la(0)))
-        tc(X("FWH", 0, 16), X("FL", 0, 16))
-        tc(X("FW", 0, 16), X("FL", 0, 16))
+        hold(X("SC", 0, 256), X("FG", 0, 256))
+        ts(X("FWH", 0, 16), X("SC", 15, 256, 16), col(7), OP.add)
+        lin("V", X("FW", 0, 16), X("SC", 15, 256, 16), 1.0, col(7))
+        cur[0] = "qd"
         together(True)
         mm(X("b2", 0, 256), m128("IDB"), X("TBIG", 0, 256), True, False)
         for r in range(16):
             mm(X("b2", r, 256, 16), m128("IDH"), X("FWH", 0, 16), False, r == 15)
         together(False)
         tt(X("EQD", 0, 256), X("FG", 0, 256), X("b2", 0, 256), OP.is_equal)
-        scan(X("SQD", 0, 256), X("RMH", 0, 256), X("EQD", 0, 256), OP.mult, OP.max)
+        cur[0] = "eq"
+        for lo, hi in ((1, 6), (6, 10), (10, 13), (13, 16)):
+            together(True)
+            for c in range(lo, hi):
+                ts(X("EQ", 8 * c * (c - 1), 8 * c * (c + 1)), X("FG", 256 - 16 * c, 256), X("FW", 15 - c, 16 - c), OP.is_equal)
+            together(False)
+        together(True)
+        mm(X("b2", 0, 256), m128("BLK"), X("EQD", 0, 256), True, False)
         for c in range(1, 16):
-            o = 8 * c * (c - 1)
-            ts(X("EQ", o, o + 16 * c), X("FG", 0, 16 * c), X("FW", c, c + 1), OP.is_equal)
-            add("A", "count", X("EQS", o, o + 16 * c), [X("EQ", o, o + 16 * c)], (X("CNT", c, c + 1),), max(64, 16 * c) * CY + 0.02)
-        aw, bw, lw = X("AW", 0, 16), X("AW", 16, 32), X("LW", 0, 16)
-        tt(w(1), X("CNT", 0, 16), X("SQD", 15, 256, 16), OP.add)
-        ts(w(2), w(1), 0, OP.is_equal)
+            if c == 10:
+                together(True)
+            mm(X("b2", 256 - 16 * c, 256), m128("BLK"), X("EQ", 8 * c * (c - 1), 8 * c * (c + 1)), False, c == 15)
+        together(False)
+        hold(X("SC", 512, 768), X("b2", 0, 256))
+        cur[0] = "pre"
+        aw, bw = X("AW", 0, 16), X("AW", 16, 32)
+        ts(w(2), X("SC", 527, 768, 16), col(8), OP.is_equal)
         tt(w(3), aw, bw, OP.not_equal)
         tt(w(5), w(3), X("CE", 0, 16), OP.mult)
         tt(w(6), w(2), w(5), OP.mult)
@@ -451,6 +473,7 @@ def build():
             lin(sm, w(26 + i), w(5), -90.0, 99.0)
         tt(w(44, 2), X("LW", 0, 32), X("DUF", 0, 32), OP.subtract)
         tt(w(16, 2), w(44, 2), w(8, 2), OP.mult)
+        tt(X("CH", 288, 384, 3), w(16, 2), X("DUF", 32, 64), OP.add)
         if not last:
             tt(w(46, 2), X("AW", 0, 32), X("DUF", 0, 32), OP.subtract)
             tt(w(18, 2), w(46, 2), w(8, 2), OP.mult)
@@ -465,12 +488,14 @@ def build():
         for i, src in enumerate(("SY", "SZ")):
             wrap(X("b0", 0, 16), "WBW", X(src, 15, 4096), i == 0, i == 1, 16)
         if not last:
-            mm(X("bs", 0, 12), m128("IDH"), X("L977", 4, 16), True, False)
-            for i in range(4):
-                wrap(X("bs", 0, 12), "WBW", X("SZ" if i > 1 else "SY", 4096 * (i % 2) + 1039, 4096 * (i % 2) + 4096), False, i == 3, 16)
-        act(X("XW", X0 + MO, X0 + MO + 256), X("SY", 15, 4096, 16))
-        act(X("XW", X0 + MO + 256, X0 + MO + 512), X("SZ", 15, 4096, 16))
-        cur[0] = ""
+            cur[0] = "sb"
+            wrap(X("bs", 0, 12), "WBW", X("SY", 4096 + 1039, 8192), True, False, 16)
+            mm(X("bs", 0, 12), m128("IDH"), X("L977", 4, 16), False, False)
+            wrap(X("bs", 0, 12), "WBW", X("SZ", 4096 + 1039, 8192), False, True, 16)
+        cur[0] = "su"
+        for i, src in enumerate(("SY", "SZ")):
+            pool(X("XW", X0 + MO + 256 * i, X0 + MO + 256 * i + 256), X(src, 15, 4096, 16))
+        cur[0] = "gl"
         for i in range(3):
             mm(X("b4", 0, 256), m128("IDN" if i == 1 else "IDB"), X("SZ" if i == 2 else "SY", 4096 * (i % 2) + 15, 4096 * (i % 2) + 4096, 16), i == 0, i == 2)
         tt(X("GL", 0, 256), X("b4", 0, 256), X("SZ", 4111, 8192, 16), OP.is_gt)
@@ -484,10 +509,16 @@ def build():
         for s in range(2):
             tt(w(52 + s), X("LW", 16 * s, 16 * s + 16), root, OP.subtract)
         cur[0] = "vd"
+        together(True)
+        for i in range(2):
+            for s in range(2):
+                ts(X("CH", 288 + 48 * i + 1 + s, 336 + 48 * i, 3), X("b2", 16 * s, 16 * s + 16), 9, OP.is_ge, -2576, OP.mult)
+        together(False)
+        scan(X("CS", 288, 384), X("R3", 0, 96), X("CH", 288, 384), OP.mult, OP.add)
+        tc(X("LF", 0, 32), X("CS", 290, 384, 3))
         tt(w(20, 2), X("b2", 0, 32), w(26, 2), OP.is_ge)
-        choose(X("LF", 0, 32), 0, [(w(16), w(16)), (w(17), w(17))], 0, OP.add)
         cur[0] = "fs"
-        put(X("F", 0, 2576), X("LF", 0, 32), X("VALF", 0, 512), CFG["PUT"][rnd])
+        put(X("F", 0, 5152), X("LF", 0, 32), X("VALF", 0, 512), CFG["PUT"][rnd])
         cur[0] = "xw"
         choose(X("LT", 0, 48), 2, [(w(48 + 2 * i), w(49 + 2 * i)) for i in range(3)], 0 if last else X0, OP.add)
         choose(X("LX", 0, 16), 5, [(w(56), w(57))], 0, OP.add)
@@ -523,21 +554,19 @@ def build():
         gat(X("G", 2560, 2816), IND(dwin, la(0)))
         hold(X("SC", 2560, 2816), X("G", 2560, 2816))
         tt(w(36), X("SC", 2575, 2816, 16), w(12), OP.add)
-        ts(kn(4), X("SC", 2575, 2624, 16), col(7), OP.add, 1, OP.add)
-        ts(X("KN", 20, 28), X("KN", 0, 8), 2047, OP.not_equal)
-        for s in range(2):
-            tt(kn(7 + s), kn(5 + s), kn(4), OP.mult)
-        ts(kn(9), X("W", 576, 580), col(7), OP.add)
-        tt(X("W", 592, 596), kn(9), kn(7), OP.subtract)
+        tc(X("LU", 16, 24), X("KN", 0, 8))
+        gat(X("G", 0, 128), IND(dwin, X("LU", 16, 24)))
+        hold(X("SC", 256, 384), X("G", 0, 128))
+        tt(X("W", 592, 596), X("W", 576, 580), X("SC", 271, 320, 16), OP.subtract)
         tt(w(38), w(13), w(12), OP.subtract)
-        tt(kn(10), kn(8), kn(7), OP.subtract)
+        tt(kn(10), X("SC", 335, 384, 16), X("SC", 271, 320, 16), OP.subtract)
         tt(X("W", 608, 612), X("W", 608, 612), kn(10), OP.subtract)
         cur[0] = "nb"
-        tc(X("LSI", 16, 28), X("bs", 0, 12))
+        tt(X("LSI", 16, 28), X("bs", 0, 12), X("SI", 4, 16), OP.add)
         ts(X("LSI", 0, 12), X("LSI", 16, 28), 2047, OP.bitwise_and)
         tc(X("LU", 0, 12), X("LSI", 0, 12))
         ts(X("PM", 20, 32), X("LSI", 0, 12), MARK[1], OP.add)
-        gat(X("G", 2816, 3008), IND(dwin, X("LU", 0, 12)), CFG["CQ"][12])
+        gat(X("G", 2816, 3008), IND(dwin, X("LU", 0, 12)), CFG["CQ"][2])
         scan(X("SC", 2816, 3008), X("G", 2816, 3008), X("HM", 0, 192), OP.min, OP.add, 4096.0)
         tt(X("W", 596, 608), X("W", 580, 592), X("SC", 2831, 3008, 16), OP.subtract)
         cur[0] = "vd"
@@ -554,8 +583,10 @@ def build():
         together(False)
         for s in range(2):
             tt(X("TK", 256 * s, 256 * s + 256), X("b1", 0, 256), X("OHS", 256 * s, 256 * s + 256), OP.mult)
+        together(True)
         mm(X("b4", 0, 512), m128("IDH"), X("KF", 0, 512), True, False)
         mm(X("b4", 0, 512), m128("IDH"), X("TK", 0, 512), False, True)
+        together(False)
         act(X("NK", 0, 512), X("b4", 0, 512))
         choose(X("LF", 32, 64), 0, [(w(18), w(18)), (w(19), w(19))], 0, OP.add)
         put(X("KD", 0, 2576), X("LF", 32, 64), X("NK", 0, 512), CFG["PUT"][4])
@@ -685,9 +716,155 @@ def order(P, preds):
         if best is None or got[0] < best[0]:
             best = got
         prio = [e for _, e in sweep(succ, [e for _, e in got[1]], got[3])[1]]
-    _, t, seq, queue, preds, bank = best
+    tau, seen = [s for s, _ in best[1]], {}
+    known = {r: min(tau[i] for i in range(n) if P[i]["b"] == "kl" + r) for r in "01"}
     for i, p in enumerate(P):
-        p["t"] = t[i]
+        if p["b"][:-1] in CFG["PLAN"]:
+            a, d = CFG["PLAN"][p["b"][:-1]]
+            seen[p["b"]] = seen.get(p["b"], -1) + (p["g"] == i and p["q"] != "T")
+            tau[i] = known[p["b"][-1]] + a + d * seen[p["b"]]
+    got = sweep(preds, [-s for s in tau], None)
+    if CFG["PLAN"]:
+        best = got
+    seq, queue = best[2:4]
+    ids = [P[i]["g"] for i in seq if P[i]["g"] == i]
+    at = {u: k for k, u in enumerate(ids)}
+    m = len(ids)
+    off, tail, need = {}, [0.0] * m, [dict() for _ in ids]
+    for u in ids:
+        s = 0.0
+        for i in units[u]:
+            off[i] = s
+            s += P[i]["cost"]
+            tail[at[u]] = max(tail[at[u]], s + late[i])
+    above = [0] * m
+    for k, u in enumerate(ids):
+        for i in units[u]:
+            for j, h in preds[i].items():
+                z = at[P[j]["g"]]
+                if z != k:
+                    need[k][z] = max(need[k].get(z, 0.0), off[j] + P[j]["cost"] + late[j] + wake(i, j, h) - off[i])
+        far = 0
+        for z in need[k]:
+            far |= above[z]
+        above[k] = far | sum(1 << z for z in need[k])
+        need[k] = [(z, d) for z, d in need[k].items() if not far >> z & 1 or d > 1.5]
+    size = [length[u] for u in ids]
+    lane = ["AVTGSNW".index(queue[u]) for u in ids]
+    inner = {z for k in range(m) for z, d in need[k]}
+    ends = [k for k in range(m) if k not in inner]
+
+    touch = [sorted({v for i in units[u] for v in P[i]["use"]}) for u in ids]
+    users = {v: len({P[i]["g"] for i in uses[v]}) for v in uses}
+    either = [P[u]["what"] in ("gat", "lin") for u in ids]
+
+    def times(row, lo, old):
+        lo -= lo % 24
+        st, by, marks = list(old[0]), list(old[1]), old[2][:lo // 24 + 1]
+        free, last, idle, bank, left, till = [z.copy() for z in marks[-1]]
+        for n_ in range(lo, span[1]):
+            k = row[n_]
+            if n_ % 24 == 0 and n_ > lo:
+                marks.append((free[:], last[:], idle[:], bank.copy(), left.copy(), till.copy()))
+            q = lane[k]
+            a, b = free[q], last[q]
+            for z, d in need[k]:
+                d += st[z]
+                if d > a:
+                    a, b = d, z
+            if not touch[k]:
+                st[k], by[k], free[q], last[q] = a, b, a + size[k], k
+                continue
+            for v in touch[k]:
+                if v not in bank:
+                    if not idle:
+                        return 1e9, None, None, None
+                    got = min(idle)
+                    idle.remove(got)
+                    bank[v], till[v] = got[1], (0.0, k)
+                    if got[0] > a:
+                        a, b = got[0], got[2]
+            st[k], by[k], free[q], last[q] = a, b, a + size[k], k
+            for v in touch[k]:
+                till[v] = max(till[v], (a + size[k] + WK, k))
+                left[v] -= 1
+                if not left[v]:
+                    idle.append((till[v][0], bank[v], till[v][1]))
+        if span[1] == m:
+            k = max(ends, key=lambda z: st[z] + tail[z])
+            end = st[k] + tail[k]
+        else:
+            k = span[2]
+            end = st[k] + 0.5 * sum(max(0.0, free[q] - st[k] - size[k]) for q in range(2))
+        chain = []
+        while k is not None and place[k] >= span[0]:
+            chain.append(k)
+            k = by[k]
+        return end + CFG["PULL"] * sum([st[z] for z in row[span[0]:span[1]]]) / (span[1] - span[0]), (st, by, marks), chain, bank
+    row, place, span, y = list(range(m)), list(range(m)), [0, m, None], 1
+    blank = ([0.0] * m, [None] * m, [([0.0] * 7, [None] * 7, [(0.0, b, None) for b in range(8)], {}, users, {})])
+    stops = [min(k for k, u in enumerate(ids) if P[u]["b"] == b and P[u]["q"] in "AV") for b in ("ya0", "gl0", "ya1", "gl1")]
+    for a, z, steps in CFG["REPAIR"]:
+        span[:] = [0, m, None]
+        row = sorted(row, key=lambda k, st=times(row, 0, blank)[1][0]: st[k])
+        for n_, k in enumerate(row):
+            place[k] = n_
+        span[:] = [max(0, place[stops[a - 1]] - CFG["LAP"]) if a else 0, place[stops[z]] + 1 if z < 4 else m, stops[z] if z < 4 else None]
+        end, now, chain, bank = times(row, 0, blank)
+        kept = (end, row, list(lane))
+        for step in range(steps):
+            y = (y * 6364136223846793005 + 1442695040888963407) % 2 ** 64
+            x = y >> 30
+            u = chain[(x >> 8) % len(chain)] if x & 255 < CFG["CHAIN"] else row[span[0] + (x >> 8) % (span[1] - span[0])]
+            y = (y * 6364136223846793005 + 1442695040888963407) % 2 ** 64
+            x = y >> 30
+            i = place[u]
+            flip = either[u] and x >> 16 & 3 == 0
+            if flip:
+                lane[u] = 1 - lane[u]
+            far, past, way = 0, 1 + min((x >> 9) % CFG["FAR"], (x >> 21) % CFG["FAR"]), -1 if x >> 8 & 1 else 1
+            while past and span[0] <= i + way * (far + 1) < span[1]:
+                far += 1
+                past -= lane[row[i + way * far]] == lane[u]
+            lo, hi = (i - far, i) if way < 0 else (i, i + far)
+            part = row[lo:hi + 1]
+            if way < 0:
+                new = [z for z in part if z == u or above[u] >> z & 1] + [z for z in part if z != u and not above[u] >> z & 1]
+            else:
+                new = [z for z in part if z != u and not above[z] >> u & 1] + [z for z in part if z == u or above[z] >> u & 1]
+            if new == part and not flip:
+                continue
+            new = row[:lo] + new + row[hi + 1:]
+            e, s, c, b = times(new, lo, now)
+            if e <= end + CFG["WORSE"] * (1 - step / steps) * (x >> 28 & 7) / 7:
+                end, now, chain, row = e, s, c, new
+                for n_ in range(lo, hi + 1):
+                    place[row[n_]] = n_
+                if end < kept[0]:
+                    kept = (end, new, list(lane))
+            elif flip:
+                lane[u] = 1 - lane[u]
+            if step % 64 == 0:
+                new = row[:span[0]] + sorted(row[span[0]:span[1]], key=lambda z: now[0][z]) + row[span[1]:]
+                e, s, c, b = times(new, span[0], now)
+                if e <= end:
+                    end, now, chain, row = e, s, c, new
+                    for n_, k in enumerate(row):
+                        place[k] = n_
+        row, lane[:] = kept[1:]
+    span[:] = [0, m, None]
+    _, (st, _, _), _, bank = times(row, 0, blank)
+    seq = [i for k in row for i in units[ids[k]]]
+    preds, holder = [dict(d) for d in preds], [None] * 8
+    for i in seq:
+        p = P[i]
+        a = st[at[p["g"]]] + off[i]
+        p["t"], queue[i] = (a, a + p["cost"] + late[i]), "AVTGSNW"[lane[at[p["g"]]]]
+        for v in p["use"]:
+            if holder[bank[v]] != v:
+                for j in uses.get(holder[bank[v]], []):
+                    preds[i][j] = preds[i].get(j, False) or P[j]["q"] != "T"
+                holder[bank[v]] = v
 
     def named(a):
         if isinstance(a, tuple) and a and a[0] == "x" and a[1][0] == "b":
@@ -792,7 +969,13 @@ def rank_program(g, core, T, topo):
             h = e.activation(out, ins[0], AF.Copy)
         elif what == "count":
             h = e.activation(out, ins[0], AF.Copy, accum_out=ap(args[0]))
-        elif what == "act":
+        elif what == "lin" and q == "V":
+            bias, scale, cut = args
+            if cut:
+                h = e.tensor_scalar(out, ins[0], bias if scale == 1.0 else scale, 0, OP.add if scale == 1.0 else OP.mult, OP.max)
+            else:
+                h = e.tensor_scalar(out, ins[0], scale, sc(bias), OP.mult, OP.add)
+        elif what in ("act", "lin"):
             bias, scale, func = args
             if bias is None and scale == 1.0 and func is None:
                 h = e.activation(out, ins[0], AF.Copy)
@@ -811,6 +994,8 @@ def rank_program(g, core, T, topo):
             h = e.transpose(out, ins[0])
         elif what == "ms":
             h = e.memset(out, args[0])
+        elif what == "sel":
+            h = e.affine_select(out, ins[0], args[0], args[3], args[4], args[2], args[1])
         elif what == "iota":
             h = e.iota(out, args[0], args[2], args[1], allow_small_or_imprecise_dtypes=True)
         h.then_inc(T.sem["q" + q], 1)

@@ -8,38 +8,39 @@ MARK = (0.25, 0.375)
 
 SCRATCH = {}
 for _n, _w, _d in (
-        ("XW", X0 + XEND, "bfloat16"), ("KD", 2576, "int32"), ("F", 5152, "float32"), ("DP", 2048, "bfloat16"),
+        ("XW", X0 + XEND, "bfloat16"), ("KD", 2576, "float32"), ("KI", 2048, "int32"), ("F", 5152, "float32"), ("DP", 2048, "bfloat16"),
+        ("ZK", 512, "uint16"), ("Z", 8192, "bfloat16"), ("SZ", 8192, "bfloat16"), ("SY", 8192, "bfloat16"), ("RMB", 1024, "bfloat16"),
         ("FAI", 128, "int32"), ("DPI", 128, "int32"), ("PAI", 16, "int32"), ("PBI", 16, "int32"), ("WTI", 1, "int32"), ("FDH", 256, "float16"),
         ("PI", 1, "int32"), ("TI", 3, "int32"), ("COL", 32, "float32"), ("NF", 128, "float32"), ("NR", 272, "float32"), ("NG", 256, "float32"),
-        ("BLK", 128, "float16"), ("NBLK", 128, "float16"), ("WBH", 144, "float16"), ("WBB", 144, "bfloat16"), ("WBW", 144, "bfloat16"),
-        ("IDB", 128, "bfloat16"), ("IDN", 128, "bfloat16"), ("ID2", 128, "bfloat16"), ("IDH", 128, "float16"), ("BSEL", 2048, "float16"), ("DELR", 16, "float32"),
-        ("RMH", 256, "float16"), ("SEL", 8, "bfloat16"), ("KC", 256, "bfloat16"), ("E0", 256, "bfloat16"), ("RMB", 1024, "bfloat16"),
-        ("L15", 16, "uint16"), ("LN", 16, "float32"), ("L977", 16, "float16"), ("QI", 64, "int32"), ("QT", 192, "float32"), ("R3", 192, "bfloat16"), ("CH", 384, "float32"), ("CS", 384, "float32"), ("MD", 96, "float32"), ("CE", 176, "float32"), ("QF", 32, "float32"), ("TBIG", 256, "bfloat16"), ("DUF", 64, "float32"),
+        ("BLK", 128, "float16"), ("NBLK", 128, "bfloat16"), ("ZB", 256, "bfloat16"), ("WBB", 144, "bfloat16"), ("WBW", 144, "bfloat16"),
+        ("IDB", 128, "bfloat16"), ("IDN", 128, "bfloat16"), ("ID2", 128, "bfloat16"), ("TRI", 128, "bfloat16"), ("BSEL", 2048, "float16"), ("DELR", 16, "float32"),
+        ("RMH", 256, "bfloat16"), ("SEL", 8, "bfloat16"), ("KC", 256, "bfloat16"), ("E0", 256, "bfloat16"),
+        ("L15", 16, "uint16"), ("LN", 16, "float32"), ("L977", 16, "float16"), ("QI", 64, "int32"), ("R3", 192, "bfloat16"), ("CH", 528, "float32"), ("CS", 528, "float32"), ("MD", 96, "float32"), ("CE", 192, "float32"), ("QF", 32, "float32"), ("TBIG", 256, "bfloat16"), ("DUF", 64, "float32"),
         ("RBK", 32, "float32"), ("EQ", 1920, "float16"),
         ("PX", 64, "float32"), ("PT", 64, "float32"), ("PU", 32, "float32"),
         ("G", 3072, "float32"), ("SC", 3072, "float32"), ("LS", 160, "uint16"), ("LU", 32, "uint16"), ("LSI", 32, "int32"), ("HM", 800, "bfloat16"), ("DS", 96, "float32"), ("PM", 32, "float32"),
         ("HK", 160, "float32"), ("C", 192, "float32"), ("E6", 112, "float32"), ("N6", 112, "float32"), ("PC", 288, "float32"), ("SS", 288, "float32"),
         ("AW", 32, "float32"), ("AWH", 32, "float16"), ("LA", 32, "uint16"), ("VALF", 512, "float32"),
         ("KL", 512, "uint16"), ("KF", 512, "float16"), ("XS", 512, "bfloat16"), ("Y", 8192, "bfloat16"), ("MM", 8192, "bfloat16"),
-        ("EJ", 128, "bfloat16"), ("PS", 512, "float32"), ("OHT", 544, "bfloat16"), ("OHS", 512, "bfloat16"), ("PL", 512, "float16"), ("LL", 32, "uint16"), ("LW", 32, "float32"),
-        ("ZK", 512, "uint16"), ("Z", 8192, "bfloat16"), ("SZ", 8192, "bfloat16"), ("SY", 8192, "bfloat16"), ("HF", 2560, "float32"), ("FG", 256, "float16"), ("FWH", 16, "float16"), ("FW", 16, "float32"), ("FL", 16, "uint16"),
+        ("EJ", 144, "bfloat16"), ("PS", 512, "float32"), ("OHT", 544, "bfloat16"), ("OHS", 512, "bfloat16"), ("PL", 512, "float16"), ("LL", 32, "uint16"), ("LW", 32, "float32"),
+        ("HF", 1024, "float32"), ("FG", 256, "float16"), ("FWH", 16, "float16"), ("FW", 16, "float32"),
         ("EQD", 256, "float16"), ("GL", 512, "bfloat16"), ("W", 1152, "float32"), ("SI", 64, "int32"), ("KDS", 128, "float32"), ("KN", 48, "float32"),
-        ("LT", 48, "uint16"), ("LX", 16, "uint16"), ("LF", 64, "uint16"), ("TG", 768, "bfloat16"), ("VI", 256, "int32"), ("TK", 512, "float16"), ("NK", 512, "float32")):
+        ("LT", 48, "uint16"), ("LX", 32, "uint16"), ("LF", 64, "uint16"), ("TG", 1024, "bfloat16"), ("VI", 512, "int32"), ("PQ", 192, "float32"), ("TK", 512, "float16"), ("NK", 512, "float32")):
     SCRATCH[_n] = ("sbuf", [128, _w], _d)
 for _b in range(8):
     SCRATCH["b%d" % _b] = ("psum", [128, 512], "float32")
-SEMAPHORES = ["qV", "qA", "qT", "qG", "sent1", "sent2", "arr1", "arr2"] + ["d%d" % _i for _i in range(12)]
+SEMAPHORES = ["qV", "qA", "qT", "qG", "sent1", "sent2", "arr1", "arr2"] + ["d%d" % _i for _i in range(11)]
 
 CFG = dict(
     HALVES=[2, 2, 2, 2],
     PLAN=dict(kl=(0, 0.1), ya=(0.6, 1.0), kf=(2.2, 0), ma=(2.4, 0.3), la=(2.0, 0.1), yb=(4.9, 1.4), mb=(7.9, 0.3), lb=(7.0, 0.1), za=(10.6, 1.4), zb=(16.3, 0.7),
-              Sya=(12, 0.5), Syb=(14, 0.5), Sza=(14.5, 0.5), Szb=(17, 0.7), eq=(13, 0.1), qd=(13.5, 0), vf=(14, 0), pre=(16, 0.05), np=(16.5, 0.05), su=(17, 0.1), sb=(17.5, 0), gl=(17.2, 0)),
-    Y00="AVAA", Y01="AAAA", Y10="AVAA", Y11="AAAA", Z00="AAAA", Z01="AAAAAAAV", Z10="AAAA", Z11="AAAAAAAV",
+              Sya=(12, 0.5), Syb=(14, 0.5), Sza=(14.5, 0.5), Szb=(17, 0.7), eq=(13, 0.1), qd=(13.5, 0), vf=(14, 0), pre=(16, 0.05), np=(16.5, 0.05), su=(17, 0.1), sb=(17.5, 0), gl=(17.2, 0), xp=(21, 0.3), du0=(-14, 0)),
+    Y00="AVAA", Y01="AAAA", Y10="AVAA", Y11="AAAA", Z00="AAAA", Z01="AAAAAAAA", Z10="AAAA", Z11="AAAAAAAA",
     RQ="VVVVVVVV",
-    CQ="VAA", C0="AAAV" * 5, C1="A" * 20, PARTS=[2, 2], FQ="AVAVAVAV", TQ="AAAAVA", SM="VA",
-    PUT=[1, 2, 1, 1, 4],
-    SLACK={'T': 0.6, 'V': 0.6, 'A': 0.6}, MARGIN=0.0, KEEP=1, SWEEPS=3, REPAIR=[(0, 0, 30000), (1, 1, 50000), (2, 2, 30000), (3, 3, 50000), (4, 4, 20000)], LAP=30, MU=2, FAR=16, CHAIN=60, PULL=0.03, WORSE=0.08,
-    BOOST={'nb0': 1, 'ya1': -1, 'gl1': 1, 'qd0': 8, 'xw1': 8, 'Sza0': 1, 'sb0': -1, 'ya0': 1, 'lb1': 5, 'fs0': 16, 'za0': -1, 'za1': 1, 'kf0': -8, 'Szb1': -12, 'Sza1': -5, 'vf0': -1, 'pre1': -3, 'qd1': 1})
+    CQ="VAA", C0="A" * 20, C1="A" * 20, PARTS=[2, 2], FQ="AVAVAVAV", TQ="AAAAAA", SM="AA",
+    PUT=[1, 1, 1, 1, 2], KLP=[(0, 4), (4, 16), (16, 32)], BOTH=[0, 1], PQ="AAA", KNOWN=(13.5, 47, 76), SEED=1,
+    SLACK={'T': 0.6, 'V': 0.6, 'A': 0.6}, MARGIN=0.0, KEEP=1, LAP=30, MU=2, FAR=16, CHAIN=100, PULL=0.03, WORSE=0.08,
+    REPAIR=[(0, 0, 30000), (1, 2, 110000), (3, 4, 90000)])
 CY, GA, SCA, WS, WK, BW = 0.00087, 0.00133, 0.003, 0.2, 0.2, 400e3
 
 
@@ -130,7 +131,7 @@ def build():
         add("V", "scan", out, [d0, d1] + ([init] if isinstance(init, tuple) else []), (o0, o1, init), ccost(out, [d0, d1], True))
 
     def act(out, a, bias=None, scale=1.0, func=None):
-        c = 0.065 + width(out) * GA if a[0] == "i" else max(64, width(out)) * CY
+        c = 0.065 + width(out) * GA if a[0] == "i" else 0.065 + width(out) * SCA if out[0] == "i" else max(64, width(out)) * CY
         add("A", "act", out, [a] + [s for s in (bias, scale) if isinstance(s, tuple)], (bias, scale, func), c)
 
     def lin(q, out, a, scale, bias, cut=False):
@@ -142,18 +143,26 @@ def build():
     def pool(out, a):
         add("G", "sel", out, [a], ([[0, width(out)]], 0, 1, OP.is_gt, 0.0), 0.17 + 2 * width(out) * CY)
 
-    def put(win, lst, src, n):
+    def sel(out, pat, cm, base, cmp, fill, same=False):
+        add("G", "sel", out, [out if same else X("ZB", 0, width(out))], (pat, cm, base, cmp, fill), 0.17 + 2 * width(out) * CY)
+
+    def put(win, lst, src, n, q=None):
         k = width(lst) // n
         for i in range(n):
-            tc(IND(win, X(lst[1], lst[2] + k * i, lst[2] + k * i + k)), X(src[1], src[2] + 16 * k * i, src[2] + 16 * k * (i + 1)))
+            out, a = IND(win, X(lst[1], lst[2] + k * i, lst[2] + k * i + k)), X(src[1], src[2] + 16 * k * i, src[2] + 16 * k * (i + 1))
+            if q:
+                add(q, "put", out, [a], (), 0.06 + 16 * k * SCA)
+            else:
+                tc(out, a)
+
 
     def mm(out, l, r, start, stop):
         add("T", "mm", out, [l, r], (start, stop), max(64, width(r)) * CY)
 
-    def wrap(out, sel, src, start=True, stop=True, step=1):
+    def wrap(out, sel, src, start=True, stop=True):
         together(True)
         for r in range(16):
-            mm(out, X(sel, 15 - r, 143 - r), X(src[1], src[2] + r * step, src[3], 16 * step), start and r == 0, stop and r == 15)
+            mm(out, X(sel, 15 - r, 143 - r), X(src[1], src[2] + r * src[4], src[3], 16 * src[4]), start and r == 0, stop and r == 15)
         together(False)
 
     def dma(q, out, a, sem):
@@ -182,8 +191,9 @@ def build():
     dma("S", X("DPI", 0, 128), ("d", "dp"), "d1")
     dma("S", X("PAI", 0, 16), ("d", "pa"), "d2")
     dma("S", X("WTI", 0, 1), ("d", "wt"), "d4")
+    for i in range(2):
+        dma("S", X("KI", 1024 * i, 1024 * i + 1024), ("d", "kd", 1024 * i, 1024 * i + 1024), ("d5", "d10")[i])
     dma("S", X("XW", X0, X0 + 2048), ("d", "xs"), "d6")
-    dma("S", X("KD", 0, 2048), ("d", "kd"), "d5")
     together(False)
     add("G", "send", None, [X("XW", X0, X0 + 128)], (1,), 1.0)
     add("N", "arrive", X("XW", 0, 896), [], (1,), 0)
@@ -194,16 +204,15 @@ def build():
     iota(X("NR", 0, 272), [[0, 17], [1, 16]], 0)
     iota(X("XW", X0 + XA, X0 + MO), [[0, MO - XA]], 0)
     iota(X("F", XA, XD), [[0, XD - XA]], 0)
-    ms(X("WBH", 0, 144), 0.0)
+    iota(X("ZB", 0, 256), [[0, 256]], 0)
     iota(X("KC", 0, 256), [[0, 16], [-1, 16]], 0, 15)
     ts(X("TI", 0, 1), X("PI", 0, 1), 15, OP.bitwise_and)
     ts(X("TI", 1, 2), X("PI", 0, 1), 4, OP.arith_shift_right)
     ts(X("TI", 2, 3), X("TI", 1, 2), 1, OP.bitwise_and)
     tc(X("COL", 0, 2), X("TI", 0, 2))
-    tc(col(2), X("PI", 0, 1))
     tc(col(3), X("TI", 2, 3))
     ts(col(4), col(3), -1, OP.mult, 1, OP.add)
-    pr, pg, pc = col(0), col(1), col(2)
+    pr, pg = col(0), col(1)
     n16 = X("NF", 0, 16)
     ts(m128("BLK"), m128("NG"), pg, OP.is_equal)
     ts(X("DELR", 0, 16), n16, pr, OP.is_equal)
@@ -227,7 +236,7 @@ def build():
     add("V", "tr", X("PT", 0, 64), [X("PX", 0, 64)], (), 0.07)
     for s in range(2):
         tt(X("PU", 16 * s, 16 * s + 16), X("PT", 32 * s, 32 * s + 16), X("PT", 32 * s + 16, 32 * s + 32), OP.add)
-    ts(X("RMH", 0, 256), X("NR", 0, 256), 0, OP.not_equal)
+    sel(X("RMH", 0, 256), [[0, 16], [1, 16]], 0, 0, OP.is_equal, 1.0)
     ts(X("HM", 256, 528), X("NR", 0, 272), pr, OP.is_equal, -4096, OP.mult)
     ts(X("HM", 544, 800), X("HM", 257, 513), -2, OP.mult)
     tt(X("HM", 0, 256), X("HM", 256, 512), X("HM", 544, 800), OP.add)
@@ -236,27 +245,26 @@ def build():
     ts(col(7), col(8), -1, OP.mult)
     tc(col(16), X("HM", 15, 16))
     ts(X("COL", 17, 22), X("NF", 1, 6), -4096, OP.mult, col(16), OP.add)
-    for i in range(10):
+    for i in range(4):
         gat(X("HF", 256 * i, 256 * i + 256), X("HM", 0, 256))
 
     def hold(out, src):
         scan(out, src, X("HM", 0, width(out)), OP.min, OP.add, 4096.0)
-    ts(X("WBH", 15, 143, 16), X("NF", 0, 8), pg, OP.is_equal)
-    tc(X("WBB", 0, 144), X("WBH", 0, 144))
+    sel(X("WBB", 0, 144), [[-16, 9], [-1001, 16]], 1, 15000, OP.is_gt, 1.0)
+    sel(X("WBB", 0, 144), [[-1, 144]], 1, 15, OP.is_ge, 0.0, True)
     tc(col(6), X("WTI", 0, 1))
-    ts(X("WBW", 0, 144), X("WBB", 0, 144), col(6), OP.mult)
-    ts(m128("IDB"), m128("NF"), pc, OP.is_equal)
-    ts(m128("NBLK"), m128("BLK"), -1, OP.mult)
-    ts(m128("IDN"), m128("IDB"), -1, OP.mult)
-    ts(m128("ID2"), m128("IDB"), 2, OP.mult)
-    tc(m128("IDH"), m128("IDB"))
-    ts(X("SEL", 0, 8), X("NF", 0, 8), pg, OP.is_equal, 16, OP.mult)
-    ts(col(5), pc, 0, OP.is_equal)
-    act(X("E0", 0, 256), X("NR", 0, 256), col(5), 0.0)
-    ts(m128("EJ"), X("NR", 0, 128), 0, OP.is_equal, col(5), OP.mult)
+    act(X("WBW", 0, 144), X("WBB", 0, 144), scale=col(6))
+    for name, v in (("IDB", 1.0), ("IDN", -1.0), ("ID2", 2.0)):
+        sel(m128(name), [[-1, 128]], 1, 0, OP.not_equal, v)
+    for out, pat, v in ((m128("NBLK"), [[16, 8], [0, 16]], -1.0), (X("SEL", 0, 8), [[16, 8]], 16.0)):
+        sel(out, pat, -1, 0, OP.is_gt, v)
+        sel(out, pat, -1, 15, OP.is_ge, 0.0, True)
+    sel(X("E0", 0, 256), [[0, 256]], 1, 0, OP.not_equal, 1.0)
+    sel(X("EJ", 0, 144), [[0, 9], [1, 16]], 1, 0, OP.not_equal, 1.0)
     for s in range(2):
         iota(X("OHT", 272 * s, 272 * s + 16), [[0, 16]], 0, 1)
     iota(X("RMB", 0, 1024), [[0, 64], [512, 16]], 0)
+    iota(X("CE", 0, 64), [[0, 64]], 0)
     tc(X("L15", 0, 16), n16)
     ln = X("LN", 0, 16)
     ts(ln, n16, 16, OP.mult, pr, OP.add)
@@ -266,20 +274,23 @@ def build():
     tt(X("QF", 16, 32), X("QF", 0, 16), ln, OP.add)
     for i, base in enumerate((-896, R2O)):
         lin("A", X("RBK", 16 * i, 16 * i + 16), X("QF", 16, 32), 128.0, float(base))
-    ts(X("TBIG", 0, 256), X("NR", 0, 256), pr, OP.is_le, 4096, OP.mult)
-    for i in range(2):
-        lin("A", X("DUF", 16 * i, 16 * i + 16), ln, 1.0, float(XD + 256 * i))
-        lin("A", X("DUF", 32 + 16 * i, 48 + 16 * i), ln, 1.0, float(XD + 256 * i + 2576))
+    sel(m128("TRI"), [[0, 8], [-1, 16]], 1, 0, OP.is_gt, 4096.0)
+    sel(X("TBIG", 0, 256), [[0, 16], [-1, 16]], 1, 0, OP.not_equal, 1.0)
+    iota(X("DUF", 0, 64), [[2576, 2], [256, 2], [16, 16]], 0, XD)
+    cur[0] = "du0"
+    act(X("DUF", 0, 64), X("DUF", 0, 64), pr, 1.0, "Silu")
+    P[-1]["cost"] += 1.3
+    cur[0] = ""
+    iota(X("PQ", 0, 64), [[0, 64]], 0)
+    pool(X("PQ", 65, 128, 2), X("DUF", 0, 32))
     dux = X("DUF", 0, 16)
 
-    iota(X("QT", 0, 192), [[0, 64], [1, 3]], 0)
-    ts(X("R3", 0, 192), X("QT", 0, 192), 0, OP.not_equal)
-    for i in range(2):
-        lin("A", X("CH", 48 * i, 48 * i + 48, 3), ln, 1.0, float(XD + 256 * i))
-        lin("A", X("CH", 96 + 48 * i, 144 + 48 * i, 3), ln, 1.0, float(MO + 256 * i))
-        for s in range(2):
-            lin("A", X("MD", 32 * i + 16 * s, 32 * i + 16 * s + 16), ln, 1.0, float(MO + 256 * i))
-        lin("A", X("MD", 64 + 16 * i, 80 + 16 * i), ln, 1.0, float(XD))
+    sel(X("R3", 0, 192), [[0, 64], [1, 3]], 0, 0, OP.is_equal, 1.0)
+    iota(X("CH", 0, 192, 3), [[MO - XD, 2], [256, 2], [16, 16]], 0, XD)
+    lin("A", X("CH", 0, 192, 3), X("CH", 0, 192, 3), 1.0, pr)
+    iota(X("MD", 0, 64), [[256, 2], [0, 2], [16, 16]], 0, MO)
+    iota(X("MD", 64, 96), [[0, 2], [16, 16]], 0, XD)
+    lin("A", X("MD", 0, 96), X("MD", 0, 96), 1.0, pr)
     ts(X("QI", 32, 48), ln, 977, OP.mult)
     ts(X("QI", 48, 64), X("QI", 32, 48), 2047, OP.bitwise_and)
     tc(X("L977", 0, 16), X("QI", 48, 64))
@@ -295,6 +306,11 @@ def build():
         ts(out, X("CS", lo + 2, hi, 3), *more)
 
     xwin, kwin, fwin, dwin = X("XW", X0, X0 + 2048), X("KD", 0, 2048), X("F", 0, XD), X("DP", 0, 2048)
+    for i in range(4):
+        pool(X("KD", 512 * i, 512 * i + 512), X("KI", 512 * i, 512 * i + 512))
+
+    def um(s, i, lo=0):
+        return X("SZ" if i else "SY", 4096 * s + 16 * lo + 15, 4096 * s + 4096, 16)
     for rnd in range(2):
         last = rnd == 1
         sm, relu = CFG["SM"][rnd], [(s, h) for s in range(2) for h in range(2) if CFG["RQ"][4 * rnd + 2 * s + h] == "A"]
@@ -316,14 +332,15 @@ def build():
         for s in range(2):
             lin(sm, X("C", 80 * s, 80 * s + 80, 5), X("DS", 64 + 16 * s, 80 + 16 * s), 1.0, col(8))
         for k in range(5):
-            ts(X("HF", 512 * k + 15, 512 * k + 512, 16), v, col(17 + k), OP.add, col(16), OP.max)
+            f = 512 * (k % 2 - k)
+            ts(X("HF", 512 * k + f + 15, 512 * k + f + 512, 16), v, col(17 + k), OP.add, col(16), OP.max)
             for s in range(2):
                 o = 512 * k + 256 * s
                 n = 16 // CFG["PARTS"][rnd]
                 for c in range(0, 16, n):
                     a, z, l = o + 16 * c, o + 16 * (c + n), 32 * k + 16 * s + c
                     gat(X("G", a, z), IND(fwin, X("LS", l, l + n)), CFG["C%d" % rnd][4 * k + 2 * s + c // 8])
-                    scan(X("SC", a, z), X("G", a, z), X("HF", a, z), OP.min, OP.add, 4096.0)
+                    scan(X("SC", a, z), X("G", a, z), X("HF", a + f, z + f), OP.min, OP.add, 4096.0)
                     if k < 4:
                         ts(X("LS", l + 32, l + 32 + n), X("SC", a + 15, z, 16), col(7), OP.add, 2048, OP.min)
                 ck = X("SC", o + 15, o + 256, 16)
@@ -340,11 +357,11 @@ def build():
             scan(X("SS", 80 * s, 80 * s + 80), eq, X("PC", 80 * s, 80 * s + 80), OP.mult, OP.add)
         top = X("SC", 2063, 2560, 16)
         for s in range(2):
-            tt(X("CE", 16 * s, 16 * s + 16), X("SC", 2063, 2304, 16), X("SC", 2319, 2560, 16), OP.is_equal)
-        tt(X("CE", 32, 64), X("SS", 4, 160, 5), top, OP.subtract)
-        tt(X("CE", 64, 96), X("CE", 32, 64), X("CE", 0, 32), OP.mult)
-        tt(X("CE", 96, 128), X("CE", 64, 96), top, OP.add)
-        ts(X("LA", 0, 32), X("CE", 96, 128), col(7), OP.add)
+            tt(X("CE", 32 * s + 1, 32 * s + 32, 2), X("SC", 2063, 2304, 16), X("SC", 2319, 2560, 16), OP.is_equal)
+        tt(X("CE", 64, 128, 2), X("SS", 4, 160, 5), top, OP.subtract)
+        gat(X("CE", 65, 128, 2), top)
+        scan(X("CE", 128, 192), X("CE", 0, 64), X("CE", 64, 128), OP.mult, OP.add)
+        ts(X("LA", 0, 32), X("CE", 129, 192, 2), col(7), OP.add)
         cur[0] = "vf"
         tc(X("AW", 0, 32), X("LA", 0, 32))
         tc(X("AWH", 0, 32), X("LA", 0, 32))
@@ -368,8 +385,8 @@ def build():
                 gat(X(out, lo, lo + 4096 // n), IND(xwin, X(lst, k, k + 256 // n)), qs[q])
                 cur[0] = "S" + mine
                 scan(X("S" + out, lo, lo + 4096 // n), X("RMB", 0, 4096 // n), X(out, lo, lo + 4096 // n), OP.min, OP.max)
-        for s in range(2):
-            tc(X("KL", 256 * s, 256 * s + 256), IND(kwin, la(s)))
+        for lo, hi in CFG["KLP"]:
+            tc(X("KL", 16 * lo, 16 * hi), IND(kwin, X("LA", lo, hi)))
         for s in range(2):
             gat(X("XS", 256 * s, 256 * s + 256), IND(xwin, la(s)))
             if (1 - s, 0) not in relu or (1 - s, 1) not in relu:
@@ -423,7 +440,7 @@ def build():
                     mm(X("b7", h, h + 128), X("OHT", e + h - 1, e + h + 127), m128("IDN"), False, h + 128 == n)
                 together(False)
                 tt(X("PL", o, o + n), X("b7", 0, n), X("KF", o, o + n), OP.mult)
-                wrap(X("b3", 0, n // 16), "WBH", X("PL", o, o + n))
+                wrap(X("b3", 0, n // 16), "WBB", X("PL", o, o + n))
                 tc(X("LL", l, l + n // 16), X("b3", 0, n // 16))
                 tc(X("ZK", o, o + n), IND(kwin, X("LL", l, l + n // 16)))
                 cur[0] = ""
@@ -440,9 +457,9 @@ def build():
         lin("V", X("FW", 0, 16), X("SC", 15, 256, 16), 1.0, col(7))
         cur[0] = "qd"
         together(True)
-        mm(X("b2", 0, 256), m128("IDB"), X("TBIG", 0, 256), True, False)
+        mm(X("b2", 0, 256), m128("TRI"), X("TBIG", 0, 256), True, False)
         for r in range(16):
-            mm(X("b2", r, 256, 16), m128("IDH"), X("FWH", 0, 16), False, r == 15)
+            mm(X("b2", r, 256, 16), m128("IDB"), X("FWH", 0, 16), False, r == 15)
         together(False)
         tt(X("EQD", 0, 256), X("FG", 0, 256), X("b2", 0, 256), OP.is_equal)
         cur[0] = "eq"
@@ -463,51 +480,85 @@ def build():
         aw, bw = X("AW", 0, 16), X("AW", 16, 32)
         ts(w(2), X("SC", 527, 768, 16), col(8), OP.is_equal)
         tt(w(3), aw, bw, OP.not_equal)
-        tt(w(5), w(3), X("CE", 0, 16), OP.mult)
+        tt(w(5), w(3), X("CE", 1, 32, 2), OP.mult)
         tt(w(6), w(2), w(5), OP.mult)
         tt(w(7), w(2), w(6), OP.subtract)
         ts(w(12, 2), X("LW", 0, 32), 2047, OP.not_equal)
         tt(w(14), w(12), w(13), OP.mult)
         for i in range(2):
             tt(w(8 + i), w(14), w(6), OP.mult)
-            lin(sm, w(26 + i), w(5), -90.0, 99.0)
+            if not (CFG["BOTH"][rnd] and last):
+                lin(sm, w(26 + i), w(5), -90.0, 99.0)
         tt(w(44, 2), X("LW", 0, 32), X("DUF", 0, 32), OP.subtract)
         tt(w(16, 2), w(44, 2), w(8, 2), OP.mult)
         tt(X("CH", 288, 384, 3), w(16, 2), X("DUF", 32, 64), OP.add)
         if not last:
             tt(w(46, 2), X("AW", 0, 32), X("DUF", 0, 32), OP.subtract)
             tt(w(18, 2), w(46, 2), w(8, 2), OP.mult)
-        for i in range(2):
-            tt(w(48 + 2 * i, 2), X("AW", 0, 32), X("MD", 32 * i, 32 * i + 32), OP.subtract)
-        tt(w(54, 2), X("AW", 0, 32), X("MD", 64, 96), OP.subtract)
-        for i in range(2):
-            tt(w(56 + i), w(54 + i), w(6), OP.mult)
-        tt(w(58), w(54), w(7), OP.mult)
-        tt(X("CH", 240, 288, 3), w(58), dux, OP.add)
+        both = CFG["BOTH"][rnd]
+        if both:
+            for i in range(2):
+                tt(w(48 + i), aw, X("MD", 32 * i, 32 * i + 16), OP.subtract)
+                tt(w(51 + i), w(48 + i), w(5), OP.mult)
+            tt(w(56, 2), w(51, 2), X("MD", 16, 48), OP.add)
+            ts(X("LT", 0, 32), w(56, 2), 0 if last else X0, OP.add)
+            tt(w(54, 2), X("AW", 0, 32), X("DUF", 0, 32), OP.subtract)
+            for s in range(2):
+                tt(X("PQ", 64 + 32 * s, 96 + 32 * s, 2), w(54 + s), w(2), OP.mult)
+            lin(sm, w(59), w(5), 10.0, -1.0)
+            lin(sm, w(60), w(5), -90.0, 99.0)
+        else:
+            for i in range(2):
+                tt(w(48 + 2 * i, 2), X("AW", 0, 32), X("MD", 32 * i, 32 * i + 32), OP.subtract)
+            tt(w(54, 2), X("AW", 0, 32), X("MD", 64, 96), OP.subtract)
+            for i in range(2):
+                tt(w(56 + i), w(54 + i), w(6), OP.mult)
+            tt(w(58), w(54), w(7), OP.mult)
+            tt(X("CH", 240, 288, 3), w(58), dux, OP.add)
         cur[0] = "su"
-        for i, src in enumerate(("SY", "SZ")):
-            wrap(X("b0", 0, 16), "WBW", X(src, 15, 4096), i == 0, i == 1, 16)
+        for i in range(2):
+            wrap(X("b0", 0, 16), "WBW", um(0, i), i == 0, i == 1)
         if not last:
             cur[0] = "sb"
-            wrap(X("bs", 0, 12), "WBW", X("SY", 4096 + 1039, 8192), True, False, 16)
-            mm(X("bs", 0, 12), m128("IDH"), X("L977", 4, 16), False, False)
-            wrap(X("bs", 0, 12), "WBW", X("SZ", 4096 + 1039, 8192), False, True, 16)
+            wrap(X("bs", 0, 12), "WBW", um(1, 0, 64), True, False)
+            mm(X("bs", 0, 12), m128("IDB"), X("L977", 4, 16), False, False)
+            wrap(X("bs", 0, 12), "WBW", um(1, 1, 64), False, True)
         cur[0] = "su"
-        for i, src in enumerate(("SY", "SZ")):
-            pool(X("XW", X0 + MO + 256 * i, X0 + MO + 256 * i + 256), X(src, 15, 4096, 16))
+        for i in range(2):
+            pool(X("XW", X0 + MO + 256 * i, X0 + MO + 256 * i + 256), um(0, i))
         cur[0] = "gl"
         for i in range(3):
-            mm(X("b4", 0, 256), m128("IDN" if i == 1 else "IDB"), X("SZ" if i == 2 else "SY", 4096 * (i % 2) + 15, 4096 * (i % 2) + 4096, 16), i == 0, i == 2)
-        tt(X("GL", 0, 256), X("b4", 0, 256), X("SZ", 4111, 8192, 16), OP.is_gt)
-        tt(X("GL", 256, 512), X("b4", 0, 256), X("SZ", 4111, 8192, 16), OP.is_lt)
+            mm(X("b4", 0, 256), m128("IDN" if i == 1 else "IDB"), um(i % 2, i // 2), i == 0, i == 2)
+        tt(X("GL", 0, 256), X("b4", 0, 256), um(1, 1), OP.is_gt)
+        tt(X("GL", 256, 512), X("b4", 0, 256), um(1, 1), OP.is_lt)
         wrap(X("b2", 0, 32), "WBB", X("GL", 0, 512))
         cur[0] = "su"
         tc(X("SI", 0, 16), X("b0", 0, 16))
         ts(X("SI", 32, 48), X("SI", 0, 16), 127, OP.bitwise_and)
         root = X("CH", 192, 240, 3)
         tt(root, X("SI", 32, 48), X("RBK", 16 * rnd, 16 * rnd + 16), OP.add)
-        for s in range(2):
-            tt(w(52 + s), X("LW", 16 * s, 16 * s + 16), root, OP.subtract)
+        twin = X("XW", X0, X0 + XEND) if last else X("XW", 0, X0 + R2O)
+        if both:
+            tt(w(50), X("LW", 0, 16), root, OP.subtract)
+            tt(w(53), w(50), w(5), OP.mult)
+            tt(w(58), w(53), root, OP.add)
+            ts(X("LT", 32, 48), w(58), 0 if last else X0, OP.add)
+            cur[0] = "xp"
+            for i in range(3):
+                gat(X("TG", 256 * i, 256 * i + 256), IND(twin, X("LT", 16 * i, 16 * i + 16)))
+            gat(X("TG", 768, 1024), IND(xwin, X("LL", 16, 32)))
+            for i in range(3):
+                mm(X("b3", 0, 256), m128("ID2" if i == 2 else "IDB"), X("TG", 256 * i, 256 * i + 256), i == 0, False)
+            mm(X("b3", 256, 512), m128("ID2"), X("XS", 256, 512), False, False)
+            mm(X("b3", 256, 512), m128("ID2"), X("TG", 768, 1024), False, True)
+            ts(X("VI", 0, 512), X("b3", 0, 512), 0.25, OP.mult, -0.375, OP.add)
+            cur[0] = "vd"
+            tt(X("PQ", 1, 64, 2), X("b2", 0, 32), w(59, 2), OP.is_ge)
+            scan(X("PQ", 128, 192), X("PQ", 0, 64), X("PQ", 64, 128), OP.mult, OP.add)
+            tc(X("LX", 0, 32), X("PQ", 129, 192, 2))
+        else:
+            for s in range(2):
+                tt(w(52 + s), X("LW", 16 * s, 16 * s + 16), root, OP.subtract)
         cur[0] = "vd"
         together(True)
         for i in range(2):
@@ -516,20 +567,21 @@ def build():
         together(False)
         scan(X("CS", 288, 384), X("R3", 0, 96), X("CH", 288, 384), OP.mult, OP.add)
         tc(X("LF", 0, 32), X("CS", 290, 384, 3))
-        tt(w(20, 2), X("b2", 0, 32), w(26, 2), OP.is_ge)
+        if not (both and last):
+            tt(w(20, 2), X("b2", 0, 32), w(26, 2), OP.is_ge)
         cur[0] = "fs"
-        put(X("F", 0, 5152), X("LF", 0, 32), X("VALF", 0, 512), CFG["PUT"][rnd])
+        put(X("F", 0, 5152), X("LF", 0, 32), X("VALF", 0, 512), CFG["PUT"][rnd], CFG["PQ"][rnd])
         cur[0] = "xw"
-        choose(X("LT", 0, 48), 2, [(w(48 + 2 * i), w(49 + 2 * i)) for i in range(3)], 0 if last else X0, OP.add)
-        choose(X("LX", 0, 16), 5, [(w(56), w(57))], 0, OP.add)
-        twin = X("XW", X0, X0 + XEND) if last else X("XW", 0, X0 + R2O)
-        for i in range(3):
-            gat(X("TG", 256 * i, 256 * i + 256), IND(twin, X("LT", 16 * i, 16 * i + 16)), CFG["TQ"][3 * rnd + i])
-        for i in range(3):
-            mm(X("b3", 0, 256), m128("ID2" if i == 2 else "IDB"), X("TG", 256 * i, 256 * i + 256), i == 0, i == 2)
-        ts(X("VI", 0, 256), X("b3", 0, 256), 0.25, OP.mult, -0.375, OP.add)
+        if not both:
+            choose(X("LT", 0, 48), 2, [(w(48 + 2 * i), w(49 + 2 * i)) for i in range(3)], 0 if last else X0, OP.add)
+            choose(X("LX", 0, 16), 5, [(w(56), w(57))], 0, OP.add)
+            for i in range(3):
+                gat(X("TG", 256 * i, 256 * i + 256), IND(twin, X("LT", 16 * i, 16 * i + 16)), CFG["TQ"][3 * rnd + i])
+            for i in range(3):
+                mm(X("b3", 0, 256), m128("ID2" if i == 2 else "IDB"), X("TG", 256 * i, 256 * i + 256), i == 0, i == 2)
+            ts(X("VI", 0, 256), X("b3", 0, 256), 0.25, OP.mult, -0.375, OP.add)
         add("W", "waitsent", X("XW", X0, X0 + 128), [], (rnd + 1,), 0)
-        put(X("XW", X0, X0 + MO), X("LX", 0, 16), X("VI", 0, 256), CFG["PUT"][2 + rnd])
+        put(X("XW", X0, X0 + MO + 256 * both), X("LX", 0, 16 + 16 * both), X("VI", 0, 256 + 256 * both), CFG["PUT"][2 + rnd])
         if last:
             dma("S", ("d", "yf"), X("F", 0, 2048), "d7")
             for i in range(2):
@@ -584,12 +636,12 @@ def build():
         for s in range(2):
             tt(X("TK", 256 * s, 256 * s + 256), X("b1", 0, 256), X("OHS", 256 * s, 256 * s + 256), OP.mult)
         together(True)
-        mm(X("b4", 0, 512), m128("IDH"), X("KF", 0, 512), True, False)
-        mm(X("b4", 0, 512), m128("IDH"), X("TK", 0, 512), False, True)
+        mm(X("b4", 0, 512), m128("IDB"), X("KF", 0, 512), True, False)
+        mm(X("b4", 0, 512), m128("IDB"), X("TK", 0, 512), False, True)
         together(False)
         act(X("NK", 0, 512), X("b4", 0, 512))
         choose(X("LF", 32, 64), 0, [(w(18), w(18)), (w(19), w(19))], 0, OP.add)
-        put(X("KD", 0, 2576), X("LF", 32, 64), X("NK", 0, 512), CFG["PUT"][4])
+        put(X("KD", 0, 2576), X("LF", 32, 64), X("NK", 0, 512), CFG["PUT"][4], CFG["PQ"][2])
     return P
 
 
@@ -707,26 +759,17 @@ def order(P, preds):
         assert len(seq) == n
         return max(e for _, e in t), t, seq, queue, pre, bank
     succ = turn(preds)
-    prio = [0.0] * n
-    for i in range(n - 1, -1, -1):
-        prio[i] = P[i]["cost"] + late[i] + max([prio[k] + wake(i, k, h) for k, h in succ[i].items()] + [0.0])
-    best = None
-    for _ in range(CFG["SWEEPS"]):
-        got = sweep(preds, [prio[i] + CFG["BOOST"].get(P[i]["b"], 0.0) for i in range(n)], None)
-        if best is None or got[0] < best[0]:
-            best = got
-        prio = [e for _, e in sweep(succ, [e for _, e in got[1]], got[3])[1]]
-    tau, seen = [s for s, _ in best[1]], {}
-    known = {r: min(tau[i] for i in range(n) if P[i]["b"] == "kl" + r) for r in "01"}
+    tau, seen = [CFG["KNOWN"][2]] * n, {}
     for i, p in enumerate(P):
-        if p["b"][:-1] in CFG["PLAN"]:
-            a, d = CFG["PLAN"][p["b"][:-1]]
-            seen[p["b"]] = seen.get(p["b"], -1) + (p["g"] == i and p["q"] != "T")
-            tau[i] = known[p["b"][-1]] + a + d * seen[p["b"]]
-    got = sweep(preds, [-s for s in tau], None)
-    if CFG["PLAN"]:
-        best = got
-    seq, queue = best[2:4]
+        a, d = CFG["PLAN"].get(p["b"], CFG["PLAN"].get(p["b"][:-1], (None, None)))
+        if a is not None:
+            seen[p["b"]] = seen.get(p["b"], -1) + (p["g"] == i)
+            tau[i] = CFG["KNOWN"][int(p["b"][-1])] + a + d * seen[p["b"]]
+    for i in range(n - 1, -1, -1):
+        tau[i] = min([tau[i] - late[i]] + [tau[k] - wake(i, k, h) - P[i]["cost"] - late[i] for k, h in succ[i].items()])
+    for m in units.values():
+        tau[m[0]] = min(tau[i] for i in m)
+    seq, queue = sweep(preds, [-s for s in tau], None)[2:4]
     ids = [P[i]["g"] for i in seq if P[i]["g"] == i]
     at = {u: k for k, u in enumerate(ids)}
     m = len(ids)
@@ -756,7 +799,7 @@ def order(P, preds):
 
     touch = [sorted({v for i in units[u] for v in P[i]["use"]}) for u in ids]
     users = {v: len({P[i]["g"] for i in uses[v]}) for v in uses}
-    either = [P[u]["what"] in ("gat", "lin") for u in ids]
+    either = [P[u]["what"] in ("gat", "lin", "put") for u in ids]
 
     def times(row, lo, old):
         lo -= lo % 24
@@ -801,7 +844,7 @@ def order(P, preds):
             chain.append(k)
             k = by[k]
         return end + CFG["PULL"] * sum([st[z] for z in row[span[0]:span[1]]]) / (span[1] - span[0]), (st, by, marks), chain, bank
-    row, place, span, y = list(range(m)), list(range(m)), [0, m, None], 1
+    row, place, span, y = list(range(m)), list(range(m)), [0, m, None], CFG["SEED"]
     blank = ([0.0] * m, [None] * m, [([0.0] * 7, [None] * 7, [(0.0, b, None) for b in range(8)], {}, users, {})])
     stops = [min(k for k, u in enumerate(ids) if P[u]["b"] == b and P[u]["q"] in "AV") for b in ("ya0", "gl0", "ya1", "gl1")]
     for a, z, steps in CFG["REPAIR"]:
@@ -892,7 +935,7 @@ def rank_program(g, core, T, topo):
         return
     P, seq, queue, preds = plan()
     eng = {"V": g.vector, "A": g.scalar, "T": g.tensor, "G": g, "S": g.sync}
-    funcs = {None: AF.Identity, "Relu": AF.Relu, "Abs": AF.Abs, "Sign": AF.Sign}
+    funcs = {None: AF.Identity, "Relu": AF.Relu, "Abs": AF.Abs, "Sign": AF.Sign, "Silu": AF.Silu}
     cores = list(T.cores)
     n = len(cores)
 
@@ -905,7 +948,7 @@ def rank_program(g, core, T, topo):
             if a[1][:2] == "yx":
                 i = int(a[1][2:])
                 return T.yx[:, 1024 * i:1024 * i + 1024]
-            return T[a[1]][:]
+            return T[a[1]][:, a[2]:a[3]] if len(a) > 2 else T[a[1]][:]
         _, name, lo, hi, st, p0, p1 = a
         return T[name][p0:p1, lo:hi] if st == 1 else T[name][p0:p1, lo:hi:st]
 
@@ -963,8 +1006,10 @@ def rank_program(g, core, T, topo):
             done[i] = [("sent%d" % args[0], ND)]
             total["sent%d" % args[0]] = ND
             continue
-        if what == "tc" or (what == "gat" and q == "V"):
+        if what == "tc" or (what in ("gat", "put") and q == "V"):
             h = e.tensor_copy(out, ins[0])
+        elif what == "put":
+            h = e.activation(out, ins[0], AF.Silu)
         elif what == "gat":
             h = e.activation(out, ins[0], AF.Copy)
         elif what == "count":
@@ -979,6 +1024,8 @@ def rank_program(g, core, T, topo):
             bias, scale, func = args
             if bias is None and scale == 1.0 and func is None:
                 h = e.activation(out, ins[0], AF.Copy)
+            elif bias is None and scale == 1.0:
+                h = e.activation(out, ins[0], funcs[func])
             else:
                 h = e.activation(out, ins[0], funcs[func], bias=0.0 if bias is None else sc(bias), scale=sc(scale))
         elif what == "tt":

from concourse.bass import DstId, RemoteDMATransfer
from concourse.mybir import AluOpType as OP, ActivationFunctionType as AF

X0, XA, XD, MO, R2O = 896, 2048, 2064, 2320, 2832
XEND = R2O + 896
ND = 4
MARK = (0.25, 0.375)

SCRATCH = {}
for _n, _w, _d in (
        ("XW", X0 + XEND, "bfloat16"), ("KD", 2576, "float32"), ("KI", 2048, "int32"), ("F", 5152, "float32"), ("DP", 2048, "bfloat16"),
        ("ZK", 512, "uint16"), ("Z", 8192, "bfloat16"), ("SZ", 8192, "bfloat16"), ("SY", 8192, "bfloat16"), ("RMB", 1024, "bfloat16"),
        ("FAI", 128, "int32"), ("DPI", 128, "int32"), ("PAI", 16, "int32"), ("PBI", 16, "int32"), ("WTI", 1, "int32"), ("FDH", 256, "float16"),
        ("PI", 1, "int32"), ("TI", 3, "int32"), ("COL", 32, "float32"), ("NF", 128, "float32"), ("NR", 272, "float32"), ("NG", 256, "float32"),
        ("BLK", 128, "float16"), ("NBLK", 128, "bfloat16"), ("ZB", 256, "bfloat16"), ("WBB", 144, "bfloat16"), ("WBW", 144, "bfloat16"),
        ("IDB", 128, "bfloat16"), ("IDN", 128, "bfloat16"), ("ID2", 128, "bfloat16"), ("TRI", 128, "bfloat16"), ("BSEL", 2048, "float16"), ("DELR", 16, "float32"),
        ("RMH", 256, "bfloat16"), ("SEL", 8, "bfloat16"), ("KC", 256, "bfloat16"), ("E0", 256, "bfloat16"),
        ("L15", 16, "uint16"), ("LN", 16, "float32"), ("L977", 16, "float16"), ("QI", 64, "int32"), ("R3", 192, "bfloat16"), ("CH", 528, "float32"), ("CS", 528, "float32"), ("MD", 96, "float32"), ("CE", 192, "float32"), ("QF", 32, "float32"), ("TBIG", 256, "bfloat16"), ("DUF", 64, "float32"),
        ("RBK", 32, "float32"), ("EQ", 1920, "float16"),
        ("PX", 64, "float32"), ("PT", 64, "float32"), ("PU", 32, "float32"),
        ("G", 3072, "float32"), ("SC", 3072, "float32"), ("LS", 160, "uint16"), ("LU", 32, "uint16"), ("LSI", 32, "int32"), ("HM", 800, "bfloat16"), ("DS", 96, "float32"), ("PM", 32, "float32"),
        ("HK", 160, "float32"), ("C", 192, "float32"), ("E6", 112, "float32"), ("N6", 112, "float32"), ("PC", 288, "float32"), ("SS", 288, "float32"),
        ("AW", 32, "float32"), ("AWH", 32, "float16"), ("LA", 32, "uint16"), ("VALF", 512, "float32"),
        ("KL", 512, "uint16"), ("KF", 512, "float16"), ("XS", 512, "bfloat16"), ("Y", 8192, "bfloat16"), ("MM", 8192, "bfloat16"),
        ("EJ", 144, "bfloat16"), ("PS", 512, "float32"), ("OHT", 544, "bfloat16"), ("OHS", 512, "bfloat16"), ("PL", 512, "float16"), ("LL", 32, "uint16"), ("LW", 32, "float32"),
        ("HF", 1024, "float32"), ("FG", 256, "float16"), ("FWH", 16, "float16"), ("FW", 16, "float32"),
        ("EQD", 256, "float16"), ("GL", 512, "bfloat16"), ("W", 1152, "float32"), ("SI", 64, "int32"), ("KDS", 128, "float32"), ("KN", 48, "float32"),
        ("LT", 48, "uint16"), ("LX", 32, "uint16"), ("LF", 64, "uint16"), ("TG", 1024, "bfloat16"), ("VI", 512, "int32"), ("PQ", 192, "float32"), ("TK", 512, "float16"), ("NK", 512, "float32")):
    SCRATCH[_n] = ("sbuf", [128, _w], _d)
for _b in range(8):
    SCRATCH["b%d" % _b] = ("psum", [128, 512], "float32")
SEMAPHORES = ["qV", "qA", "qT", "qG", "sent1", "sent2", "arr1", "arr2"] + ["d%d" % _i for _i in range(11)]

CFG = dict(
    HALVES=[2, 2, 2, 2],
    PLAN=dict(kl=(0, 0.1), ya=(0.6, 1.0), kf=(2.2, 0), ma=(2.4, 0.3), la=(2.0, 0.1), yb=(4.9, 1.4), mb=(7.9, 0.3), lb=(7.0, 0.1), za=(10.6, 1.4), zb=(16.3, 0.7),
              Sya=(12, 0.5), Syb=(14, 0.5), Sza=(14.5, 0.5), Szb=(17, 0.7), eq=(13, 0.1), qd=(13.5, 0), vf=(14, 0), pre=(16, 0.05), np=(16.5, 0.05), su=(17, 0.1), sb=(17.5, 0), gl=(17.2, 0), xp=(21, 0.3), du0=(-14, 0)),
    Y00="AVAA", Y01="AAAA", Y10="AVAA", Y11="AAAA", Z00="AAAA", Z01="AAAAAAAA", Z10="AAAA", Z11="AAAAAAAA",
    RQ="VVVVVVVV",
    CQ="VAA", C0="A" * 20, C1="A" * 20, PARTS=[2, 2], FQ="AVAVAVAV", TQ="AAAAAA", SM="AA",
    PUT=[1, 1, 1, 1, 2], KLP=[(0, 4), (4, 16), (16, 32)], BOTH=[0, 1], PQ="AAA", KNOWN=(13.5, 47, 76), SEED=1,
    SLACK={'T': 0.6, 'V': 0.6, 'A': 0.6}, MARGIN=0.0, KEEP=1, LAP=30, MU=2, FAR=16, CHAIN=100, PULL=0.03, WORSE=0.08,
    REPAIR=[(0, 0, 30000), (1, 2, 110000), (3, 4, 90000)])
CY, GA, SCA, WS, WK, BW = 0.00087, 0.00133, 0.003, 0.2, 0.2, 400e3


def X(name, lo, hi, st=1, p0=0, p1=128):
    return ("x", name, lo, hi, st, p0, p1)


def IND(win, off):
    return ("i", win, off)


def width(a):
    if a[0] == "i":
        return 16 * (a[2][3] - a[2][2])
    return (a[3] - a[2] + a[4] - 1) // a[4]


def spans(a):
    return [a[1], a[2]] if a[0] == "i" else [a]


def gcd(a, b):
    while b:
        a, b = b, a % b
    return a


def clash(a, b):
    if a[2] >= b[3] or b[2] >= a[3] or a[5] >= b[6] or b[5] >= a[6]:
        return False
    return (a[2] - b[2]) % gcd(a[4], b[4]) == 0


def two(a):
    return a[0] == "x" and a[1][0] != "b" and SCRATCH[a[1]][2] in ("bfloat16", "float16", "uint16")


def psum(a):
    return a[0] == "x" and a[1][0] == "b"


def build():
    P = []
    cur = ["", ""]
    now, nuse, unit = {}, [0], [None]

    def content(a, fresh=False):
        if not (isinstance(a, tuple) and a and psum(a)):
            return a
        if fresh and now.get(a[1], (0, True))[1]:
            nuse[0] += 1
            now[a[1]] = (nuse[0], False)
        return ("x", "b%d" % now[a[1]][0]) + a[2:]

    def add(qs, what, out, ins, args, cost):
        for a in ins:
            if psum(a):
                now[a[1]] = (now[a[1]][0], True)
        out, ins, args = content(out, what == "mm" and args[0]), [content(a) for a in ins], tuple(content(a) for a in args)
        use = sorted({int(a[1][1:]) for a in [out] + ins if a and psum(a)})
        P.append(dict(b=cur[0] + cur[1], g=len(P) if unit[0] is None else unit[0], use=use, q=qs, what=what, out=out, ins=ins, args=args, cost=cost,
                      w=(spans(out) if out else []) + (list(args) if what == "count" else []), r=[s for i in ins for s in spans(i)]))

    def together(on):
        unit[0] = len(P) if on else None

    def ccost(out, ins, fast):
        n = width(out)
        if out[0] == "i":
            return 0.05 + n * SCA
        if ins[0][0] == "i":
            return 0.05 + n * GA
        return max(64, n * (0.5 if fast and two(out) and all(two(i) for i in ins) else 1)) * CY

    def tc(out, a, q="V"):
        add(q, "tc", out, [a], (), ccost(out, [a], True))

    def tt(out, a, b, op):
        n = width(b)
        c = ccost(out, [a], False) if "i" in (a[0], out[0]) else max(64, n * (1 if psum(a) or psum(b) else 2)) * CY
        add("V", "tt", out, [a, b], (op,), c)

    def ts(out, a, s1, o1, s2=None, o2=None):
        ins = [a] + [s for s in (s1, s2) if isinstance(s, tuple)]
        add("V", "ts", out, ins, (s1, o1, s2, o2), ccost(out, [a], True))

    def scan(out, d0, d1, o0, o1, init=0.0):
        add("V", "scan", out, [d0, d1] + ([init] if isinstance(init, tuple) else []), (o0, o1, init), ccost(out, [d0, d1], True))

    def act(out, a, bias=None, scale=1.0, func=None):
        c = 0.065 + width(out) * GA if a[0] == "i" else 0.065 + width(out) * SCA if out[0] == "i" else max(64, width(out)) * CY
        add("A", "act", out, [a] + [s for s in (bias, scale) if isinstance(s, tuple)], (bias, scale, func), c)

    def lin(q, out, a, scale, bias, cut=False):
        add(q, "lin", out, [a] + ([bias] if isinstance(bias, tuple) else []), (bias, scale, "Relu" if cut else None), max(64, width(out)) * CY)

    def gat(out, a, q="A"):
        add(q, "gat", out, [a], (), 0.06 + width(out) * GA if a[0] == "i" else max(64, width(out)) * CY)

    def pool(out, a):
        add("G", "sel", out, [a], ([[0, width(out)]], 0, 1, OP.is_gt, 0.0), 0.17 + 2 * width(out) * CY)

    def sel(out, pat, cm, base, cmp, fill, same=False):
        add("G", "sel", out, [out if same else X("ZB", 0, width(out))], (pat, cm, base, cmp, fill), 0.17 + 2 * width(out) * CY)

    def put(win, lst, src, n, q=None):
        k = width(lst) // n
        for i in range(n):
            out, a = IND(win, X(lst[1], lst[2] + k * i, lst[2] + k * i + k)), X(src[1], src[2] + 16 * k * i, src[2] + 16 * k * (i + 1))
            if q:
                add(q, "put", out, [a], (), 0.06 + 16 * k * SCA)
            else:
                tc(out, a)


    def mm(out, l, r, start, stop):
        add("T", "mm", out, [l, r], (start, stop), max(64, width(r)) * CY)

    def wrap(out, sel, src, start=True, stop=True):
        together(True)
        for r in range(16):
            mm(out, X(sel, 15 - r, 143 - r), X(src[1], src[2] + r * src[4], src[3], 16 * src[4]), start and r == 0, stop and r == 15)
        together(False)

    def dma(q, out, a, sem):
        s = out if out[0] == "x" else a
        add(q, "dma", out, [a], (sem, width(s) * (2 if two(s) else 4) * (8 if out[1] == "yf" else 128) / BW), 0.06)

    def iota(out, pat, cm, base=0):
        add("G", "iota", out, [], (pat, cm, base), 0.13 + 2 * width(out) * CY)

    def ms(out, v):
        add("V", "ms", out, [], (v,), max(64, width(out) * (0.5 if two(out) else 1)) * CY)

    def col(i):
        return X("COL", i, i + 1)

    def m128(n):
        return X(n, 0, 128)

    def w(i, n=1):
        return X("W", 16 * i, 16 * (i + n))

    together(True)
    dma("A", X("FAI", 0, 128), ("d", "fa"), "d0")
    dma("A", X("PBI", 0, 16), ("d", "pb"), "d3")
    together(True)
    dma("S", X("DPI", 0, 128), ("d", "dp"), "d1")
    dma("S", X("PAI", 0, 16), ("d", "pa"), "d2")
    dma("S", X("WTI", 0, 1), ("d", "wt"), "d4")
    for i in range(2):
        dma("S", X("KI", 1024 * i, 1024 * i + 1024), ("d", "kd", 1024 * i, 1024 * i + 1024), ("d5", "d10")[i])
    dma("S", X("XW", X0, X0 + 2048), ("d", "xs"), "d6")
    together(False)
    add("G", "send", None, [X("XW", X0, X0 + 128)], (1,), 1.0)
    add("N", "arrive", X("XW", 0, 896), [], (1,), 0)

    iota(X("PI", 0, 1), [[0, 1]], 1)
    iota(m128("NG"), [[1, 8], [0, 16]], 0)
    iota(m128("NF"), [[1, 128]], 0)
    iota(X("NR", 0, 272), [[0, 17], [1, 16]], 0)
    iota(X("XW", X0 + XA, X0 + MO), [[0, MO - XA]], 0)
    iota(X("F", XA, XD), [[0, XD - XA]], 0)
    iota(X("ZB", 0, 256), [[0, 256]], 0)
    iota(X("KC", 0, 256), [[0, 16], [-1, 16]], 0, 15)
    ts(X("TI", 0, 1), X("PI", 0, 1), 15, OP.bitwise_and)
    ts(X("TI", 1, 2), X("PI", 0, 1), 4, OP.arith_shift_right)
    ts(X("TI", 2, 3), X("TI", 1, 2), 1, OP.bitwise_and)
    tc(X("COL", 0, 2), X("TI", 0, 2))
    tc(col(3), X("TI", 2, 3))
    ts(col(4), col(3), -1, OP.mult, 1, OP.add)
    pr, pg = col(0), col(1)
    n16 = X("NF", 0, 16)
    ts(m128("BLK"), m128("NG"), pg, OP.is_equal)
    ts(X("DELR", 0, 16), n16, pr, OP.is_equal)
    together(True)
    for r in range(16):
        ts(X("BSEL", 128 * r, 128 * r + 128), m128("BLK"), X("DELR", r, r + 1), OP.mult)
    together(False)
    tc(X("FDH", 0, 128), m128("DPI"))
    tc(X("FDH", 128, 256), m128("FAI"))
    for k in range(2):
        for i in range(4):
            together(True)
            for r in range(4 * i, 4 * i + 4):
                mm(X("b0", 128 * (r % 4), 128 * (r % 4) + 128), X("BSEL", 128 * r, 128 * r + 128), X("FDH", 128 * k, 128 * k + 128), True, True)
            together(False)
            gat(X("F" if k else "DP", 512 * i, 512 * i + 512), X("b0", 0, 512), CFG["FQ"][4 * k + i])
    for s in range(2):
        src = X("PBI" if s else "PAI", 0, 16)
        ts(X("PX", 32 * s, 32 * s + 16), src, col(4), OP.mult)
        ts(X("PX", 32 * s + 16, 32 * s + 32), src, col(3), OP.mult)
    add("V", "tr", X("PT", 0, 64), [X("PX", 0, 64)], (), 0.07)
    for s in range(2):
        tt(X("PU", 16 * s, 16 * s + 16), X("PT", 32 * s, 32 * s + 16), X("PT", 32 * s + 16, 32 * s + 32), OP.add)
    sel(X("RMH", 0, 256), [[0, 16], [1, 16]], 0, 0, OP.is_equal, 1.0)
    ts(X("HM", 256, 528), X("NR", 0, 272), pr, OP.is_equal, -4096, OP.mult)
    ts(X("HM", 544, 800), X("HM", 257, 513), -2, OP.mult)
    tt(X("HM", 0, 256), X("HM", 256, 512), X("HM", 544, 800), OP.add)
    ts(col(9), pr, 0, OP.is_equal, 8192, OP.mult)
    ts(col(8), col(9), -4096, OP.add)
    ts(col(7), col(8), -1, OP.mult)
    tc(col(16), X("HM", 15, 16))
    ts(X("COL", 17, 22), X("NF", 1, 6), -4096, OP.mult, col(16), OP.add)
    for i in range(4):
        gat(X("HF", 256 * i, 256 * i + 256), X("HM", 0, 256))

    def hold(out, src):
        scan(out, src, X("HM", 0, width(out)), OP.min, OP.add, 4096.0)
    sel(X("WBB", 0, 144), [[-16, 9], [-1001, 16]], 1, 15000, OP.is_gt, 1.0)
    sel(X("WBB", 0, 144), [[-1, 144]], 1, 15, OP.is_ge, 0.0, True)
    tc(col(6), X("WTI", 0, 1))
    act(X("WBW", 0, 144), X("WBB", 0, 144), scale=col(6))
    for name, v in (("IDB", 1.0), ("IDN", -1.0), ("ID2", 2.0)):
        sel(m128(name), [[-1, 128]], 1, 0, OP.not_equal, v)
    for out, pat, v in ((m128("NBLK"), [[16, 8], [0, 16]], -1.0), (X("SEL", 0, 8), [[16, 8]], 16.0)):
        sel(out, pat, -1, 0, OP.is_gt, v)
        sel(out, pat, -1, 15, OP.is_ge, 0.0, True)
    sel(X("E0", 0, 256), [[0, 256]], 1, 0, OP.not_equal, 1.0)
    sel(X("EJ", 0, 144), [[0, 9], [1, 16]], 1, 0, OP.not_equal, 1.0)
    for s in range(2):
        iota(X("OHT", 272 * s, 272 * s + 16), [[0, 16]], 0, 1)
    iota(X("RMB", 0, 1024), [[0, 64], [512, 16]], 0)
    iota(X("CE", 0, 64), [[0, 64]], 0)
    tc(X("L15", 0, 16), n16)
    ln = X("LN", 0, 16)
    ts(ln, n16, 16, OP.mult, pr, OP.add)
    ts(X("QI", 0, 16), ln, 9363, OP.mult)
    ts(X("QI", 16, 32), X("QI", 0, 16), 16, OP.arith_shift_right)
    ts(X("QF", 0, 16), X("QI", 16, 32), -7, OP.mult)
    tt(X("QF", 16, 32), X("QF", 0, 16), ln, OP.add)
    for i, base in enumerate((-896, R2O)):
        lin("A", X("RBK", 16 * i, 16 * i + 16), X("QF", 16, 32), 128.0, float(base))
    sel(m128("TRI"), [[0, 8], [-1, 16]], 1, 0, OP.is_gt, 4096.0)
    sel(X("TBIG", 0, 256), [[0, 16], [-1, 16]], 1, 0, OP.not_equal, 1.0)
    iota(X("DUF", 0, 64), [[2576, 2], [256, 2], [16, 16]], 0, XD)
    cur[0] = "du0"
    act(X("DUF", 0, 64), X("DUF", 0, 64), pr, 1.0, "Silu")
    P[-1]["cost"] += 1.3
    cur[0] = ""
    iota(X("PQ", 0, 64), [[0, 64]], 0)
    pool(X("PQ", 65, 128, 2), X("DUF", 0, 32))
    dux = X("DUF", 0, 16)

    sel(X("R3", 0, 192), [[0, 64], [1, 3]], 0, 0, OP.is_equal, 1.0)
    iota(X("CH", 0, 192, 3), [[MO - XD, 2], [256, 2], [16, 16]], 0, XD)
    lin("A", X("CH", 0, 192, 3), X("CH", 0, 192, 3), 1.0, pr)
    iota(X("MD", 0, 64), [[256, 2], [0, 2], [16, 16]], 0, MO)
    iota(X("MD", 64, 96), [[0, 2], [16, 16]], 0, XD)
    lin("A", X("MD", 0, 96), X("MD", 0, 96), 1.0, pr)
    ts(X("QI", 32, 48), ln, 977, OP.mult)
    ts(X("QI", 48, 64), X("QI", 32, 48), 2047, OP.bitwise_and)
    tc(X("L977", 0, 16), X("QI", 48, 64))

    def choose(out, first, changes, *more):
        together(True)
        for i, d in enumerate(changes):
            for s in range(2):
                tt(X("CH", 48 * (first + i) + 1 + s, 48 * (first + i + 1), 3), w(20 + s), d[s], OP.mult)
        together(False)
        lo, hi = 48 * first, 48 * (first + len(changes))
        scan(X("CS", lo, hi), X("R3", 0, hi - lo), X("CH", lo, hi), OP.mult, OP.add)
        ts(out, X("CS", lo + 2, hi, 3), *more)

    xwin, kwin, fwin, dwin = X("XW", X0, X0 + 2048), X("KD", 0, 2048), X("F", 0, XD), X("DP", 0, 2048)
    for i in range(4):
        pool(X("KD", 512 * i, 512 * i + 512), X("KI", 512 * i, 512 * i + 512))

    def um(s, i, lo=0):
        return X("SZ" if i else "SY", 4096 * s + 16 * lo + 15, 4096 * s + 4096, 16)
    for rnd in range(2):
        last = rnd == 1
        sm, relu = CFG["SM"][rnd], [(s, h) for s in range(2) for h in range(2) if CFG["RQ"][4 * rnd + 2 * s + h] == "A"]
        cur[0], cur[1] = "cl", str(rnd)
        if not last:
            tc(X("LU", 0, 32), X("PU", 0, 32))
            for s in range(2):
                lin(sm, X("PM", 16 * s, 16 * s + 16), X("PU", 16 * s, 16 * s + 16), 1.0, MARK[s])
                for h in range(2):
                    o = 2560 + 256 * s + 128 * h
                    gat(X("G", o, o + 128), IND(dwin, X("LU", 16 * s + 8 * h, 16 * s + 8 * h + 8)), CFG["CQ"][s])
                    hold(X("SC", o, o + 128), X("G", o, o + 128))
            tt(X("DS", 16, 32), X("SC", 2575, 2816, 16), X("SC", 2831, 3072, 16), OP.subtract)
        for s in range(2):
            lin("V", X("DS", 32 + 16 * s, 48 + 16 * s), X("DS", 16, 32), 4096.0 if s else -4096.0, 0.0, True)
        v = X("DS", 64, 96)
        tt(v, X("DS", 32, 64), X("PM", 0, 32), OP.add)
        ts(X("LS", 0, 32), v, 2048, OP.min)
        for s in range(2):
            lin(sm, X("C", 80 * s, 80 * s + 80, 5), X("DS", 64 + 16 * s, 80 + 16 * s), 1.0, col(8))
        for k in range(5):
            f = 512 * (k % 2 - k)
            ts(X("HF", 512 * k + f + 15, 512 * k + f + 512, 16), v, col(17 + k), OP.add, col(16), OP.max)
            for s in range(2):
                o = 512 * k + 256 * s
                n = 16 // CFG["PARTS"][rnd]
                for c in range(0, 16, n):
                    a, z, l = o + 16 * c, o + 16 * (c + n), 32 * k + 16 * s + c
                    gat(X("G", a, z), IND(fwin, X("LS", l, l + n)), CFG["C%d" % rnd][4 * k + 2 * s + c // 8])
                    scan(X("SC", a, z), X("G", a, z), X("HF", a + f, z + f), OP.min, OP.add, 4096.0)
                    if k < 4:
                        ts(X("LS", l + 32, l + 32 + n), X("SC", a + 15, z, 16), col(7), OP.add, 2048, OP.min)
                ck = X("SC", o + 15, o + 256, 16)
                if k < 4:
                    if k < 3:
                        pool(X("C", 80 * s + k + 1, 80 * s + 80, 5), ck)
                    else:
                        gat(X("C", 80 * s + k + 1, 80 * s + 80, 5), ck, "V")
        eq, ne = X("E6", 16, 96), X("N6", 16, 96)
        tt(eq, X("C", 0, 80), X("C", 80, 160), OP.is_equal)
        tt(ne, X("C", 0, 80), X("C", 80, 160), OP.not_equal)
        for s in range(2):
            tt(X("PC", 80 * s, 80 * s + 80), ne, X("C", 80 * s, 80 * s + 80), OP.mult)
            scan(X("SS", 80 * s, 80 * s + 80), eq, X("PC", 80 * s, 80 * s + 80), OP.mult, OP.add)
        top = X("SC", 2063, 2560, 16)
        for s in range(2):
            tt(X("CE", 32 * s + 1, 32 * s + 32, 2), X("SC", 2063, 2304, 16), X("SC", 2319, 2560, 16), OP.is_equal)
        tt(X("CE", 64, 128, 2), X("SS", 4, 160, 5), top, OP.subtract)
        gat(X("CE", 65, 128, 2), top)
        scan(X("CE", 128, 192), X("CE", 0, 64), X("CE", 64, 128), OP.mult, OP.add)
        ts(X("LA", 0, 32), X("CE", 129, 192, 2), col(7), OP.add)
        cur[0] = "vf"
        tc(X("AW", 0, 32), X("LA", 0, 32))
        tc(X("AWH", 0, 32), X("LA", 0, 32))
        together(True)
        for r in range(16):
            mm(X("b3", r, 512, 16), X("BSEL", 128 * r, 128 * r + 128), X("AWH", 0, 32), True, True)
        together(False)
        act(X("VALF", 256, 512), X("b3", 0, 256))
        act(X("VALF", 0, 256), X("b3", 256, 512))

        cur[0] = "kl"

        def la(s):
            return X("LA", 16 * s, 16 * s + 16)

        def kids(out, lst, s, qs):
            n, mine = len(qs), cur[0]
            for q in range(n):
                lo, k = 4096 * s + 4096 // n * q, 256 * s + 256 // n * q
                cur[0] = mine
                gat(X(out, lo, lo + 4096 // n), IND(xwin, X(lst, k, k + 256 // n)), qs[q])
                cur[0] = "S" + mine
                scan(X("S" + out, lo, lo + 4096 // n), X("RMB", 0, 4096 // n), X(out, lo, lo + 4096 // n), OP.min, OP.max)
        for lo, hi in CFG["KLP"]:
            tc(X("KL", 16 * lo, 16 * hi), IND(kwin, X("LA", lo, hi)))
        for s in range(2):
            gat(X("XS", 256 * s, 256 * s + 256), IND(xwin, la(s)))
            if (1 - s, 0) not in relu or (1 - s, 1) not in relu:
                mm(X("bx%d" % (1 - s), 0, 256), m128("IDB"), X("XS", 256 * s, 256 * s + 256), True, True)
        for s in range(2):
            cur[0] = "yb" if s else "ya"
            kids("Y", "KL", s, CFG["Y%d%d" % (rnd, s)])
        cur[0] = "kf"
        for s in range(2):
            tc(X("KF", 256 * s, 256 * s + 256), X("KL", 256 * s, 256 * s + 256))
        for s in range(2):
            cur[0] = "mb" if s else "ma"
            for h in range(2):
                base = 4096 * s + 2048 * h
                soft = (s, h) in relu
                for i in range(4):
                    together(soft)
                    for j in range(4 * i, 4 * i + 4):
                        if not soft and j % CFG["MU"] == 0:
                            together(True)
                        y, m = X("Y", base + j, base + 2048, 16), X("MM", base + 128 * j, base + 128 * j + 128)
                        if soft:
                            c = 128 * (j - 4 * i)
                            mm(X("b1", c, c + 128), m128("IDB"), y, True, False)
                            mm(X("b1", c, c + 128), m128("IDN"), X("XS", 256 - 256 * s + 128 * h, 384 - 256 * s + 128 * h), False, True)
                        else:
                            tt(m, y, X("bx%d" % s, 128 * h, 128 * h + 128), OP.max)
                    together(False)
                    if soft:
                        act(X("MM", base + 512 * i, base + 512 * i + 512), X("b1", 0, 512), func="Relu")
                    together(True)
                    apart = CFG["HALVES"][2 * rnd + s] == 2
                    kb = "bk%d%d" % (s, h * apart)
                    if i == 0 and (apart or h == 0):
                        mm(X(kb, 128 * h, 128 * h + (128 if apart else 256)), m128("E0"), X("KC", 0, 128 if apart else 256), True, False)
                    for j in range(4 * i, 4 * i + 4):
                        mm(X(kb, 128 * h + j, 128 * h + 128, 16), X("MM", base + 128 * j, base + 128 * j + 128), X("SEL", 0, 8), False, (apart or h == 1) and j == 15)
                    together(False)
        for s in range(2):
            n = 256 // CFG["HALVES"][2 * rnd + s]
            for a in range(0, 256, n):
                o, l, e = 256 * s + a, 16 * s + a // 16, 16 + 272 * s + a
                cur[0] = "lb" if s else "la"
                scan(X("PS", o, o + n), X("RMH", 0, n), X("bk%d%d" % (s, a // 128), a, a + n), OP.mult, OP.max)
                tc(X("HK", l, l + n // 16), X("PS", o + 15, o + n, 16))
                tt(X("OHT", e, e + n), IND(X("HK", l, l + n // 16), X("L15", 0, n // 16)), X("PS", o, o + n), OP.is_equal)
                together(True)
                mm(X("b7", 0, n), m128("EJ"), X("E0", 0, n), True, False)
                for h in range(0, n, 128):
                    mm(X("b7", h, h + 128), X("OHT", e + h, e + h + 128), m128("IDB"), False, False)
                    mm(X("b7", h, h + 128), X("OHT", e + h - 1, e + h + 127), m128("IDN"), False, h + 128 == n)
                together(False)
                tt(X("PL", o, o + n), X("b7", 0, n), X("KF", o, o + n), OP.mult)
                wrap(X("b3", 0, n // 16), "WBB", X("PL", o, o + n))
                tc(X("LL", l, l + n // 16), X("b3", 0, n // 16))
                tc(X("ZK", o, o + n), IND(kwin, X("LL", l, l + n // 16)))
                cur[0] = ""
                if not last:
                    act(X("OHS", o, o + n), X("b7", 0, n), scale=-1.0 if s else 1.0)
            cur[0] = "zb" if s else "za"
            kids("Z", "ZK", s, CFG["Z%d%d" % (rnd, s)])
        cur[0] = ""
        tc(X("LW", 0, 32), X("LL", 0, 32))
        cur[0] = "eq"
        tc(X("FG", 0, 256), IND(fwin, la(0)))
        hold(X("SC", 0, 256), X("FG", 0, 256))
        ts(X("FWH", 0, 16), X("SC", 15, 256, 16), col(7), OP.add)
        lin("V", X("FW", 0, 16), X("SC", 15, 256, 16), 1.0, col(7))
        cur[0] = "qd"
        together(True)
        mm(X("b2", 0, 256), m128("TRI"), X("TBIG", 0, 256), True, False)
        for r in range(16):
            mm(X("b2", r, 256, 16), m128("IDB"), X("FWH", 0, 16), False, r == 15)
        together(False)
        tt(X("EQD", 0, 256), X("FG", 0, 256), X("b2", 0, 256), OP.is_equal)
        cur[0] = "eq"
        for lo, hi in ((1, 6), (6, 10), (10, 13), (13, 16)):
            together(True)
            for c in range(lo, hi):
                ts(X("EQ", 8 * c * (c - 1), 8 * c * (c + 1)), X("FG", 256 - 16 * c, 256), X("FW", 15 - c, 16 - c), OP.is_equal)
            together(False)
        together(True)
        mm(X("b2", 0, 256), m128("BLK"), X("EQD", 0, 256), True, False)
        for c in range(1, 16):
            if c == 10:
                together(True)
            mm(X("b2", 256 - 16 * c, 256), m128("BLK"), X("EQ", 8 * c * (c - 1), 8 * c * (c + 1)), False, c == 15)
        together(False)
        hold(X("SC", 512, 768), X("b2", 0, 256))
        cur[0] = "pre"
        aw, bw = X("AW", 0, 16), X("AW", 16, 32)
        ts(w(2), X("SC", 527, 768, 16), col(8), OP.is_equal)
        tt(w(3), aw, bw, OP.not_equal)
        tt(w(5), w(3), X("CE", 1, 32, 2), OP.mult)
        tt(w(6), w(2), w(5), OP.mult)
        tt(w(7), w(2), w(6), OP.subtract)
        ts(w(12, 2), X("LW", 0, 32), 2047, OP.not_equal)
        tt(w(14), w(12), w(13), OP.mult)
        for i in range(2):
            tt(w(8 + i), w(14), w(6), OP.mult)
            if not (CFG["BOTH"][rnd] and last):
                lin(sm, w(26 + i), w(5), -90.0, 99.0)
        tt(w(44, 2), X("LW", 0, 32), X("DUF", 0, 32), OP.subtract)
        tt(w(16, 2), w(44, 2), w(8, 2), OP.mult)
        tt(X("CH", 288, 384, 3), w(16, 2), X("DUF", 32, 64), OP.add)
        if not last:
            tt(w(46, 2), X("AW", 0, 32), X("DUF", 0, 32), OP.subtract)
            tt(w(18, 2), w(46, 2), w(8, 2), OP.mult)
        both = CFG["BOTH"][rnd]
        if both:
            for i in range(2):
                tt(w(48 + i), aw, X("MD", 32 * i, 32 * i + 16), OP.subtract)
                tt(w(51 + i), w(48 + i), w(5), OP.mult)
            tt(w(56, 2), w(51, 2), X("MD", 16, 48), OP.add)
            ts(X("LT", 0, 32), w(56, 2), 0 if last else X0, OP.add)
            tt(w(54, 2), X("AW", 0, 32), X("DUF", 0, 32), OP.subtract)
            for s in range(2):
                tt(X("PQ", 64 + 32 * s, 96 + 32 * s, 2), w(54 + s), w(2), OP.mult)
            lin(sm, w(59), w(5), 10.0, -1.0)
            lin(sm, w(60), w(5), -90.0, 99.0)
        else:
            for i in range(2):
                tt(w(48 + 2 * i, 2), X("AW", 0, 32), X("MD", 32 * i, 32 * i + 32), OP.subtract)
            tt(w(54, 2), X("AW", 0, 32), X("MD", 64, 96), OP.subtract)
            for i in range(2):
                tt(w(56 + i), w(54 + i), w(6), OP.mult)
            tt(w(58), w(54), w(7), OP.mult)
            tt(X("CH", 240, 288, 3), w(58), dux, OP.add)
        cur[0] = "su"
        for i in range(2):
            wrap(X("b0", 0, 16), "WBW", um(0, i), i == 0, i == 1)
        if not last:
            cur[0] = "sb"
            wrap(X("bs", 0, 12), "WBW", um(1, 0, 64), True, False)
            mm(X("bs", 0, 12), m128("IDB"), X("L977", 4, 16), False, False)
            wrap(X("bs", 0, 12), "WBW", um(1, 1, 64), False, True)
        cur[0] = "su"
        for i in range(2):
            pool(X("XW", X0 + MO + 256 * i, X0 + MO + 256 * i + 256), um(0, i))
        cur[0] = "gl"
        for i in range(3):
            mm(X("b4", 0, 256), m128("IDN" if i == 1 else "IDB"), um(i % 2, i // 2), i == 0, i == 2)
        tt(X("GL", 0, 256), X("b4", 0, 256), um(1, 1), OP.is_gt)
        tt(X("GL", 256, 512), X("b4", 0, 256), um(1, 1), OP.is_lt)
        wrap(X("b2", 0, 32), "WBB", X("GL", 0, 512))
        cur[0] = "su"
        tc(X("SI", 0, 16), X("b0", 0, 16))
        ts(X("SI", 32, 48), X("SI", 0, 16), 127, OP.bitwise_and)
        root = X("CH", 192, 240, 3)
        tt(root, X("SI", 32, 48), X("RBK", 16 * rnd, 16 * rnd + 16), OP.add)
        twin = X("XW", X0, X0 + XEND) if last else X("XW", 0, X0 + R2O)
        if both:
            tt(w(50), X("LW", 0, 16), root, OP.subtract)
            tt(w(53), w(50), w(5), OP.mult)
            tt(w(58), w(53), root, OP.add)
            ts(X("LT", 32, 48), w(58), 0 if last else X0, OP.add)
            cur[0] = "xp"
            for i in range(3):
                gat(X("TG", 256 * i, 256 * i + 256), IND(twin, X("LT", 16 * i, 16 * i + 16)))
            gat(X("TG", 768, 1024), IND(xwin, X("LL", 16, 32)))
            for i in range(3):
                mm(X("b3", 0, 256), m128("ID2" if i == 2 else "IDB"), X("TG", 256 * i, 256 * i + 256), i == 0, False)
            mm(X("b3", 256, 512), m128("ID2"), X("XS", 256, 512), False, False)
            mm(X("b3", 256, 512), m128("ID2"), X("TG", 768, 1024), False, True)
            ts(X("VI", 0, 512), X("b3", 0, 512), 0.25, OP.mult, -0.375, OP.add)
            cur[0] = "vd"
            tt(X("PQ", 1, 64, 2), X("b2", 0, 32), w(59, 2), OP.is_ge)
            scan(X("PQ", 128, 192), X("PQ", 0, 64), X("PQ", 64, 128), OP.mult, OP.add)
            tc(X("LX", 0, 32), X("PQ", 129, 192, 2))
        else:
            for s in range(2):
                tt(w(52 + s), X("LW", 16 * s, 16 * s + 16), root, OP.subtract)
        cur[0] = "vd"
        together(True)
        for i in range(2):
            for s in range(2):
                ts(X("CH", 288 + 48 * i + 1 + s, 336 + 48 * i, 3), X("b2", 16 * s, 16 * s + 16), 9, OP.is_ge, -2576, OP.mult)
        together(False)
        scan(X("CS", 288, 384), X("R3", 0, 96), X("CH", 288, 384), OP.mult, OP.add)
        tc(X("LF", 0, 32), X("CS", 290, 384, 3))
        if not (both and last):
            tt(w(20, 2), X("b2", 0, 32), w(26, 2), OP.is_ge)
        cur[0] = "fs"
        put(X("F", 0, 5152), X("LF", 0, 32), X("VALF", 0, 512), CFG["PUT"][rnd], CFG["PQ"][rnd])
        cur[0] = "xw"
        if not both:
            choose(X("LT", 0, 48), 2, [(w(48 + 2 * i), w(49 + 2 * i)) for i in range(3)], 0 if last else X0, OP.add)
            choose(X("LX", 0, 16), 5, [(w(56), w(57))], 0, OP.add)
            for i in range(3):
                gat(X("TG", 256 * i, 256 * i + 256), IND(twin, X("LT", 16 * i, 16 * i + 16)), CFG["TQ"][3 * rnd + i])
            for i in range(3):
                mm(X("b3", 0, 256), m128("ID2" if i == 2 else "IDB"), X("TG", 256 * i, 256 * i + 256), i == 0, i == 2)
            ts(X("VI", 0, 256), X("b3", 0, 256), 0.25, OP.mult, -0.375, OP.add)
        add("W", "waitsent", X("XW", X0, X0 + 128), [], (rnd + 1,), 0)
        put(X("XW", X0, X0 + MO + 256 * both), X("LX", 0, 16 + 16 * both), X("VI", 0, 256 + 256 * both), CFG["PUT"][2 + rnd])
        if last:
            dma("S", ("d", "yf"), X("F", 0, 2048), "d7")
            for i in range(2):
                dma("SA"[i], ("d", "yx%d" % i), X("XW", X0 + 1024 * i, X0 + 1024 * i + 1024), "d%d" % (8 + i))
            break
        add("G", "send", None, [X("XW", X0, X0 + 128)], (2,), 1.0)
        add("N", "arrive", X("XW", X0 + R2O, X0 + XEND), [], (2,), 0)
        cur[0] = "np"

        def kn(i):
            return X("KN", 4 * i, 4 * i + 4)
        tt(w(28, 2), X("LW", 0, 32), X("AW", 0, 32), OP.subtract)
        tt(w(30, 2), w(28, 2), w(12, 2), OP.mult)
        tt(w(32, 2), w(30, 2), X("AW", 0, 32), OP.add)
        tt(w(34), w(33), w(32), OP.subtract)
        lin(sm, w(35), w(32), 1.0, MARK[0])
        for s in range(2):
            hold(X("KDS", 64 * s, 64 * s + 64), X("KF", 256 * s, 256 * s + 64))
        ts(X("KN", 0, 8), X("KDS", 15, 128, 16), col(7), OP.add)
        tt(kn(2), kn(1), kn(0), OP.subtract)
        ts(kn(3), kn(0), MARK[1], OP.add)
        gat(X("G", 2560, 2816), IND(dwin, la(0)))
        hold(X("SC", 2560, 2816), X("G", 2560, 2816))
        tt(w(36), X("SC", 2575, 2816, 16), w(12), OP.add)
        tc(X("LU", 16, 24), X("KN", 0, 8))
        gat(X("G", 0, 128), IND(dwin, X("LU", 16, 24)))
        hold(X("SC", 256, 384), X("G", 0, 128))
        tt(X("W", 592, 596), X("W", 576, 580), X("SC", 271, 320, 16), OP.subtract)
        tt(w(38), w(13), w(12), OP.subtract)
        tt(kn(10), X("SC", 335, 384, 16), X("SC", 271, 320, 16), OP.subtract)
        tt(X("W", 608, 612), X("W", 608, 612), kn(10), OP.subtract)
        cur[0] = "nb"
        tt(X("LSI", 16, 28), X("bs", 0, 12), X("SI", 4, 16), OP.add)
        ts(X("LSI", 0, 12), X("LSI", 16, 28), 2047, OP.bitwise_and)
        tc(X("LU", 0, 12), X("LSI", 0, 12))
        ts(X("PM", 20, 32), X("LSI", 0, 12), MARK[1], OP.add)
        gat(X("G", 2816, 3008), IND(dwin, X("LU", 0, 12)), CFG["CQ"][2])
        scan(X("SC", 2816, 3008), X("G", 2816, 3008), X("HM", 0, 192), OP.min, OP.add, 4096.0)
        tt(X("W", 596, 608), X("W", 580, 592), X("SC", 2831, 3008, 16), OP.subtract)
        cur[0] = "vd"
        tt(w(39), w(21), w(38), OP.mult)
        tt(X("DS", 16, 32), w(39), w(37), OP.add)
        tt(w(40), w(21), w(34), OP.mult)
        tt(X("PM", 0, 16), w(40), w(35), OP.add)
        tt(kn(11), X("W", 336, 340), kn(2), OP.mult)
        tt(X("PM", 16, 20), kn(11), kn(3), OP.add)
        cur[0] = "kd"
        together(True)
        mm(X("b1", 0, 256), m128("BLK"), X("PL", 256, 512), True, False)
        mm(X("b1", 0, 256), m128("NBLK"), X("PL", 0, 256), False, True)
        together(False)
        for s in range(2):
            tt(X("TK", 256 * s, 256 * s + 256), X("b1", 0, 256), X("OHS", 256 * s, 256 * s + 256), OP.mult)
        together(True)
        mm(X("b4", 0, 512), m128("IDB"), X("KF", 0, 512), True, False)
        mm(X("b4", 0, 512), m128("IDB"), X("TK", 0, 512), False, True)
        together(False)
        act(X("NK", 0, 512), X("b4", 0, 512))
        choose(X("LF", 32, 64), 0, [(w(18), w(18)), (w(19), w(19))], 0, OP.add)
        put(X("KD", 0, 2576), X("LF", 32, 64), X("NK", 0, 512), CFG["PUT"][4], CFG["PQ"][2])
    return P


def deps(P):
    hist = {}
    preds = [dict() for _ in P]
    for i, p in enumerate(P):
        for acc, wr in [(a, False) for a in p["r"]] + [(a, True) for a in p["w"]]:
            if acc[0] != "x":
                continue
            L = hist.setdefault(acc[1], [])
            for j, b, bw in L:
                if j == i:
                    continue
                if acc[1][0] == "b":
                    both = p["q"] == "T" and P[j]["q"] == "T"
                    if p["q"] != P[j]["q"] or ((wr or bw) and clash(acc, b) and not both):
                        preds[i][j] = True
                    elif both:
                        preds[i].setdefault(j, False)
                elif (wr or bw) and clash(acc, b):
                    preds[i][j] = True
            L.append((i, acc, wr))
    return preds


def order(P, preds):
    n = len(P)
    units, uses = {}, {}
    for i, p in enumerate(P):
        units.setdefault(p["g"], []).append(i)
        for v in p["use"]:
            uses.setdefault(v, []).append(i)
    late = [2.0 + p["args"][1] if p["what"] == "dma" else 12.0 if p["what"] == "arrive" else 0.0 for p in P]

    length = {u: sum(P[i]["cost"] for i in m) for u, m in units.items()}

    def wake(i, j, hard):
        return (WS if P[i]["q"] == P[j]["q"] else WK) if hard else 0.0

    def turn(pre):
        suc = [dict() for _ in P]
        for i in range(n):
            for j, h in pre[i].items():
                suc[j][i] = h
        return suc

    def sweep(pre, prio, fixed):
        back = fixed is not None
        pre = [dict(d) for d in pre]
        member = {u: m[::-1] if back else m for u, m in units.items()}
        ext = {u: {j for i in m for j in pre[i] if P[j]["g"] != u} for u, m in member.items()}
        left = {u: len(e) for u, e in ext.items()}
        waits = {}
        for u, e in ext.items():
            for j in e:
                waits.setdefault(j, []).append(u)
        t = [None] * n

        def when(u):
            at, off = 0.0, 0.0
            for i in member[u]:
                at = max([at] + [t[j][1] + wake(i, j, h) + (late[i] if back else 0.0) - off for j, h in pre[i].items() if P[j]["g"] != u])
                off += P[i]["cost"]
            return at
        ready = {u: when(u) + (late[member[u][0]] if back else 0.0) for u in units if not left[u]}
        free = {q: 0.0 for q in "AVTGSNWD"}
        seq, queue = [], [None] * n
        bank, holder, unopened, open_ = {}, [None] * 8, sorted(uses), {v: len(m) for v, m in uses.items()}
        while ready:
            idle = [] if back else sorted((max([t[j][1] for j in uses[v]]) + WK if v is not None else 0.0, b) for b, v in enumerate(holder) if v is None or not open_[v])
            cand = []
            for u, at in ready.items():
                i = member[u][0]
                new = [] if back else [v for v in P[i]["use"] if v not in bank]
                if new:
                    if len(idle) < (1 if new[0] == unopened[0] else 1 + CFG["KEEP"]):
                        continue
                    at = max(at, idle[0][0])
                q = P[i]["q"]
                cand.append((max(free[q], at), -prio[i], u, q))
            first = min(cand)
            mine = [c for c in cand if c[3] == first[3]]
            soon = min((c for c in mine if c[0] <= first[0] + CFG["SLACK"].get(first[3], 0.0) * length[first[2]]), key=lambda c: (c[1], c[0]))
            if soon[1] < first[1] - CFG["MARGIN"]:
                first = min([c for c in mine if c[0] + length[c[2]] <= soon[0] + 0.03] or [soon], key=lambda c: (c[1], c[0]))
            st, _, u, q = first
            del ready[u]
            for i in member[u]:
                for v in P[i]["use"]:
                    open_[v] -= 1
                    if not back and v not in bank:
                        b = idle[0][1]
                        if holder[b] is not None:
                            for j in uses[holder[b]]:
                                pre[i][j] = pre[i].get(j, False) or P[j]["q"] != "T"
                        bank[v], holder[b] = b, v
                        unopened.remove(v)
                queue[i] = q
                end = st + P[i]["cost"]
                free[q] = end
                if not back and P[i]["what"] == "dma" and P[i]["args"][1] > 0.5:
                    free["D"] = max(end + 1.3, free["D"]) + P[i]["args"][1]
                    end = free["D"] + 0.7
                elif not back:
                    end += late[i]
                t[i] = (st, end)
                st = free[q]
                seq.append(i)
            for i in member[u]:
                for k in waits.get(i, []):
                    left[k] -= 1
                    if not left[k]:
                        ready[k] = when(k)
        assert len(seq) == n
        return max(e for _, e in t), t, seq, queue, pre, bank
    succ = turn(preds)
    tau, seen = [CFG["KNOWN"][2]] * n, {}
    for i, p in enumerate(P):
        a, d = CFG["PLAN"].get(p["b"], CFG["PLAN"].get(p["b"][:-1], (None, None)))
        if a is not None:
            seen[p["b"]] = seen.get(p["b"], -1) + (p["g"] == i)
            tau[i] = CFG["KNOWN"][int(p["b"][-1])] + a + d * seen[p["b"]]
    for i in range(n - 1, -1, -1):
        tau[i] = min([tau[i] - late[i]] + [tau[k] - wake(i, k, h) - P[i]["cost"] - late[i] for k, h in succ[i].items()])
    for m in units.values():
        tau[m[0]] = min(tau[i] for i in m)
    seq, queue = sweep(preds, [-s for s in tau], None)[2:4]
    ids = [P[i]["g"] for i in seq if P[i]["g"] == i]
    at = {u: k for k, u in enumerate(ids)}
    m = len(ids)
    off, tail, need = {}, [0.0] * m, [dict() for _ in ids]
    for u in ids:
        s = 0.0
        for i in units[u]:
            off[i] = s
            s += P[i]["cost"]
            tail[at[u]] = max(tail[at[u]], s + late[i])
    above = [0] * m
    for k, u in enumerate(ids):
        for i in units[u]:
            for j, h in preds[i].items():
                z = at[P[j]["g"]]
                if z != k:
                    need[k][z] = max(need[k].get(z, 0.0), off[j] + P[j]["cost"] + late[j] + wake(i, j, h) - off[i])
        far = 0
        for z in need[k]:
            far |= above[z]
        above[k] = far | sum(1 << z for z in need[k])
        need[k] = [(z, d) for z, d in need[k].items() if not far >> z & 1 or d > 1.5]
    size = [length[u] for u in ids]
    lane = ["AVTGSNW".index(queue[u]) for u in ids]
    inner = {z for k in range(m) for z, d in need[k]}
    ends = [k for k in range(m) if k not in inner]

    touch = [sorted({v for i in units[u] for v in P[i]["use"]}) for u in ids]
    users = {v: len({P[i]["g"] for i in uses[v]}) for v in uses}
    either = [P[u]["what"] in ("gat", "lin", "put") for u in ids]

    def times(row, lo, old):
        lo -= lo % 24
        st, by, marks = list(old[0]), list(old[1]), old[2][:lo // 24 + 1]
        free, last, idle, bank, left, till = [z.copy() for z in marks[-1]]
        for n_ in range(lo, span[1]):
            k = row[n_]
            if n_ % 24 == 0 and n_ > lo:
                marks.append((free[:], last[:], idle[:], bank.copy(), left.copy(), till.copy()))
            q = lane[k]
            a, b = free[q], last[q]
            for z, d in need[k]:
                d += st[z]
                if d > a:
                    a, b = d, z
            if not touch[k]:
                st[k], by[k], free[q], last[q] = a, b, a + size[k], k
                continue
            for v in touch[k]:
                if v not in bank:
                    if not idle:
                        return 1e9, None, None, None
                    got = min(idle)
                    idle.remove(got)
                    bank[v], till[v] = got[1], (0.0, k)
                    if got[0] > a:
                        a, b = got[0], got[2]
            st[k], by[k], free[q], last[q] = a, b, a + size[k], k
            for v in touch[k]:
                till[v] = max(till[v], (a + size[k] + WK, k))
                left[v] -= 1
                if not left[v]:
                    idle.append((till[v][0], bank[v], till[v][1]))
        if span[1] == m:
            k = max(ends, key=lambda z: st[z] + tail[z])
            end = st[k] + tail[k]
        else:
            k = span[2]
            end = st[k] + 0.5 * sum(max(0.0, free[q] - st[k] - size[k]) for q in range(2))
        chain = []
        while k is not None and place[k] >= span[0]:
            chain.append(k)
            k = by[k]
        return end + CFG["PULL"] * sum([st[z] for z in row[span[0]:span[1]]]) / (span[1] - span[0]), (st, by, marks), chain, bank
    row, place, span, y = list(range(m)), list(range(m)), [0, m, None], CFG["SEED"]
    blank = ([0.0] * m, [None] * m, [([0.0] * 7, [None] * 7, [(0.0, b, None) for b in range(8)], {}, users, {})])
    stops = [min(k for k, u in enumerate(ids) if P[u]["b"] == b and P[u]["q"] in "AV") for b in ("ya0", "gl0", "ya1", "gl1")]
    for a, z, steps in CFG["REPAIR"]:
        span[:] = [0, m, None]
        row = sorted(row, key=lambda k, st=times(row, 0, blank)[1][0]: st[k])
        for n_, k in enumerate(row):
            place[k] = n_
        span[:] = [max(0, place[stops[a - 1]] - CFG["LAP"]) if a else 0, place[stops[z]] + 1 if z < 4 else m, stops[z] if z < 4 else None]
        end, now, chain, bank = times(row, 0, blank)
        kept = (end, row, list(lane))
        for step in range(steps):
            y = (y * 6364136223846793005 + 1442695040888963407) % 2 ** 64
            x = y >> 30
            u = chain[(x >> 8) % len(chain)] if x & 255 < CFG["CHAIN"] else row[span[0] + (x >> 8) % (span[1] - span[0])]
            y = (y * 6364136223846793005 + 1442695040888963407) % 2 ** 64
            x = y >> 30
            i = place[u]
            flip = either[u] and x >> 16 & 3 == 0
            if flip:
                lane[u] = 1 - lane[u]
            far, past, way = 0, 1 + min((x >> 9) % CFG["FAR"], (x >> 21) % CFG["FAR"]), -1 if x >> 8 & 1 else 1
            while past and span[0] <= i + way * (far + 1) < span[1]:
                far += 1
                past -= lane[row[i + way * far]] == lane[u]
            lo, hi = (i - far, i) if way < 0 else (i, i + far)
            part = row[lo:hi + 1]
            if way < 0:
                new = [z for z in part if z == u or above[u] >> z & 1] + [z for z in part if z != u and not above[u] >> z & 1]
            else:
                new = [z for z in part if z != u and not above[z] >> u & 1] + [z for z in part if z == u or above[z] >> u & 1]
            if new == part and not flip:
                continue
            new = row[:lo] + new + row[hi + 1:]
            e, s, c, b = times(new, lo, now)
            if e <= end + CFG["WORSE"] * (1 - step / steps) * (x >> 28 & 7) / 7:
                end, now, chain, row = e, s, c, new
                for n_ in range(lo, hi + 1):
                    place[row[n_]] = n_
                if end < kept[0]:
                    kept = (end, new, list(lane))
            elif flip:
                lane[u] = 1 - lane[u]
            if step % 64 == 0:
                new = row[:span[0]] + sorted(row[span[0]:span[1]], key=lambda z: now[0][z]) + row[span[1]:]
                e, s, c, b = times(new, span[0], now)
                if e <= end:
                    end, now, chain, row = e, s, c, new
                    for n_, k in enumerate(row):
                        place[k] = n_
        row, lane[:] = kept[1:]
    span[:] = [0, m, None]
    _, (st, _, _), _, bank = times(row, 0, blank)
    seq = [i for k in row for i in units[ids[k]]]
    preds, holder = [dict(d) for d in preds], [None] * 8
    for i in seq:
        p = P[i]
        a = st[at[p["g"]]] + off[i]
        p["t"], queue[i] = (a, a + p["cost"] + late[i]), "AVTGSNW"[lane[at[p["g"]]]]
        for v in p["use"]:
            if holder[bank[v]] != v:
                for j in uses.get(holder[bank[v]], []):
                    preds[i][j] = preds[i].get(j, False) or P[j]["q"] != "T"
                holder[bank[v]] = v

    def named(a):
        if isinstance(a, tuple) and a and a[0] == "x" and a[1][0] == "b":
            return ("x", "b%d" % bank[int(a[1][1:])]) + a[2:]
        return a
    for p in P:
        p["out"], p["ins"], p["args"] = named(p["out"]), [named(a) for a in p["ins"]], tuple(named(a) for a in p["args"])
    return seq, queue, preds


PLAN = {}


def plan():
    if not PLAN:
        P = build()
        preds = deps(P)
        PLAN["p"] = (P,) + order(P, preds)
    return PLAN["p"]


def rank_program(g, core, T, topo):
    rank = T.rank_of(core)
    if rank is None:
        return
    P, seq, queue, preds = plan()
    eng = {"V": g.vector, "A": g.scalar, "T": g.tensor, "G": g, "S": g.sync}
    funcs = {None: AF.Identity, "Relu": AF.Relu, "Abs": AF.Abs, "Sign": AF.Sign, "Silu": AF.Silu}
    cores = list(T.cores)
    n = len(cores)

    def ap(a):
        if a[0] == "i":
            return ap(a[1]).indirect(ap(a[2]))
        if a[0] == "d":
            if a[1] == "yf":
                return T.yf[:]
            if a[1][:2] == "yx":
                i = int(a[1][2:])
                return T.yx[:, 1024 * i:1024 * i + 1024]
            return T[a[1]][:, a[2]:a[3]] if len(a) > 2 else T[a[1]][:]
        _, name, lo, hi, st, p0, p1 = a
        return T[name][p0:p1, lo:hi] if st == 1 else T[name][p0:p1, lo:hi:st]

    def sc(s):
        return ap(s) if isinstance(s, tuple) else s

    count = {"V": 0, "A": 0, "T": 0, "G": 0}
    done, total = {}, {}
    seen = {q: {} for q in "VATGS"}

    def wait(q, sem, v):
        if seen[q].get(sem, 0) < v:
            seen[q][sem] = v
            eng[q].wait_ge(T.sem[sem], v)

    for i in seq:
        p, q = P[i], queue[i]
        what, args = p["what"], p["args"]
        if what == "arrive":
            done[i] = [("arr%d" % args[0], ND * (n - 1))]
            total["arr%d" % args[0]] = ND * (n - 1)
            continue
        if what == "waitsent":
            done[i] = [s for j in preds[i] for s in done[j]] + [("sent%d" % args[0], ND)]
            continue
        need = {}
        for j, hard in preds[i].items():
            if hard:
                for sem, v in done[j]:
                    need[sem] = max(need.get(sem, 0), v)
        for sem in sorted(need):
            wait(q, sem, need[sem])
        out = p["out"] and ap(p["out"])
        ins = [ap(a) for a in p["ins"]]
        e = eng[q]
        if what == "dma":
            src = ins[0]
            if p["out"][1] == "yf":
                src = T.F[0::16, 0:2048]
            e.dma_start(out, src).then_inc(T.sem[args[0]], 16)
            done[i] = [(args[0], 16)]
            total[args[0]] = 16
            continue
        if what == "send":
            base = (0 if args[0] == 1 else X0 + R2O)
            others = [cores[(rank + d) % n] for d in range(1, n)]
            engines = [x for x in topo.engines(core, others[0]) if all(x in topo.engines(core, o) for o in others)][:ND]
            ids, dsts = [], []
            for o in others:
                rid, pid, _s = topo.addr(o)
                slot = (rank - T.rank_of(o) - 1) % n
                ids.append(DstId(rid=rid, pnc=pid))
                dsts.append(T.XW[:, base + 128 * slot:base + 128 * slot + 128])
            g.remote_dma_fused([RemoteDMATransfer(dst_ids=ids, dma_engine_mask=sum(1 << x for x in engines), remote_sem=T.sem["arr%d" % args[0]], srcs=[ins[0]], dsts=dsts)], local_sem=T.sem["sent%d" % args[0]])
            done[i] = [("sent%d" % args[0], ND)]
            total["sent%d" % args[0]] = ND
            continue
        if what == "tc" or (what in ("gat", "put") and q == "V"):
            h = e.tensor_copy(out, ins[0])
        elif what == "put":
            h = e.activation(out, ins[0], AF.Silu)
        elif what == "gat":
            h = e.activation(out, ins[0], AF.Copy)
        elif what == "count":
            h = e.activation(out, ins[0], AF.Copy, accum_out=ap(args[0]))
        elif what == "lin" and q == "V":
            bias, scale, cut = args
            if cut:
                h = e.tensor_scalar(out, ins[0], bias if scale == 1.0 else scale, 0, OP.add if scale == 1.0 else OP.mult, OP.max)
            else:
                h = e.tensor_scalar(out, ins[0], scale, sc(bias), OP.mult, OP.add)
        elif what in ("act", "lin"):
            bias, scale, func = args
            if bias is None and scale == 1.0 and func is None:
                h = e.activation(out, ins[0], AF.Copy)
            elif bias is None and scale == 1.0:
                h = e.activation(out, ins[0], funcs[func])
            else:
                h = e.activation(out, ins[0], funcs[func], bias=0.0 if bias is None else sc(bias), scale=sc(scale))
        elif what == "tt":
            h = e.tensor_tensor(out, ins[0], ins[1], args[0])
        elif what == "ts":
            s1, o1, s2, o2 = args
            h = e.tensor_scalar(out, ins[0], sc(s1), None, o1) if o2 is None else e.tensor_scalar(out, ins[0], sc(s1), sc(s2), o1, o2)
        elif what == "scan":
            h = e.tensor_tensor_scan(out, ins[0], ins[1], sc(args[2]), args[0], args[1])
        elif what == "mm":
            h = e.matmul(out, ins[0], ins[1], args[0], args[1])
        elif what == "tr":
            h = e.transpose(out, ins[0])
        elif what == "ms":
            h = e.memset(out, args[0])
        elif what == "sel":
            h = e.affine_select(out, ins[0], args[0], args[3], args[4], args[2], args[1])
        elif what == "iota":
            h = e.iota(out, args[0], args[2], args[1], allow_small_or_imprecise_dtypes=True)
        h.then_inc(T.sem["q" + q], 1)
        count[q] += 1
        done[i] = [("q" + q, count[q])]
    for q in "VATG":
        if count[q]:
            wait("S", "q" + q, count[q])
    for sem in sorted(total):
        wait("S", sem, total[sem])
